import numpy as np, ml_dtypes
CORES = [5,29,101,125,133,157,229,253]
N = 8
import mx_ref
BF = ml_dtypes.bfloat16
def gcols(t, e):
    v = np.concatenate([t.reshape(8, 16, -1, 4), np.zeros((8, 16, 1, 4), BF)], axis=2)
    return np.ascontiguousarray(np.stack([v[g][:, e[g]] for g in range(8)])).reshape(128, -1)
def tile(rs):
    return np.stack(rs, axis=2).reshape(128, -1).astype(BF)
def cut(t, i, w=512):
    return t[:, w * i:w * i + w]
def pick(q, e):
    c = np.concatenate([q[0].reshape(128, -1, 4), np.zeros((128, 1, 4), np.uint8)], axis=1); s = np.concatenate([q[1], np.ones((16, 1), np.uint8)], axis=1)
    return (np.ascontiguousarray(c[:, e].reshape(128, -1)), np.ascontiguousarray(s[:, e]))
def join(*qs):
    return (np.concatenate([q[0] for q in qs], axis=1), np.concatenate([q[1] for q in qs], axis=1))
def put(q, e, v):
    c, s = q[0].reshape(128, -1, 4).copy(), q[1].copy(); c[:, e] = v[0].reshape(128, -1, 4); s[:, e] = v[1]
    return (c.reshape(128, -1), s)
def pk(c, s):
    return (np.ascontiguousarray(c), mx_ref.live(s))
def emit(q):
    return q[0], q[1]
def packed(v, rng):
    q = [mx_ref.quantize(np.ascontiguousarray(v[r])) for r in range(N)]
    return np.stack([a for a, b in q]), np.stack([mx_ref.plane(b, rng) for a, b in q])
def values_of_codes():
    e, c = np.zeros((128, 128, 4), np.float32), np.zeros((128, 2, 4), np.uint8)
    e[np.arange(128), np.arange(128), 0] = 1
    c[:127, :, 0] = np.arange(256).reshape(2, 128).T[:127]
    return mx_ref.matmul(mx_ref.quantize(e.reshape(128, 512).astype(BF)), (c.reshape(128, 8), np.full((16, 2), 127, np.uint8))).T.reshape(-1).astype(np.float64)
CODE_VALUE, SCALE_VALUE = values_of_codes(), 2.0 ** (np.arange(256) - 127.0)
def decode(q):
    return (CODE_VALUE[q[0]].reshape(16, 8, -1, 4) * SCALE_VALUE[q[1]][:, None, :, None] + 0.0).reshape(128, -1).astype(np.float32)
def f(rng, *shape):
    return mx_ref.flush((rng.standard_normal(shape, dtype=np.float32) * np.exp2(rng.integers(-2, 3, shape[:-1] + (1,)))).astype(BF))
def wide(rng, *shape, cols=0):
    v = rng.standard_normal(shape, dtype=np.float32) * np.exp2(rng.integers(-12, 13, shape)).astype(np.float32)
    if cols: v *= np.repeat(np.exp2(rng.integers(-cols, cols + 1, shape[:-2] + (1, shape[-1] // 4))) * (rng.random(shape[:-2] + (1, shape[-1] // 4)) > 0.0625), 4, axis=-1).astype(np.float32)
    return mx_ref.flush(v.astype(BF))
C, T, R = 384, 64, 2
def match(o):
    m, stack, closes = np.full(C, -1), [], []
    for j in range(C):
        if o[j]:
            stack.append(j)
        elif stack:
            i = stack.pop()
            m[i], m[j] = j, i
        else:
            closes.append(j)
    return m, np.array(stack[::-1], int)[:T], np.array(closes, int)[:T]
def big(v, k):
    v = v.astype(np.float32) * np.float32(k)
    v[np.abs(v) < np.float32(2.0 ** -16)] = 0
    return v.astype(BF)
def same(v):
    return np.stack([v] * N)
def weights(rng, h=-1):
    w = big(f(rng, 128, 2048), 0.25)
    if h >= 0:
        w = w.reshape(128, 4, 128, 4)
        w[:, :, 16 * h:16 * h + 8] = 0
        p = np.arange(16 * h, 16 * h + 8)
        for b in range(2): w[p + 8, b, p, b] = 16
        w = w.reshape(128, 2048)
    c, s = packed(same(w), rng)
    return {"wc": c, "ws": s}
def numbers_of(rng):
    return {"x": big(f(rng, N, 128, 4 * C), 1), "u": same(np.array(f(rng, 128, 512))), "v": np.array(f(rng, N, 128, 512))}
def plant(rng, h, first, then, size=np.ones(8), less=(False, False)):
    d = {**numbers_of(rng), **weights(rng, h)}
    x = d["x"].reshape(N, 128, C, 4)
    x[:, 16 * h:16 * h + 16] = 0
    for t, s in enumerate((first, then)):
        p = 16 * h + 8 * t
        x[:, p:p + 8, :, 0] = (np.where(less[t], -1.25 * s, s) + 0.0).astype(np.float32).astype(BF)
        x[:, p:p + 8, :, 1] = np.roll(np.where(less[t], 1.125 * s, 0.0), 1, axis=1).astype(np.float32).astype(BF)
    d["x"] = x.reshape(N, 128, 4 * C)
    for g in range(8):
        d["u"][:, :, 64 * g:64 * g + 4] = 0
        d["u"][:, 16 * h + g, 64 * g] = float(size[g])
        d["u"][:, 16 * h + (g + 1) % 8, 64 * g + 1] = 1.125 * float(size[g])
    return d
def half(rng, n, b):
    v = rng.permutation(np.repeat([1.0, -1.0], [n + b, n]))
    if n + b == 0: return v
    return np.roll(v, -1 - int(np.argmin(np.cumsum(v))))
def word(rng, a, b):
    n = (C - a - b) // 2
    m = int(rng.integers(0, n + 1))
    return np.concatenate([-half(rng, m, a)[::-1], half(rng, n - m, b)])
def brackets(rng, a, b):
    return np.stack([np.stack([word(rng, int(a[r, g]), int(b[r, g])) for g in range(8)]) for r in range(N)])
def setup_inputs(rng):
    return {**numbers_of(rng), **weights(rng)}
def setup_inputs_zeros(rng):
    h = int(rng.integers(0, 8))
    size = np.exp2(rng.integers(-30, 1, (N, 1, C)))
    first, then = [rng.choice([-1.0, -1.0, 0.0, 1.0], (N, 8, C)) for t in range(2)]
    first[:, h] = rng.integers(0, 2, (N, C))
    less = rng.random((2, N, 8, C)) < 0.5
    return plant(rng, h, first * size, then * size, np.exp2(rng.permutation(np.repeat([-30.0, -12.0, 12.0], [4, 2, 2]))), less)
def counts(rng):
    e = rng.permutation(8) % 2 == 0
    a, b = [np.where(e, rng.choice([0, T, T + 2, 2 * T], (N, 8)), rng.choice([T - 1, T + 1], (N, 8))) for i in range(2)]
    g = np.arange(8)
    i = rng.integers(0, N - 1, 8)
    j = (i + 1) % (N - 1)
    b[i, g] = np.where(e, T, T + 1)
    a[i + 1, g] = np.where(e, T, T + 1)
    b[j, g] = np.where(e, 2 * T, T - 1)
    a[j + 1, g] = np.where(e, 2 * T, T + 1)
    return a, b
def setup_inputs_cap(rng):
    h = int(rng.integers(0, 8))
    first, then = brackets(rng, *counts(rng)), brackets(rng, *counts(rng))
    first[:, h] = 1
    return plant(rng, h, first, then)
def setup_inputs_nest(rng):
    h = int(rng.integers(0, 8))
    n = np.arange(C)
    s = np.stack([np.ones(C), -np.ones(C), np.where(n < C // 2, 1.0, -1.0), np.where(n < C // 2, -1.0, 1.0), 1.0 - 2 * (n % 2), 2.0 * (n % 2) - 1,
                  np.where(n < 7 * C // 8, 1.0, -1.0), np.where(n < C - 1, 1.0, -1.0)] + [np.where((n >= c) & (n < (c + C) // 2), 1.0, -1.0) for c in (3 * C // 4, C - 4, C - 2)])
    o = []
    for t in range(2):
        k = np.zeros((N, 8), int)
        lead = rng.permutation(8) % 3 if N < 8 else np.zeros(8, int)
        deep = rng.permutation(np.repeat([8, 9, 10], [4, 2, 2]))
        for g in range(8):
            pairs = [[0, 1], [2, 3], [7, int(rng.integers(4, 6))]]
            l = int(lead[g])
            e = pairs[l] + [6, int(deep[g])] + pairs[(l + 1) % 3] + pairs[(l + 2) % 3]
            k[(int(rng.integers(0, N - 1)) + np.arange(N)) % N, g] = np.resize(e, N)
        o.append(s[k])
    o[0][:, h] = 1
    return plant(rng, h, *o)
def setup_inputs_turns(rng):
    h = int(rng.integers(0, 8))
    e = rng.permutation(8) % 2 == 0
    a, b = [rng.choice([T, 2 * T], (N, 8)) for i in range(2)]
    first, then = brackets(rng, np.where(e, a, 0), np.where(e, b, 0)), brackets(rng, np.where(e, 0, a), np.where(e, 0, b))
    first[:, h] = 1
    return plant(rng, h, first, then)
def setup_inputs_spread(rng):
    d = setup_inputs(rng)
    d["x"] = big(wide(rng, N, 128, 4 * C, cols=6), 1)
    return d
def check_inputs(d):
    b = []
    for k in ("x", "u", "v"):
        a = np.abs(d[k].astype(np.float32))
        if not (np.isfinite(a).all() and ((a == 0) | (a >= 2.0 ** -30) & (a <= 2.0 ** 30)).all()): b.append("a value of " + k)
    if (d["u"].astype(np.float32) != d["u"][:1].astype(np.float32)).any(): b.append("u differs between ranks")
    if (d["wc"] != d["wc"][:1]).any(): b.append("wc differs between ranks")
    s = [mx_ref.live(p) for p in d["ws"]]
    if any((p != s[0]).any() for p in s): b.append("ws differs between ranks")
    c = d["wc"] & 127
    if (c == 127).any(): b.append("a code of wc")
    zero, low, high = [emit(mx_ref.quantize(np.full((128, 16), k).astype(BF)))[1].astype(int) for k in (0.0, 2.0 ** -30, 2.0 ** 30)]
    full = (c.reshape(N, 16, 8, 512, 4) != 0).any(axis=(2, 4))
    l = np.stack(s).astype(int)
    if (((l < np.min(low)) | (l > np.max(high))) & (full | (l != zero[0, 0]))).any(): b.append("a scale of ws")
    return b
def reference(x, u, v, wc, ws):
    w = pk(wc[0], ws[0])
    w = [pick(w, np.arange(128 * b, 128 * b + 128)) for b in range(4)]
    qu = mx_ref.quantize(np.ascontiguousarray(u[0]))
    a = [mx_ref.quantize(np.ascontiguousarray(x[r])) for r in range(N)]
    none = np.zeros((128, 4 * T), BF)
    for t in range(R):
        p, get, mo, mc = [], [], [], []
        for r in range(N):
            s = mx_ref.matmul(qu, a[r])[::16]
            p.append(tile([mx_ref.matmul(w[b], a[r]) * np.float32(0.0625) for b in range(4)]))
            e, o, c = np.full((8, C), -1), np.full((8, T), -1), np.full((8, T), -1)
            for g in range(8):
                e[g], opens, closes = match(s[g] >= 0)
                o[g, :len(opens)] = opens
                c[g, :len(closes)] = closes
                e[g, closes] = C + np.arange(len(closes))
                e[g, opens] = C + T + np.arange(len(opens))
            get.append(e)
            mo.append(mx_ref.quantize(gcols(p[r], o)))
            mc.append(mx_ref.quantize(gcols(p[r], c)))
        d = decode(join(*mo, *mc)).astype(BF)
        for r in range(N):
            left = cut(d, r - 1, 4 * T) if r > 0 else none
            right = cut(d, N + r + 1, 4 * T) if r < N - 1 else none
            z = gcols(np.concatenate([p[r], left, right], axis=1), get[r])
            a[r] = mx_ref.quantize((p[r].astype(np.float32) + z.astype(np.float32)).astype(BF))
    y, oc, osc = np.zeros((N, 128, C), np.float32), np.zeros((N, 128, 4 * C), np.uint8), np.zeros((N, 16, C), np.uint8)
    for r in range(N):
        y[r] = mx_ref.matmul(mx_ref.quantize(np.ascontiguousarray(v[r])), a[r])
        oc[r], osc[r] = emit(a[r])
    return {"y": y, "oc": oc, "osc": osc}

@@ -1,0 +1,461 @@
+from concourse.bass import DstId, RemoteDMATransfer
+from concourse.mybir import dt, AluOpType as A, ActivationFunctionType as F
+
+C, TM, ROUNDS = 384, 64, 2
+ZW = 544
+DL = C + 15
+NEAR, FAR = 8, 8
+VM = (2, 0)
+X4, U8, BF, F32, I32, U16 = "float8_e4m3fn_x4", "uint8", "bfloat16", "float32", "int32", "uint16"
+
+
+def _sb(n, d):
+    return ("sbuf", [128, n], d)
+
+
+SCRATCH = {
+    "xb": _sb(4 * C, BF), "ub": _sb(512, BF), "vb": _sb(512, BF),
+    "aq0": _sb(C, X4), "as0": _sb(C, U8), "aq1": _sb(C, X4), "as1": _sb(C, U8), "aq2": _sb(C, X4), "as2": _sb(C, U8),
+    "uq": _sb(128, X4), "us": _sb(128, U8), "uq2": _sb(128, X4), "us2": _sb(128, U8),
+    "vq": _sb(128, X4), "vs": _sb(128, U8), "wq": _sb(512, X4), "wsc": _sb(512, U8),
+    "eb": _sb(2048, BF), "eq": _sb(512, X4), "es": _sb(512, U8),
+    "zz": _sb(4 * ZW, BF), "xt": _sb(4 * C, BF), "mt": _sb(512, BF), "yb": _sb(C, F32), "pp": _sb(4 * C, BF),
+    "mq0": _sb(128, X4), "ms0": _sb(128, U8), "mq1": _sb(128, X4), "ms1": _sb(128, U8),
+    "hq0": _sb(64, X4), "hs0": _sb(64, U8), "hq1": _sb(64, X4), "hs1": _sb(64, U8),
+    "lq0": _sb(256, X4), "ls0": _sb(256, U8), "lq1": _sb(256, X4), "ls1": _sb(256, U8),
+    "ps": ("psum", [128, 512 * 6], F32),
+    "zero": _sb(512, BF), "ci": _sb(16, I32), "cf": _sb(16, F32), "cb": _sb(2, BF), "r4": _sb(400, BF),
+    "kh": _sb(784, BF), "kd": _sb(C, BF), "kb": _sb(C, BF), "k16": _sb(800, BF), "k32": _sb(256, BF),
+    "k8": _sb(4, F32), "b8": _sb(8, F32), "kk2": _sb(128, F32), "thr2": _sb(256, BF), "idm": _sb(128, BF),
+    "upi": _sb(8, I32), "upl": _sb(8, U16), "c24": _sb(24, F32), "yf": _sb(352, F32),
+    "arow": _sb(176, I32), "gi": _sb(24, I32), "gl": _sb(24, U16), "posi": _sb(192, BF), "pos": _sb(C, BF),
+    "e3": _sb(48, BF), "tm": _sb(144, BF), "ta": _sb(144, BF), "tb": _sb(144, BF),
+    "cl": _sb(48, BF), "sf": _sb(2, F32), "sl": _sb(2, U16),
+    "sg": _sb(C, BF), "ns": _sb(C, BF), "dr": _sb(C, BF), "rr": _sb(C, BF), "uv": _sb(800, BF), "hb": _sb(800, BF),
+    "jk": _sb(192, BF), "n1": _sb(8, F32), "o16": _sb(16, U16), "off": _sb(8, F32), "c2": _sb(256, BF),
+    "t2": _sb(256, BF), "n2": _sb(256, BF), "mi": _sb(8, F32), "ml": _sb(8, U16),
+    "hr": _sb(C, BF), "gr": _sb(C + 16, BF), "xx": _sb(2 * C, BF), "yy": _sb(800, BF),
+    "sm": _sb(24 * 16, F32), "li": _sb(48, I32), "ri": _sb(24, I32), "sh": _sb(56, I32),
+    "o1": _sb(24, U16), "og": _sb(24, U16), "ol": _sb(24, U16),
+    "xa": _sb(C, BF), "xc": _sb(C, BF), "xm": _sb(C, BF), "ar": _sb(C, BF), "br": _sb(C, BF), "bx": _sb(C, BF),
+    "pa": _sb(32, BF), "pb": _sb(32, BF),
+    "ea": _sb(176, BF), "ec": _sb(176, BF), "ga": _sb(176, BF), "gb": _sb(176, BF), "grid": _sb(352, BF),
+    "x1": _sb(C, BF), "rb": _sb(416, BF), "tt": _sb(800, BF), "ts": _sb(800, BF), "pt": _sb(32, F32),
+    "lim": _sb(2, F32), "cc": _sb(48, F32), "ee": _sb(48, F32), "ff": _sb(48, F32),
+}
+SEMAPHORES = ["nv", "na", "nt", "ng", "lx", "lu", "lw", "lv", "le", "st", "sent",
+              "ha0", "hb0", "ha1", "hb1", "arr0", "arr1"]
+
+
+def _bits(es):
+    m = 0
+    for e in es:
+        m |= 1 << e
+    return m
+
+
+def _helpers(T, topo):
+    out = {}
+    for r, c in enumerate(T.cores):
+        used = []
+        for side, n in ((0, r - 1), (1, r + 1)):
+            if 0 <= n < len(T.cores):
+                ok = [h for h in topo.cores_of(c) if T.rank_of(h) is None and h not in used and topo.may_write(h, T.cores[n])]
+                ok.sort(key=lambda h: topo.die(h) != topo.die(c))
+                used.append(ok[0])
+                out[(r, side)] = ok[0]
+    return out
+
+
+def _helper_program(g, core, T, topo, rank, side):
+    dst = T.cores[rank - 1 if side == 0 else rank + 1]
+    rid, pid = topo.addr(dst, core)
+    m = _bits(topo.engines(core, dst)[:FAR])
+    lo = 128 - TM * side
+    for t in range(ROUNDS):
+        g.wait_ge(T.sem["ha%d" % t], NEAR)
+        g.remote_dma(T["lq%d" % t][:, lo:lo + TM].bitcast(dt.uint8), T["hq%d" % t][:].bitcast(dt.uint8),
+                     T.sem["arr%d" % t], T.sem.sent, pid, rid, m)
+        g.wait_ge(T.sem["hb%d" % t], NEAR)
+        g.remote_dma(T["ls%d" % t][:, lo:lo + TM], T["hs%d" % t][:], T.sem["arr%d" % t], T.sem.sent, pid, rid, m)
+    g.wait_ge(T.sem.sent, 2 * ROUNDS * FAR)
+
+
+def rank_program(g, core, T, topo):
+    rank = T.rank_of(core)
+    helpers = _helpers(T, topo)
+    if rank is None:
+        for (r, side), h in helpers.items():
+            if h == core:
+                _helper_program(g, core, T, topo, r, side)
+        return
+    N = len(T.cores)
+    Q = {"v": g.vector, "a": g.scalar, "t": g.tensor, "g": g, "y": g.sync}
+    SEM = {"v": T.sem.nv, "a": T.sem.na, "t": T.sem.nt, "g": T.sem.ng}
+    cnt = {"v": 0, "a": 0, "t": 0, "g": 0}
+    seen = {}
+    hist = {}
+
+    def vw(name, a=0, b=None, s=1, rev=False):
+        t = T[name]
+        if b is None:
+            b = t.shape[1]
+        if rev:
+            p = t[:, b - 1::-1] if a == 0 else t[:, b - 1:a - 1:-1]
+        else:
+            p = t[:, a:b:s] if s != 1 else t[:, a:b]
+        if name == "ps":
+            return (p, [(name, a // 512 * 512, (b + 511) // 512 * 512, 1)])
+        return (p, [(name, a, b, s)])
+
+    def ind(w, o):
+        return (w[0].indirect(o[0]), w[1] + o[1])
+
+    def need(q, key, val):
+        if seen.get((q, key), 0) < val:
+            seen[(q, key)] = val
+            Q[q].wait_ge(SEM[key] if key in SEM else T.sem[key], val)
+
+    def order(q, outs, ins):
+        want = {}
+        for views, wr in ((outs, True), (ins, False)):
+            for v in views:
+                if isinstance(v, tuple):
+                    for name, a, b, s in v[1]:
+                        for (x, y, z, k, n, w) in hist.get(name, []):
+                            if x < b and a < y and not (z == s and (x - a) % s) and not (k == "t" and q == "t"):
+                                if w or wr or (name == "ps" and k != q):
+                                    want[k] = max(want.get(k, 0), n)
+        for k in want:
+            need(q, k, want[k])
+
+    def run(q, outs, ins, fn):
+        order(q, outs, ins)
+        cnt[q] += 1
+        fn().then_inc(SEM[q], 1)
+        for views, wr in ((outs, True), (ins, False)):
+            for v in views:
+                if isinstance(v, tuple):
+                    for name, a, b, s in v[1]:
+                        hist.setdefault(name, []).append((a, b, s, q, cnt[q], wr))
+
+    def ap(x):
+        return x[0] if isinstance(x, tuple) else x
+
+    def ts(o, i, s1, op0, s2=None, op1=None):
+        if op1 is None:
+            run("v", [o], [i, s1], lambda: g.vector.tensor_scalar(o[0], i[0], ap(s1), None, op0))
+        else:
+            run("v", [o], [i, s1, s2], lambda: g.vector.tensor_scalar(o[0], i[0], ap(s1), ap(s2), op0, op1))
+
+    def tt(o, a, b, op):
+        run("v", [o], [a, b], lambda: g.vector.tensor_tensor(o[0], a[0], b[0], op))
+
+    def cp(o, i):
+        run("v", [o], [i], lambda: g.vector.tensor_copy(o[0], i[0]))
+
+    def scan(o, d0, d1, op0, op1):
+        run("v", [o], [d0, d1], lambda: g.vector.tensor_tensor_scan(o[0], d0[0], d1[0], 0.0, op0, op1))
+
+    def tr(o, i):
+        run("v", [o], [i], lambda: g.vector.transpose(o[0], i[0]))
+
+    def qz(o, s, i):
+        run("v", [o, s], [i], lambda: g.vector.quantize_mx(o[0], s[0], i[0]))
+
+    def act(o, i, f=F.Copy, scale=None, bias=None):
+        if bias is not None:
+            h = F.Identity if f == F.Copy else f
+            run("a", [o], [i, bias], lambda: g.scalar.activation(o[0], i[0], h, bias=ap(bias), scale=scale))
+        elif scale is not None:
+            run("a", [o], [i], lambda: g.scalar.activation(o[0], i[0], f, scale=scale))
+        else:
+            run("a", [o], [i], lambda: g.scalar.activation(o[0], i[0], f))
+
+    def count(o, signs, i, bias):
+        run("a", [o, signs], [i, bias],
+            lambda: g.scalar.activation(signs[0], i[0], F.Sign, bias=bias[0], scale=1.0, accum_out=o[0]))
+
+    def mm(o, l, ls, r, rs):
+        run("t", [o], [l, ls, r, rs], lambda: g.tensor.matmul_mx(o[0], l[0], ls[0], r[0], rs[0], True, True))
+
+    def iota(o, pat, base=0, cm=0, whole=False):
+        if whole:
+            run("g", [o], [], lambda: g.iota(o[0], pat, base, cm))
+        else:
+            run("g", [o], [], lambda: g.iota(o[0], pat, base, cm, allow_small_or_imprecise_dtypes=True))
+
+    def sel(o, pat, base, fill, cm=0):
+        n = o[1][0][2] - o[1][0][1]
+        run("g", [o], [vw("zero")], lambda: g.affine_select(o[0], T.zero[:, 0:n], pat, A.not_equal, fill, base, cm))
+
+    g.sync.dma_start(T.xb[:], T.x[:]).then_inc(T.sem.lx, 16)
+    g.scalar.dma_start(T.ub[:], T.u[:]).then_inc(T.sem.lu, 16)
+    g.sync.dma_start(T.wq[:].bitcast(dt.uint8), T.wc[:]).then_inc(T.sem.lw, 16)
+    g.sync.dma_start(T.wsc[:], T.ws[:]).then_inc(T.sem.lw, 16)
+    g.sync.dma_start(T.vb[:], T.v[:]).then_inc(T.sem.lv, 16)
+
+    def col(i):
+        return vw("cf", i, i + 1)
+    TC, HC, PAR, T15, W16, EA, EB, EDG, HN, NA, NEH, PN, TH = [col(i) for i in range(13)]
+    TCB = vw("cb", 0, 1)
+    Z = vw("zero", 0, C)
+    run("v", [vw("zero")], [], lambda: g.vector.memset(T.zero[:], 0.0))
+    order("y", [], [vw("zero")])
+    for b in range(4):
+        g.sync.dma_start(T.eb[:, 512 * b:512 * b + 512], T.zero[:]).then_inc(T.sem.le, 16)
+    iota(vw("ci", 0, 1), [[0, 1]], 0, 1, True)
+    iota(vw("upi"), [[16, 8]], 0, 0, True)
+    iota(vw("r4"), [[0, 25], [1, 16]])
+    iota(vw("k8"), [[8, 4]])
+    at = 0
+    for a in range(12):
+        iota(vw("yf", at, at + 25 - 2 * a), [[1, 25 - 2 * a]], 33 * a)
+        at += 25 - 2 * a
+    iota(vw("yf", at, 176), [[0, 176 - at]], 384)
+    iota(vw("c24"), [[1, 24]])
+    for name, lo, hi in (("uv", 0, 1), ("uv", 385, 399), ("uv", 783, 784), ("gr", C, C + 1), ("yy", DL, DL + 1)):
+        iota(vw(name, lo, hi), [[0, hi - lo]])
+    iota(vw("kk2"), [[16, 4], [1024, 2], [1, 16]])
+    iota(vw("posi"), [[1, 192]], 8)
+    sel(vw("ta", 0, 96), [[0, 2], [1, 3], [0, 16]], -1, -1.0)
+    sel(vw("tb", 48, 144), [[0, 2], [1, 3], [0, 16]], -2, 1.0)
+    sel(vw("idm"), [[-1, 128]], 0, 1.0, 1)
+    iota(vw("sh", 48, 49), [[0, 1]], 0, 0, True)
+    for name, lo, hi, c in (("tm", 48, 96, 0), ("pa", 0, 1, 0), ("pb", 24, 25, 1), ("ec", 175, 176, 0), ("rb", 0, 16, 0), ("rb", 400, 416, 0)):
+        iota(vw(name, lo, hi), [[0, hi - lo]], c)
+
+    ts(vw("ci", 1, 2), vw("ci", 0, 1), 15, A.bitwise_and)
+    ts(vw("ci", 2, 3), vw("ci", 0, 1), 4, A.logical_shift_right, 1, A.bitwise_and)
+    ts(vw("ci", 3, 4), vw("ci", 0, 1), 1, A.bitwise_and)
+    cp(vw("upl"), vw("upi"))
+    cp(vw("cf", 0, 3), vw("ci", 1, 4))
+    cp(TCB, vw("ci", 1, 2))
+    if rank == 0 or rank == N - 1:
+        lo = 0 if rank == 0 else 128
+        for t in range(ROUNDS):
+            qz(vw("lq%d" % t, lo, lo + 128), vw("ls%d" % t, lo, lo + 128), vw("zero"))
+    ts(T15, TC, -1.0, A.mult, 15.0, A.add)
+    ts(PN, PAR, -1.0, A.mult, 1.0, A.add)
+    ts(EA, TC, 0.0, A.is_equal, 16.0, A.mult)
+    ts(EB, TC, 15.0, A.is_equal, 32.0, A.mult)
+    ts(NA, PAR, HC, A.not_equal, 400.0, A.mult)
+    ts(vw("kh", 0, 400), vw("r4"), TCB, A.is_equal, -512.0, A.mult)
+    ts(vw("kh", 400, 784), vw("r4", 0, C), TCB, A.is_equal, -512.0, A.mult)
+    ts(vw("e3"), vw("r4", 0, 48), TCB, A.is_equal, 64.0, A.mult)
+    ts(EDG, EA, EB, A.add, 48.0, A.add)
+    act(vw("k32"), vw("zero", 0, 256), scale=1.0, bias=1.0)
+    for b in range(4):
+        act(vw("zz", ZW * b, ZW * b + 16), vw("zero", 0, 16))
+        act(vw("zz", ZW * b + 400, ZW * b + 416), vw("zero", 0, 16))
+    act(vw("k32", 0, 256, 32), vw("zero", 0, 8))
+    act(W16, TC, F.Copy, 16.0)
+    act(TH, TC, scale=0.5, bias=0.25)
+    act(HN, HC, F.Copy, -512.0)
+    act(vw("kd"), vw("kh", 0, C), scale=-1.0, bias=-0.5)
+    act(vw("b8", 0, 4), vw("k8"), scale=1.0, bias=TH)
+    act(vw("kb"), Z)
+    act(vw("b8", 4, 8), vw("b8", 0, 4), F.Copy, -1.0)
+    act(vw("kb", 0, C, 16), vw("zero", 0, 24), scale=1.0, bias=512.0)
+    for e in range(3):
+        act(vw("ta", 96 + 16 * e, 112 + 16 * e), vw("e3", 0, 16), scale=1.0, bias=-1.0 * (e == 1))
+        act(vw("tb", 16 * e, 16 + 16 * e), vw("e3", 0, 16), scale=-1.0, bias=1.0 * (e == 2))
+    act(vw("tm", 0, 48), vw("e3"), F.Copy, 1.0 / 64)
+    act(vw("tm", 96, 144), vw("e3"), F.Copy, 1.0 / 64)
+    ts(NEH, NA, W16, A.add, 15.0, A.add)
+    need("v", "lu", 16)
+    qz(vw("uq"), vw("us"), vw("ub"))
+    run("v", [vw("uq2")], [vw("uq"), vw("upl")],
+        lambda: g.vector.tensor_copy(T.uq2[:, 0:128].bitcast(dt.uint32), T.uq[:, 0:128].bitcast(dt.uint32).indirect(T.upl[:, 0:8])))
+    run("v", [vw("us2")], [vw("us"), vw("upl")],
+        lambda: g.vector.tensor_copy(T.us2[:, 0:128], T.us[:, 0:128].indirect(T.upl[:, 0:8])))
+    scan(vw("yf", 176, 352), vw("kd", 0, 176), vw("yf", 0, 176), A.add, A.min)
+    ts(vw("arow"), vw("yf", 0, 176), 1.0 / 32, A.mult, -0.49, A.add)
+    ts(vw("gi", 0, 11), vw("yf", 191, 352, 16), 2.0, A.mult, T15, A.add)
+    act(vw("sf"), vw("c24", 0, 2), scale=256.0, bias=NEH)
+    act(vw("cl", 0, 24), vw("c24"), scale=8.0 / 256, bias=8.0 / 256)
+    act(vw("cl", 24, 48), vw("c24"), scale=8.0 / 256, bias=15.0 / 256)
+    act(vw("k16", 0, 400), vw("r4"), F.Sign)
+    act(vw("thr2", 128, 256), vw("kk2"), F.Abs, 0.5, HN)
+    act(vw("thr2", 0, 128), vw("thr2", 128, 256), F.Copy, -1.0)
+    need("v", "lx", 16)
+    qz(vw("aq0"), vw("as0"), vw("xb"))
+    ts(vw("gi", 12, 23), vw("gi", 0, 11), 1, A.logical_shift_right, 31, A.bitwise_and)
+    ts(vw("sl"), vw("sf"), 799.0, A.min)
+    cp(vw("gl", 0, 11), vw("gi", 12, 23))
+    ts(vw("gl", 12, 23), vw("gi", 12, 23), 7.0, A.add)
+
+    sides = [s for s in (0, 1) if (rank, s) in helpers]
+    sent = [0]
+
+    def send(t):
+        for kind, sem in (("q", "ha%d"), ("s", "hb%d")):
+            xs = []
+            for s in sides:
+                h = helpers[(rank, s)]
+                rid, pid = topo.addr(h, core)
+                es = topo.engines(core, h)
+                src, dst = T["m%s%d" % (kind, t)][:, TM * s:TM * s + TM], T["h%s%d" % (kind, t)][:]
+                if kind == "q":
+                    src, dst = src.bitcast(dt.uint8), dst.bitcast(dt.uint8)
+                xs.append(RemoteDMATransfer(dst_ids=[DstId(rid=rid, pnc=pid)], dma_engine_mask=_bits(es[NEAR * s:NEAR * s + NEAR]),
+                                            remote_sem=T.sem[sem % t], src=src, dst=dst))
+                sent[0] += NEAR
+            g.remote_dma_fused(xs, local_sem=T.sem.sent)
+
+    arrive = 2 * FAR * len(sides)
+
+    def sm(i, k=1):
+        return vw("sm", 24 * i, 24 * (i + k))
+
+    def bank(b, n):
+        return vw("ps", 512 * b, 512 * b + n)
+
+    def plane(b, a, e):
+        return vw("zz", ZW * b + a, ZW * b + e)
+
+    def lay(b):
+        act(plane(b, 16, 400), bank(b + 1, C), F.Copy, 0.0625)
+
+    def again(b):
+        act(vw("pp", C * b, C * b + C), plane(b, 16, 400))
+
+    for t in range(ROUNDS):
+        aq, asc = vw("aq%d" % t), vw("as%d" % t)
+        mm(bank(0, C), vw("uq2"), vw("us2"), aq, asc)
+        if t == 0:
+            need("t", "lw", 32)
+        for b in range(4):
+            mm(bank(b + 1, C), vw("wq", 128 * b, 128 * b + 128), vw("wsc", 128 * b, 128 * b + 128), aq, asc)
+        S, Sr = vw("sg"), vw("sg", rev=True)
+        ts(S, bank(0, C), 0.0, A.is_ge, -0.5, A.add)
+        if t > 0:
+            lay(0)
+        act(vw("ns"), S, F.Copy, -1.0)
+        lay(t)
+        scan(vw("dr"), S, Z, A.add, A.add)
+        scan(vw("rr", rev=True), Sr, Z, A.add, A.add)
+        scan(vw("uv", 1, 385), vw("dr"), Z, A.min, A.min)
+        scan(vw("uv", 399, 783, rev=True), vw("rr", rev=True), Z, A.max, A.max)
+        for i in range(8):
+            ends = vw("uv", 16, 385, 16) if i < 4 else vw("uv", 399, 783, 16)
+            count(vw("n1", i, i + 1), vw("jk", 24 * i, 24 * i + 24), ends, vw("b8", i, i + 1))
+        lay(t + 1)
+        act(vw("off", 0, 4), vw("n1", 0, 4), scale=8.0, bias=191.0)
+        act(vw("off", 4, 8), vw("n1", 4, 8), scale=8.0, bias=192.0)
+        for b in range(t + 2, 4):
+            lay(b)
+        scan(vw("hr"), S, Z, A.add, A.max)
+        scan(vw("hb", 1, 785), vw("kh"), vw("uv", 0, 784), A.add, A.max)
+        scan(vw("gr", 0, C, rev=True), vw("ns", rev=True), Z, A.add, A.max)
+        ts(vw("o16", 0, 16, 2), vw("n1"), 8.0, A.mult, 192.0, A.add)
+        ts(vw("o16", 1, 16, 2), vw("n1"), 8.0, A.mult, 192.0, A.add)
+        tt(vw("c2", 0, 128), ind(vw("hb", 16, 401), vw("o16", 0, 8)), vw("thr2", 0, 128), A.is_ge)
+        tt(vw("c2", 128, 256), ind(vw("hb", 400, 785), vw("o16", 8, 16)), vw("thr2", 128, 256), A.is_gt)
+        tr(vw("t2"), vw("c2"))
+        scan(vw("n2"), vw("k32"), vw("t2"), A.mult, A.add)
+        tt(vw("mi"), vw("n2", 31, 256, 32), vw("off"), A.add)
+        cp(vw("ml"), vw("mi"))
+        for b in range(4):
+            (cp if b < VM[t] else act)(vw("mt", b, 512, 4), ind(plane(b, 0, 416), vw("ml")))
+        mq, msc = vw("mq%d" % t), vw("ms%d" % t)
+        steps = [lambda: tt(vw("yy", DL + 1, DL + 1 + C), vw("hr"), vw("gr", 1, C + 1), A.min),
+                 lambda: scan(vw("xx", 0, C), vw("kd"), vw("yy", DL + 1, DL + 1 + C), A.add, A.min),
+                 lambda: scan(vw("yy", 0, C), vw("kd"), vw("yy", DL, DL + C), A.add, A.min)]
+        steps.insert(0 if VM[t] else 3, lambda: qz(mq, msc, vw("mt")))
+        for step in steps:
+            step()
+        order("g", [], [mq, msc])
+        send(t)
+        act(vw("lim", 0, 1), vw("uv", 384, 385), F.Relu, 1.0, 32.0)
+        act(vw("lim", 1, 2), vw("uv", 399, 400), F.Relu, -1.0, 32.0)
+        if t == 0:
+            act(vw("pos", 0, C, 2), vw("posi"), F.Copy, 1.0 / 256)
+            act(vw("pos", 1, C, 2), vw("posi"), F.Copy, 1.0 / 256)
+        again(0)
+        scan(vw("xx", C, 2 * C), vw("kb"), vw("yy", DL + 1, DL + 1 + C), A.add, A.min)
+        tt(sm(2), vw("xx", 15, C, 16), vw("yy", 15, C, 16), A.subtract)
+        tt(sm(0, 2), vw("xx", 15, 2 * C, 16), vw("yy", 15, 2 * C, 16), A.min)
+        ts(sm(3), sm(2), 96.0, A.mult, EDG, A.add)
+        ts(vw("li"), sm(0, 2), 2.0, A.mult, T15, A.add)
+        act(vw("ee", 0, 24), vw("hb", 16, 400, 16), scale=-2.0, bias=416.0)
+        act(vw("ee", 24, 48), vw("hb", 416, 785, 16), scale=2.0, bias=480.0)
+        if t == 0:
+            act(vw("k16", 400, 800), vw("r4"), F.Sign)
+        act(sm(6), sm(2), scale=177.0, bias=88.5)
+        ts(vw("cc", 0, 24), vw("hb", 16, 400, 16), 32.0, A.add, vw("lim", 0, 1), A.is_gt)
+        ts(vw("ri"), vw("li", 0, 24), 15, A.bitwise_and)
+        ts(vw("sh", 0, 48), vw("li"), 4, A.logical_shift_right)
+        tt(sm(4), sm(3), vw("ri"), A.add)
+        ts(sm(10), sm(2), 0.0, A.is_equal)
+        cp(vw("o1"), sm(4))
+        act(vw("xa"), ind(vw("ta"), vw("o1")))
+        act(vw("xc"), ind(vw("tb"), vw("o1")))
+        GL = vw("gl", 0, 11)
+        tt(vw("ea"), ind(vw("sh", 16, 49), vw("gl", 12, 23)), vw("arow"), A.is_equal)
+        ts(sm(5), vw("sh", 0, 24), -1.0, A.mult, 25.0, A.add)
+        tt(sm(8), sm(6), vw("c24"), A.add)
+        tt(sm(7), sm(5), vw("sh", 0, 24), A.mult)
+        scan(vw("ar"), vw("xa"), vw("pos"), A.add, A.min)
+        tt(sm(9), sm(7), sm(8), A.add)
+        tt(vw("pa", 1, 25), vw("ar", 15, C, 16), vw("cl", 0, 24), A.max)
+        ts(vw("cc", 24, 48), vw("hb", 416, 785, 16), vw("lim", 1, 2), A.add, 32.0, A.is_lt)
+        act(vw("ga"), ind(vw("pa", 0, 25), GL))
+        act(vw("xm"), ind(vw("tm"), vw("o1")))
+        scan(vw("br", rev=True), vw("xc", rev=True), vw("pos", rev=True), A.add, A.max)
+        cp(vw("og"), sm(9))
+        tt(vw("pb", 0, 24), vw("br", 0, C, 16), vw("cl", 24, 48), A.min)
+        act(vw("gb"), ind(vw("pb", 0, 25), GL))
+        act(vw("ec", 0, 175), vw("ea", 1, 176), scale=-1.0, bias=1.0)
+        if t == 0:
+            need("a", "le", 64)
+            for b in range(4):
+                act(vw("eb", 512 * b + b, 512 * b + 512, 4), vw("idm"))
+        again(1)
+        again(2)
+        again(3)
+        scan(vw("grid", 0, 176), vw("ea"), vw("ga"), A.add, A.min)
+        tt(vw("ff"), vw("cc"), vw("ee"), A.mult)
+        if t > 0:
+            need("v", "lv", 16)
+            qz(vw("vq"), vw("vs"), vw("vb"))
+        tt(vw("bx"), vw("br"), vw("xm"), A.mult)
+        scan(vw("grid", 176, 352, rev=True), vw("ec", rev=True), vw("gb", rev=True), A.mult, A.max)
+        tt(sm(12), vw("ff", 0, 24), vw("ff", 24, 48), A.add)
+        tt(vw("x1"), ind(vw("grid"), vw("og")), vw("ar"), A.max)
+        if t == 0:
+            qz(vw("eq"), vw("es"), vw("eb"))
+        need("t", "arr%d" % t, arrive)
+        for b in range(4):
+            mm(bank(b + 1, 128), vw("eq", 128 * b, 128 * b + 128), vw("es", 128 * b, 128 * b + 128),
+               vw("lq%d" % t, 64, 192), vw("ls%d" % t, 64, 192))
+        for b in range(4):
+            act(plane(b, 416, ZW), bank(b + 1, 128))
+        tt(vw("rb", 16, 400), vw("x1"), vw("bx"), A.min)
+        tt(sm(13), sm(12), sm(10), A.mult)
+        tr(vw("tt", 0, C), vw("rb", 16, 400))
+        tr(vw("tt", C, 800), vw("rb"))
+        scan(vw("ts"), vw("k16"), vw("tt"), A.mult, A.max)
+        ts(vw("pt"), ind(vw("ts"), vw("sl")), 512.0, A.mult, PN, A.add)
+        tt(sm(15), vw("pt", 0, 24), sm(13), A.max)
+        cp(vw("ol"), sm(15))
+        for b in range(4):
+            tt(vw("xt", b, 4 * C, 4), ind(plane(b, 0, ZW), vw("ol")), vw("pp", C * b, C * b + C), A.add)
+        qz(vw("aq%d" % (t + 1)), vw("as%d" % (t + 1)), vw("xt"))
+
+    aq, asc = "aq%d" % ROUNDS, "as%d" % ROUNDS
+    H = C // 2
+    mm(bank(0, H), vw("vq"), vw("vs"), vw(aq, 0, H), vw(asc, 0, H))
+    mm(bank(5, H), vw("vq"), vw("vs"), vw(aq, H, C), vw(asc, H, C))
+    order("y", [], [vw(aq), vw(asc)])
+    g.sync.dma_start(T.oc[:], T[aq][:].bitcast(dt.uint8)).then_inc(T.sem.st, 16)
+    cp(vw("yb", 0, H), bank(0, H))
+    act(vw("yb", H, C), bank(5, H))
+    for k in range(4):
+        g.sync.dma_start(T.osc[4 * k:4 * k + 4, :], T[asc][32 * k:32 * k + 4, :]).then_inc(T.sem.st, 16)
+    order("a", [], [vw("yb")])
+    g.scalar.dma_start(T.y[:], T.yb[:]).then_inc(T.sem.st, 16)
+    g.wait_ge(T.sem.sent, sent[0])
+    for k in cnt:
+        need("y", k, cnt[k])
+    g.sync.wait_ge(T.sem.st, 16 * 6)

@@ -3,8 +3,9 @@ from concourse.mybir import dt, AluOpType as A, ActivationFunctionType as F
 
 C, TM, ROUNDS = 384, 64, 2
 ZW = 544
-DL = C + 15
+DL = 2 * C + 30
 NEAR, FAR = 8, 8
+HALF = 256
 VM = (2, 0)
 X4, U8, BF, F32, I32, U16 = "float8_e4m3fn_x4", "uint8", "bfloat16", "float32", "int32", "uint16"
 
@@ -31,19 +32,19 @@ SCRATCH = {
     "arow": _sb(176, I32), "gi": _sb(24, I32), "gl": _sb(24, U16), "posi": _sb(192, BF), "pos": _sb(C, BF),
     "e3": _sb(48, BF), "tm": _sb(144, BF), "ta": _sb(144, BF), "tb": _sb(144, BF),
     "cl": _sb(48, BF), "sf": _sb(2, F32), "sl": _sb(2, U16),
-    "sg": _sb(C, BF), "ns": _sb(C, BF), "dr": _sb(C, BF), "rr": _sb(C, BF), "uv": _sb(800, BF), "hb": _sb(800, BF),
+    "sg": _sb(C, BF), "ns": _sb(2 * C, BF), "dr": _sb(C, BF), "rr": _sb(C, BF), "uv": _sb(800, BF), "hb": _sb(800, BF),
     "jk": _sb(192, BF), "n1": _sb(8, F32), "o16": _sb(16, U16), "off": _sb(8, F32), "c2": _sb(256, BF),
     "t2": _sb(256, BF), "n2": _sb(256, BF), "mi": _sb(8, F32), "ml": _sb(8, U16),
-    "hr": _sb(C, BF), "gr": _sb(C + 16, BF), "xx": _sb(2 * C, BF), "yy": _sb(800, BF),
+    "hr": _sb(2 * C + 16, BF), "xx": _sb(2 * C, BF), "yy": _sb(1600, BF),
     "sm": _sb(24 * 16, F32), "li": _sb(48, I32), "ri": _sb(24, I32), "sh": _sb(56, I32),
     "o1": _sb(24, U16), "og": _sb(24, U16), "ol": _sb(24, U16),
-    "xa": _sb(C, BF), "xc": _sb(C, BF), "xm": _sb(C, BF), "ar": _sb(C, BF), "br": _sb(C, BF), "bx": _sb(C, BF),
+    "xa": _sb(C, BF), "xc": _sb(C, BF), "xm": _sb(2 * C, BF), "ar": _sb(C, BF), "br": _sb(2 * C, BF),
     "pa": _sb(32, BF), "pb": _sb(32, BF),
     "ea": _sb(176, BF), "ec": _sb(176, BF), "ga": _sb(176, BF), "gb": _sb(176, BF), "grid": _sb(352, BF),
-    "x1": _sb(C, BF), "rb": _sb(416, BF), "tt": _sb(800, BF), "ts": _sb(800, BF), "pt": _sb(32, F32),
+    "rb": _sb(832, BF), "tt": _sb(800, BF), "ts": _sb(800, BF), "pt": _sb(32, F32),
     "lim": _sb(2, F32), "cc": _sb(48, F32), "ee": _sb(48, F32), "ff": _sb(48, F32),
 }
-SEMAPHORES = ["nv", "na", "nt", "ng", "lx", "lu", "lw", "lv", "le", "st", "sent",
+SEMAPHORES = ["nv", "na", "nt", "ng", "lx", "lx2", "lu", "lw", "lv", "le", "st", "sent",
               "ha0", "hb0", "ha1", "hb1", "arr0", "arr1"]
 
 
@@ -101,7 +102,8 @@ def rank_program(g, core, T, topo):
         if b is None:
             b = t.shape[1]
         if rev:
-            p = t[:, b - 1::-1] if a == 0 else t[:, b - 1:a - 1:-1]
+            e = a + (b - 1 - a) // s * s
+            p = t[:, e::-s] if a == 0 else t[:, e:a - 1:-s]
         else:
             p = t[:, a:b:s] if s != 1 else t[:, a:b]
         if name == "ps":
@@ -189,7 +191,8 @@ def rank_program(g, core, T, topo):
         n = o[1][0][2] - o[1][0][1]
         run("g", [o], [vw("zero")], lambda: g.affine_select(o[0], T.zero[:, 0:n], pat, A.not_equal, fill, base, cm))
 
-    g.sync.dma_start(T.xb[:], T.x[:]).then_inc(T.sem.lx, 16)
+    g.sync.dma_start(T.xb[:, 0:4 * HALF], T.x[:, 0:4 * HALF]).then_inc(T.sem.lx, 16)
+    g.sync.dma_start(T.xb[:, 4 * HALF:4 * C], T.x[:, 4 * HALF:4 * C]).then_inc(T.sem.lx2, 16)
     g.scalar.dma_start(T.ub[:], T.u[:]).then_inc(T.sem.lu, 16)
     g.sync.dma_start(T.wq[:].bitcast(dt.uint8), T.wc[:]).then_inc(T.sem.lw, 16)
     g.sync.dma_start(T.wsc[:], T.ws[:]).then_inc(T.sem.lw, 16)
@@ -208,21 +211,21 @@ def rank_program(g, core, T, topo):
     iota(vw("upi"), [[16, 8]], 0, 0, True)
     iota(vw("r4"), [[0, 25], [1, 16]])
     iota(vw("k8"), [[8, 4]])
+    for name, lo, hi in (("uv", 0, 1), ("uv", 385, 399), ("uv", 783, 784), ("hr", 0, 1), ("yy", DL + 2 * C, DL + 2 * C + 1)):
+        iota(vw(name, lo, hi), [[0, hi - lo]])
+    iota(vw("kk2"), [[16, 4], [1024, 2], [1, 16]])
     at = 0
     for a in range(12):
         iota(vw("yf", at, at + 25 - 2 * a), [[1, 25 - 2 * a]], 33 * a)
         at += 25 - 2 * a
     iota(vw("yf", at, 176), [[0, 176 - at]], 384)
     iota(vw("c24"), [[1, 24]])
-    for name, lo, hi in (("uv", 0, 1), ("uv", 385, 399), ("uv", 783, 784), ("gr", C, C + 1), ("yy", DL, DL + 1)):
-        iota(vw(name, lo, hi), [[0, hi - lo]])
-    iota(vw("kk2"), [[16, 4], [1024, 2], [1, 16]])
     iota(vw("posi"), [[1, 192]], 8)
     sel(vw("ta", 0, 96), [[0, 2], [1, 3], [0, 16]], -1, -1.0)
     sel(vw("tb", 48, 144), [[0, 2], [1, 3], [0, 16]], -2, 1.0)
     sel(vw("idm"), [[-1, 128]], 0, 1.0, 1)
     iota(vw("sh", 48, 49), [[0, 1]], 0, 0, True)
-    for name, lo, hi, c in (("tm", 48, 96, 0), ("pa", 0, 1, 0), ("pb", 24, 25, 1), ("ec", 175, 176, 0), ("rb", 0, 16, 0), ("rb", 400, 416, 0)):
+    for name, lo, hi, c in (("tm", 48, 96, -64), ("pa", 0, 1, 0), ("pb", 24, 25, 1), ("ec", 175, 176, 0), ("rb", 0, 32, 0), ("rb", 800, 832, 0)):
         iota(vw(name, lo, hi), [[0, hi - lo]], c)
 
     ts(vw("ci", 1, 2), vw("ci", 0, 1), 15, A.bitwise_and)
@@ -240,10 +243,12 @@ def rank_program(g, core, T, topo):
     ts(EA, TC, 0.0, A.is_equal, 16.0, A.mult)
     ts(EB, TC, 15.0, A.is_equal, 32.0, A.mult)
     ts(NA, PAR, HC, A.not_equal, 400.0, A.mult)
+    ts(EDG, EA, EB, A.add, 48.0, A.add)
     ts(vw("kh", 0, 400), vw("r4"), TCB, A.is_equal, -512.0, A.mult)
     ts(vw("kh", 400, 784), vw("r4", 0, C), TCB, A.is_equal, -512.0, A.mult)
     ts(vw("e3"), vw("r4", 0, 48), TCB, A.is_equal, 64.0, A.mult)
-    ts(EDG, EA, EB, A.add, 48.0, A.add)
+    act(vw("ns", 0, 2 * C, 2), Z)
+    act(vw("hr", 1, 2 * C, 2), Z)
     act(vw("k32"), vw("zero", 0, 256), scale=1.0, bias=1.0)
     for b in range(4):
         act(vw("zz", ZW * b, ZW * b + 16), vw("zero", 0, 16))
@@ -260,30 +265,21 @@ def rank_program(g, core, T, topo):
     for e in range(3):
         act(vw("ta", 96 + 16 * e, 112 + 16 * e), vw("e3", 0, 16), scale=1.0, bias=-1.0 * (e == 1))
         act(vw("tb", 16 * e, 16 + 16 * e), vw("e3", 0, 16), scale=-1.0, bias=1.0 * (e == 2))
-    act(vw("tm", 0, 48), vw("e3"), F.Copy, 1.0 / 64)
-    act(vw("tm", 96, 144), vw("e3"), F.Copy, 1.0 / 64)
-    ts(NEH, NA, W16, A.add, 15.0, A.add)
+    act(vw("tm", 0, 48), vw("e3"), scale=1.0, bias=-64.0)
+    act(vw("tm", 96, 144), vw("e3"), scale=1.0, bias=-64.0)
     need("v", "lu", 16)
     qz(vw("uq"), vw("us"), vw("ub"))
     run("v", [vw("uq2")], [vw("uq"), vw("upl")],
         lambda: g.vector.tensor_copy(T.uq2[:, 0:128].bitcast(dt.uint32), T.uq[:, 0:128].bitcast(dt.uint32).indirect(T.upl[:, 0:8])))
     run("v", [vw("us2")], [vw("us"), vw("upl")],
         lambda: g.vector.tensor_copy(T.us2[:, 0:128], T.us[:, 0:128].indirect(T.upl[:, 0:8])))
-    scan(vw("yf", 176, 352), vw("kd", 0, 176), vw("yf", 0, 176), A.add, A.min)
-    ts(vw("arow"), vw("yf", 0, 176), 1.0 / 32, A.mult, -0.49, A.add)
-    ts(vw("gi", 0, 11), vw("yf", 191, 352, 16), 2.0, A.mult, T15, A.add)
-    act(vw("sf"), vw("c24", 0, 2), scale=256.0, bias=NEH)
-    act(vw("cl", 0, 24), vw("c24"), scale=8.0 / 256, bias=8.0 / 256)
-    act(vw("cl", 24, 48), vw("c24"), scale=8.0 / 256, bias=15.0 / 256)
-    act(vw("k16", 0, 400), vw("r4"), F.Sign)
     act(vw("thr2", 128, 256), vw("kk2"), F.Abs, 0.5, HN)
     act(vw("thr2", 0, 128), vw("thr2", 128, 256), F.Copy, -1.0)
     need("v", "lx", 16)
-    qz(vw("aq0"), vw("as0"), vw("xb"))
-    ts(vw("gi", 12, 23), vw("gi", 0, 11), 1, A.logical_shift_right, 31, A.bitwise_and)
-    ts(vw("sl"), vw("sf"), 799.0, A.min)
-    cp(vw("gl", 0, 11), vw("gi", 12, 23))
-    ts(vw("gl", 12, 23), vw("gi", 12, 23), 7.0, A.add)
+    qz(vw("aq0", 0, HALF), vw("as0", 0, HALF), vw("xb", 0, 4 * HALF))
+    need("v", "lx2", 16)
+    qz(vw("aq0", HALF, C), vw("as0", HALF, C), vw("xb", 4 * HALF, 4 * C))
+    ts(NEH, NA, W16, A.add, 15.0, A.add)
 
     sides = [s for s in (0, 1) if (rank, s) in helpers]
     sent = [0]
@@ -320,6 +316,12 @@ def rank_program(g, core, T, topo):
     def again(b):
         act(vw("pp", C * b, C * b + C), plane(b, 16, 400))
 
+    def leave(t):
+        mq, msc = vw("mq%d" % t), vw("ms%d" % t)
+        qz(mq, msc, vw("mt"))
+        order("g", [], [mq, msc])
+        send(t)
+
     for t in range(ROUNDS):
         aq, asc = vw("aq%d" % t), vw("as%d" % t)
         mm(bank(0, C), vw("uq2"), vw("us2"), aq, asc)
@@ -327,11 +329,14 @@ def rank_program(g, core, T, topo):
             need("t", "lw", 32)
         for b in range(4):
             mm(bank(b + 1, C), vw("wq", 128 * b, 128 * b + 128), vw("wsc", 128 * b, 128 * b + 128), aq, asc)
+        if t > 0:
+            need("v", "lv", 16)
+            qz(vw("vq"), vw("vs"), vw("vb"))
         S, Sr = vw("sg"), vw("sg", rev=True)
         ts(S, bank(0, C), 0.0, A.is_ge, -0.5, A.add)
         if t > 0:
             lay(0)
-        act(vw("ns"), S, F.Copy, -1.0)
+        act(vw("ns", 1, 2 * C, 2), S)
         lay(t)
         scan(vw("dr"), S, Z, A.add, A.add)
         scan(vw("rr", rev=True), Sr, Z, A.add, A.add)
@@ -345,9 +350,13 @@ def rank_program(g, core, T, topo):
         act(vw("off", 4, 8), vw("n1", 4, 8), scale=8.0, bias=192.0)
         for b in range(t + 2, 4):
             lay(b)
-        scan(vw("hr"), S, Z, A.add, A.max)
+        scan(vw("hr", 2, 2 * C + 2, 2), S, Z, A.add, A.max)
         scan(vw("hb", 1, 785), vw("kh"), vw("uv", 0, 784), A.add, A.max)
-        scan(vw("gr", 0, C, rev=True), vw("ns", rev=True), Z, A.add, A.max)
+        scan(vw("yy", DL, DL + 2 * C, rev=True), vw("ns", rev=True), vw("hr", 0, 2 * C, rev=True), A.subtract, A.min)
+        act(vw("lim", 0, 1), vw("uv", 384, 385), F.Relu, 1.0, 32.0)
+        act(vw("lim", 1, 2), vw("uv", 399, 400), F.Relu, -1.0, 32.0)
+        act(vw("ee", 0, 24), vw("hb", 16, 400, 16), scale=-2.0, bias=416.0)
+        act(vw("ee", 24, 48), vw("hb", 416, 785, 16), scale=2.0, bias=480.0)
         ts(vw("o16", 0, 16, 2), vw("n1"), 8.0, A.mult, 192.0, A.add)
         ts(vw("o16", 1, 16, 2), vw("n1"), 8.0, A.mult, 192.0, A.add)
         tt(vw("c2", 0, 128), ind(vw("hb", 16, 401), vw("o16", 0, 8)), vw("thr2", 0, 128), A.is_ge)
@@ -358,30 +367,25 @@ def rank_program(g, core, T, topo):
         cp(vw("ml"), vw("mi"))
         for b in range(4):
             (cp if b < VM[t] else act)(vw("mt", b, 512, 4), ind(plane(b, 0, 416), vw("ml")))
-        mq, msc = vw("mq%d" % t), vw("ms%d" % t)
-        steps = [lambda: tt(vw("yy", DL + 1, DL + 1 + C), vw("hr"), vw("gr", 1, C + 1), A.min),
-                 lambda: scan(vw("xx", 0, C), vw("kd"), vw("yy", DL + 1, DL + 1 + C), A.add, A.min),
-                 lambda: scan(vw("yy", 0, C), vw("kd"), vw("yy", DL, DL + C), A.add, A.min)]
-        steps.insert(0 if VM[t] else 3, lambda: qz(mq, msc, vw("mt")))
-        for step in steps:
-            step()
-        order("g", [], [mq, msc])
-        send(t)
-        act(vw("lim", 0, 1), vw("uv", 384, 385), F.Relu, 1.0, 32.0)
-        act(vw("lim", 1, 2), vw("uv", 399, 400), F.Relu, -1.0, 32.0)
+        if VM[t]:
+            leave(t)
+        after = vw("yy", DL + 2, DL + 2 + 2 * C, 2)
+        scan(vw("xx", 0, C), vw("kd"), after, A.add, A.min)
+        scan(vw("yy", 0, 2 * C, 2), vw("kd"), vw("yy", DL, DL + 2 * C, 2), A.add, A.min)
         if t == 0:
+            scan(vw("yf", 176, 352), vw("kd", 0, 176), vw("yf", 0, 176), A.add, A.min)
+            ts(vw("arow"), vw("yf", 0, 176), 1.0 / 32, A.mult, -0.49, A.add)
+            ts(vw("gi", 0, 11), vw("yf", 191, 352, 16), 2.0, A.mult, T15, A.add)
             act(vw("pos", 0, C, 2), vw("posi"), F.Copy, 1.0 / 256)
             act(vw("pos", 1, C, 2), vw("posi"), F.Copy, 1.0 / 256)
-        again(0)
-        scan(vw("xx", C, 2 * C), vw("kb"), vw("yy", DL + 1, DL + 1 + C), A.add, A.min)
-        tt(sm(2), vw("xx", 15, C, 16), vw("yy", 15, C, 16), A.subtract)
-        tt(sm(0, 2), vw("xx", 15, 2 * C, 16), vw("yy", 15, 2 * C, 16), A.min)
+            act(vw("sf"), vw("c24", 0, 2), scale=256.0, bias=NEH)
+            act(vw("cl", 0, 24), vw("c24"), scale=8.0 / 256, bias=8.0 / 256)
+            act(vw("cl", 24, 48), vw("c24"), scale=8.0 / 256, bias=15.0 / 256)
+        scan(vw("xx", C, 2 * C), vw("kb"), after, A.add, A.min)
+        tt(sm(2), vw("xx", 15, C, 16), vw("yy", 30, 2 * C, 32), A.subtract)
+        tt(sm(0, 2), vw("xx", 15, 2 * C, 16), vw("yy", 30, 4 * C, 32), A.min)
         ts(sm(3), sm(2), 96.0, A.mult, EDG, A.add)
         ts(vw("li"), sm(0, 2), 2.0, A.mult, T15, A.add)
-        act(vw("ee", 0, 24), vw("hb", 16, 400, 16), scale=-2.0, bias=416.0)
-        act(vw("ee", 24, 48), vw("hb", 416, 785, 16), scale=2.0, bias=480.0)
-        if t == 0:
-            act(vw("k16", 400, 800), vw("r4"), F.Sign)
         act(sm(6), sm(2), scale=177.0, bias=88.5)
         ts(vw("cc", 0, 24), vw("hb", 16, 400, 16), 32.0, A.add, vw("lim", 0, 1), A.is_gt)
         ts(vw("ri"), vw("li", 0, 24), 15, A.bitwise_and)
@@ -389,6 +393,16 @@ def rank_program(g, core, T, topo):
         tt(sm(4), sm(3), vw("ri"), A.add)
         ts(sm(10), sm(2), 0.0, A.is_equal)
         cp(vw("o1"), sm(4))
+        if not VM[t]:
+            leave(t)
+        if t == 0:
+            ts(vw("gi", 12, 23), vw("gi", 0, 11), 1, A.logical_shift_right, 31, A.bitwise_and)
+            ts(vw("sl"), vw("sf"), 799.0, A.min)
+            ts(vw("gl", 12, 23), vw("gi", 12, 23), 7.0, A.add)
+            cp(vw("gl", 0, 11), vw("gi", 12, 23))
+            iota(vw("xm", 0, 2 * C, 2), [[0, C]], 256)
+            for a in (0, 400):
+                sel(vw("k16", a, a + 400), [[0, 25], [1, 16]], 0, -256.0)
         act(vw("xa"), ind(vw("ta"), vw("o1")))
         act(vw("xc"), ind(vw("tb"), vw("o1")))
         GL = vw("gl", 0, 11)
@@ -400,29 +414,26 @@ def rank_program(g, core, T, topo):
         tt(sm(9), sm(7), sm(8), A.add)
         tt(vw("pa", 1, 25), vw("ar", 15, C, 16), vw("cl", 0, 24), A.max)
         ts(vw("cc", 24, 48), vw("hb", 416, 785, 16), vw("lim", 1, 2), A.add, 32.0, A.is_lt)
-        act(vw("ga"), ind(vw("pa", 0, 25), GL))
-        act(vw("xm"), ind(vw("tm"), vw("o1")))
-        scan(vw("br", rev=True), vw("xc", rev=True), vw("pos", rev=True), A.add, A.max)
-        cp(vw("og"), sm(9))
-        tt(vw("pb", 0, 24), vw("br", 0, C, 16), vw("cl", 24, 48), A.min)
-        act(vw("gb"), ind(vw("pb", 0, 25), GL))
         act(vw("ec", 0, 175), vw("ea", 1, 176), scale=-1.0, bias=1.0)
+        act(vw("ga"), ind(vw("pa", 0, 25), GL))
+        scan(vw("br", 1, 2 * C, 2, rev=True), vw("xc", rev=True), vw("pos", rev=True), A.add, A.max)
+        cp(vw("og"), sm(9))
+        tt(vw("pb", 0, 24), vw("br", 1, 2 * C, 32), vw("cl", 24, 48), A.min)
+        act(vw("gb"), ind(vw("pb", 0, 25), GL))
+        act(vw("xm", 1, 2 * C, 2), ind(vw("tm"), vw("o1")))
         if t == 0:
             need("a", "le", 64)
             for b in range(4):
                 act(vw("eb", 512 * b + b, 512 * b + 512, 4), vw("idm"))
-        again(1)
-        again(2)
-        again(3)
+        for b in range(4):
+            again(b)
         scan(vw("grid", 0, 176), vw("ea"), vw("ga"), A.add, A.min)
         tt(vw("ff"), vw("cc"), vw("ee"), A.mult)
-        if t > 0:
-            need("v", "lv", 16)
-            qz(vw("vq"), vw("vs"), vw("vb"))
-        tt(vw("bx"), vw("br"), vw("xm"), A.mult)
         scan(vw("grid", 176, 352, rev=True), vw("ec", rev=True), vw("gb", rev=True), A.mult, A.max)
         tt(sm(12), vw("ff", 0, 24), vw("ff", 24, 48), A.add)
-        tt(vw("x1"), ind(vw("grid"), vw("og")), vw("ar"), A.max)
+        tt(vw("br", 0, 2 * C, 2), ind(vw("grid"), vw("og")), vw("ar"), A.max)
+        scan(vw("rb", 32, 800), vw("xm"), vw("br"), A.add, A.min)
+        tt(sm(13), sm(12), sm(10), A.mult)
         if t == 0:
             qz(vw("eq"), vw("es"), vw("eb"))
         need("t", "arr%d" % t, arrive)
@@ -431,31 +442,28 @@ def rank_program(g, core, T, topo):
                vw("lq%d" % t, 64, 192), vw("ls%d" % t, 64, 192))
         for b in range(4):
             act(plane(b, 416, ZW), bank(b + 1, 128))
-        tt(vw("rb", 16, 400), vw("x1"), vw("bx"), A.min)
-        tt(sm(13), sm(12), sm(10), A.mult)
-        tr(vw("tt", 0, C), vw("rb", 16, 400))
-        tr(vw("tt", C, 800), vw("rb"))
-        scan(vw("ts"), vw("k16"), vw("tt"), A.mult, A.max)
+        tr(vw("tt", 0, C), vw("rb", 33, 800, 2))
+        tr(vw("tt", C, 800), vw("rb", 1, 832, 2))
+        scan(vw("ts"), vw("k16"), vw("tt"), A.add, A.max)
         ts(vw("pt"), ind(vw("ts"), vw("sl")), 512.0, A.mult, PN, A.add)
         tt(sm(15), vw("pt", 0, 24), sm(13), A.max)
         cp(vw("ol"), sm(15))
-        for b in range(4):
-            tt(vw("xt", b, 4 * C, 4), ind(plane(b, 0, ZW), vw("ol")), vw("pp", C * b, C * b + C), A.add)
-        qz(vw("aq%d" % (t + 1)), vw("as%d" % (t + 1)), vw("xt"))
+        aq, asc = "aq%d" % (t + 1), "as%d" % (t + 1)
+        for n, (a, e) in enumerate(((0, C),) if t < ROUNDS - 1 else ((0, HALF), (HALF, C))):
+            for b in range(4):
+                tt(vw("xt", 4 * a + b, 4 * e, 4), ind(plane(b, 0, ZW), vw("ol", a // 16, e // 16)), vw("pp", C * b + a, C * b + e), A.add)
+            qz(vw(aq, a, e), vw(asc, a, e), vw("xt", 4 * a, 4 * e))
+            if t == ROUNDS - 1:
+                mm(bank(5 * n, e - a), vw("vq"), vw("vs"), vw(aq, a, e), vw(asc, a, e))
+                order("y", [], [vw(aq, a, e), vw(asc, a, e)])
+                g.sync.dma_start(T.oc[:, 4 * a:4 * e], T[aq][:, a:e].bitcast(dt.uint8)).then_inc(T.sem.st, 16)
+                (cp if n else act)(vw("yb", a, e), bank(5 * n, e - a))
+                order("a", [], [vw("yb", a, e)])
+                g.scalar.dma_start(T.y[:, a:e], T.yb[:, a:e]).then_inc(T.sem.st, 16)
 
-    aq, asc = "aq%d" % ROUNDS, "as%d" % ROUNDS
-    H = C // 2
-    mm(bank(0, H), vw("vq"), vw("vs"), vw(aq, 0, H), vw(asc, 0, H))
-    mm(bank(5, H), vw("vq"), vw("vs"), vw(aq, H, C), vw(asc, H, C))
-    order("y", [], [vw(aq), vw(asc)])
-    g.sync.dma_start(T.oc[:], T[aq][:].bitcast(dt.uint8)).then_inc(T.sem.st, 16)
-    cp(vw("yb", 0, H), bank(0, H))
-    act(vw("yb", H, C), bank(5, H))
     for k in range(4):
         g.sync.dma_start(T.osc[4 * k:4 * k + 4, :], T[asc][32 * k:32 * k + 4, :]).then_inc(T.sem.st, 16)
-    order("a", [], [vw("yb")])
-    g.scalar.dma_start(T.y[:], T.yb[:]).then_inc(T.sem.st, 16)
     g.wait_ge(T.sem.sent, sent[0])
     for k in cnt:
         need("y", k, cnt[k])
-    g.sync.wait_ge(T.sem.st, 16 * 6)
+    g.sync.wait_ge(T.sem.st, 16 * 8)

@@ -2,11 +2,12 @@ from concourse.bass import DstId, RemoteDMATransfer
 from concourse.mybir import dt, AluOpType as A, ActivationFunctionType as F
 
 C, TM, ROUNDS = 384, 64, 2
-ZW = 544
-DL = 2 * C + 30
+ZW = 528
+P0, DR = 68, 454
+GF = 784
 NEAR, FAR = 8, 8
 HALF = 256
-VM = (2, 0)
+PIECES = ((0, HALF), (HALF, C))
 X4, U8, BF, F32, I32, U16 = "float8_e4m3fn_x4", "uint8", "bfloat16", "float32", "int32", "uint16"
 
 
@@ -19,33 +20,34 @@ SCRATCH = {
     "aq0": _sb(C, X4), "as0": _sb(C, U8), "aq1": _sb(C, X4), "as1": _sb(C, U8), "aq2": _sb(C, X4), "as2": _sb(C, U8),
     "uq": _sb(128, X4), "us": _sb(128, U8), "uq2": _sb(128, X4), "us2": _sb(128, U8),
     "vq": _sb(128, X4), "vs": _sb(128, U8), "wq": _sb(512, X4), "wsc": _sb(512, U8),
-    "eb": _sb(2048, BF), "eq": _sb(512, X4), "es": _sb(512, U8),
-    "zz": _sb(4 * ZW, BF), "xt": _sb(4 * C, BF), "mt": _sb(512, BF), "yb": _sb(C, F32), "pp": _sb(4 * C, BF),
+    "eb": _sb(528, BF), "eq": _sb(512, X4), "es": _sb(512, U8),
+    "zz": _sb(ROUNDS * 4 * ZW, BF), "xt": _sb(4 * C, BF), "mt": _sb(512, BF), "yb": _sb(C, F32), "pp": _sb(4 * C, BF),
     "mq0": _sb(128, X4), "ms0": _sb(128, U8), "mq1": _sb(128, X4), "ms1": _sb(128, U8),
     "hq0": _sb(64, X4), "hs0": _sb(64, U8), "hq1": _sb(64, X4), "hs1": _sb(64, U8),
     "lq0": _sb(256, X4), "ls0": _sb(256, U8), "lq1": _sb(256, X4), "ls1": _sb(256, U8),
-    "ps": ("psum", [128, 512 * 6], F32),
-    "zero": _sb(512, BF), "ci": _sb(16, I32), "cf": _sb(16, F32), "cb": _sb(2, BF), "r4": _sb(400, BF),
-    "kh": _sb(784, BF), "kd": _sb(C, BF), "kb": _sb(C, BF), "k16": _sb(800, BF), "k32": _sb(256, BF),
-    "k8": _sb(4, F32), "b8": _sb(8, F32), "kk2": _sb(128, F32), "thr2": _sb(256, BF), "idm": _sb(128, BF),
-    "upi": _sb(8, I32), "upl": _sb(8, U16), "c24": _sb(24, F32), "yf": _sb(352, F32),
-    "arow": _sb(176, I32), "gi": _sb(24, I32), "gl": _sb(24, U16), "posi": _sb(192, BF), "pos": _sb(C, BF),
-    "e3": _sb(48, BF), "tm": _sb(144, BF), "ta": _sb(144, BF), "tb": _sb(144, BF),
-    "cl": _sb(48, BF), "sf": _sb(2, F32), "sl": _sb(2, U16),
-    "sg": _sb(C, BF), "ns": _sb(2 * C, BF), "dr": _sb(C, BF), "rr": _sb(C, BF), "uv": _sb(800, BF), "hb": _sb(800, BF),
-    "jk": _sb(192, BF), "n1": _sb(8, F32), "o16": _sb(16, U16), "off": _sb(8, F32), "c2": _sb(256, BF),
-    "t2": _sb(256, BF), "n2": _sb(256, BF), "mi": _sb(8, F32), "ml": _sb(8, U16),
-    "hr": _sb(2 * C + 16, BF), "xx": _sb(2 * C, BF), "yy": _sb(1600, BF),
-    "sm": _sb(24 * 16, F32), "li": _sb(48, I32), "ri": _sb(24, I32), "sh": _sb(56, I32),
-    "o1": _sb(24, U16), "og": _sb(24, U16), "ol": _sb(24, U16),
-    "xa": _sb(C, BF), "xc": _sb(C, BF), "xm": _sb(2 * C, BF), "ar": _sb(C, BF), "br": _sb(2 * C, BF),
-    "pa": _sb(32, BF), "pb": _sb(32, BF),
-    "ea": _sb(176, BF), "ec": _sb(176, BF), "ga": _sb(176, BF), "gb": _sb(176, BF), "grid": _sb(352, BF),
-    "rb": _sb(832, BF), "tt": _sb(800, BF), "ts": _sb(800, BF), "pt": _sb(32, F32),
-    "lim": _sb(2, F32), "cc": _sb(48, F32), "ee": _sb(48, F32), "ff": _sb(48, F32),
+    "ps": ("psum", [128, 512 * 8], F32),
+    "zero": _sb(800, BF), "ci": _sb(16, I32), "cf": _sb(24, F32), "cb": _sb(2, BF), "r4": _sb(C, BF),
+    "kh": _sb(C, BF), "kd": _sb(C, BF), "kd2": _sb(C, BF), "k16": _sb(800, BF), "hi": _sb(128, BF),
+    "ka": _sb(128, BF), "kb": _sb(128, BF), "kc": _sb(8, F32), "kk2": _sb(256, F32), "thr": _sb(256, BF),
+    "upi": _sb(8, I32), "upl": _sb(8, U16), "yf": _sb(352, F32), "arow": _sb(192, BF),
+    "gi": _sb(24, I32), "gl": _sb(24, U16), "posi": _sb(192, BF), "pos": _sb(C, BF),
+    "ta": _sb(128, BF), "tb": _sb(128, BF), "tm": _sb(128, BF), "rsf": _sb(192, BF), "rsb": _sb(176, BF),
+    "sf": _sb(4, F32), "sl": _sb(4, U16), "vi": _sb(64, BF),
+    "sg": _sb(C, BF), "dv": _sb(400, BF), "lr": _sb(400, BF), "rr": _sb(400, BF), "sd": _sb(C, BF), "dd": _sb(C, BF),
+    "th": _sb(8, F32), "jk": _sb(192, BF), "n1": _sb(8, F32), "o16": _sb(16, U16), "off": _sb(8, F32),
+    "vl": _sb(32, F32), "vr": _sb(32, F32), "c2": _sb(256, BF), "t2": _sb(256, BF), "n2": _sb(256, BF),
+    "mi": _sb(8, F32), "ml": _sb(8, U16), "sm": _sb(24 * 8, F32), "sb": _sb(32 * 5, BF), "al": _sb(2, F32),
+    "e0": _sb(96, F32), "e1": _sb(104, F32), "e2": _sb(96, F32), "f0": _sb(96, F32), "f1": _sb(96, F32), "f2": _sb(96, F32),
+    "o1": _sb(24, U16), "og": _sb(24, U16), "ol": _sb(32, U16),
+    "xa": _sb(C, BF), "xc": _sb(C, BF), "ar": _sb(1168, BF), "br": _sb(1168, BF),
+    "ea": _sb(176, BF), "ec": _sb(176, BF), "ga": _sb(176, BF), "gb": _sb(176, BF), "vt": _sb(GF + 352, BF),
+    "rb": _sb(1248, BF), "tt": _sb(800, BF), "ts": _sb(800, BF),
 }
-SEMAPHORES = ["nv", "na", "nt", "ng", "lx", "lx2", "lu", "lw", "lv", "le", "st", "sent",
-              "ha0", "hb0", "ha1", "hb1", "arr0", "arr1"]
+DMAS = ["lxa", "lxb", "lu", "lw", "ls", "lv", "z0", "z1", "z2", "z3", "z4", "p0", "p1", "p2", "p3"]
+SEMAPHORES = ["nv", "na", "nt", "ng", "st", "sent", "ha0", "hb0", "ha1", "hb1", "arr0", "arr1"] + DMAS
+PLAN = """
+zero:v lxa:y ci:g lu:y lxb:y r4:g lw:y ls:y c1:v c2:v c3:v zz67:a z3:y zz65:v z0:y zz64:a f4:v z2:y f9:a z4:y cb:v f8:a z1:y f1:v f13:a cf:v upi:g hn:v pn:a zz452:a hi:g kh:v f17:v tm1:v thc:v kd2:a kk0:g na:v f16:v f14:v ka:v upl:v zz66:v t15:a yf5:g tm0:v f10:a kd:v kb:a yf3:g bo:a xqa:v b1:a yf8:g w16:a yf11:g uq:v kc1:g f12:v yf6:g uq2:v us2:a kk1:g zq0:v ka1:a b2:a zz453:a kc0:g xqb:v 0.ms0:t yf9:g thr:a sf1:v f11:v yf7:g tao:v 0.ms1:t tm:v tac:v f5:g f0:v 0.sg0:a tbo:v yf1:g tbc:v f15:v yf12:g bs:v 0.sg1:a yf0:g kc:a 0.dl:v zz0:a 0.mp00:t kb1:a 0.dr:v yf10:g 0.sd:v 0.nd:a nb:g 0.th1:a 0.mp11:t 0.R:v 0.qb:a yf2:g 0.lay00:a 0.mp02:t 0.L:v yf4:g posi:g 0.s1:v 0.n5:a 0.th0:v 0.n7:a 0.mp10:t 0.q16:v 0.n6:a 0.dd:v 0.n4:a 0.mp12:t 0.n3:a 0.base:v 0.n0:a 0.s2:v 0.mp03:t f2:g 0.n2:a 0.al:v 0.hv:v 0.n1:a eb:g yd:v 0.lay02:a 0.mp13:t 0.o160:v 0.o161:v 0.vl:a 0.bn:v 0.mp01:t 0.q2:a 0.vr:v ari:a 0.hr:v 0.c20:v 0.b0:a 0.of0:a 0.open:a 0.c21:v 0.q1:a 0.lay10:a 0.ow:a 0.of1:v 0.lay12:a 0.t20:v 0.t21:v 0.lay01:a vi:g gi0:v 0.n20:v 0.pp2:y 0.n21:v arow:v 0.lay13:a f7:g gi1:v 0.es:a 0.mi:v 0.lay11:a 0.o1:v pos0:v 0.lay03:a 0.ml:v 0.de:v 0.pp1:y 0.cc:v lv:y 0.mt2:a gl1:v 0.vi:v gl0:v 0.pp3:y pos1:v 0.pp0:y 0.mt3:a 0.ab:v f6:g 0.mt1:v 0.mt0:a 0.ea:v 0.xa:a 0.mq:v rsf:v 0.sendq:g 0.xc:v 0.rp:a 0.v2:a 0.xm:a 0.ec:v 0.ar:v rsb:a 0.sends:g 0.br:v 0.sq:a vt0:a 0.ga:v 0.arr:- vt1:a 0.gb:v 0.ogs:v vt2:a 0.gf:v 0.gr:v vt4:a vt3:a 0.og:v eq3:v 0.lk0:a sf0:v eq0:v eq1:v sl0:v eq2:v 0.lk1:a sl1:v 0.rb0:v f3:a 0.rb1:v 0.t2a:v 0.t1a:v 0.mu1:t 0.t2b:v 0.t1b:v 0.mu3:t 0.tsa:v 0.ul1:a 0.mu0:t 0.tsb:v 0.mu2:t 0.ur1:a 0.ola:v 0.ul0:a 0.ul3:a 0.olb:v 0.x01:v 0.ur0:a 0.ur3:a 0.ul2:a 0.ur2:a 0.x11:v 0.x03:v 0.x00:v 0.x02:v 0.x13:v 0.aq0:v 0.x12:v 1.ms0:t 0.x10:v 1.mp00:t 1.sg0:a 0.aq1:v vq:v 1.ms1:t 1.lay00:a 1.dl:v 1.mp11:t 1.sg1:a 1.nd:v 1.mp02:t 1.th0:a 1.dr:v 1.mp10:t 1.sd:v 1.th1:a 1.mp01:t 1.L:v 1.q1:a 1.al:a 1.open:a 1.R:v 1.s1:a 1.qb:a 1.mp13:t 1.n3:a 1.dd:v 1.n2:a 1.mp03:t 1.n1:a zq1:v 1.n6:a 1.n5:a 1.q16:v 1.n4:a 1.hv:v 1.mp12:t 1.n7:a 1.base:v 1.lay11:v 1.n0:a 1.es:a 1.vl:v 1.vr:a 1.of1:a 1.o160:v 1.q2:a 1.o161:v 1.bn:a 1.vi:v 1.lay01:a 1.b0:v 1.c20:v 1.lay12:a 1.c21:v 1.of0:a 1.pp1:y 1.ow:a 1.lay02:a 1.t20:v 1.de:v 1.t21:v 1.lay10:a 1.n20:v 1.s2:v 1.ab:a 1.pp2:y 1.lay03:a 1.n21:v 1.hr:v 1.mi:v 1.lay13:a 1.rp:v 1.sq:a 1.ml:v 1.v2:a 1.o1:v 1.pp3:y 1.cc:v 1.pp0:y 1.mt0:a 1.mt2:v 1.xa:v 1.mt3:a 1.mt1:a 1.xc:a 1.mq:v 1.ea:v 1.sendq:g 1.ar:v 1.xm:a 1.br:v 1.sends:g 1.ogs:v 1.ec:v 1.ga:v 1.arr:- 1.gb:v 1.og:v 1.gf:v 1.gr:v 1.lk1:a 1.lk0:v 1.rb1:v 1.rb0:v 1.t1a:v 1.t2a:v 1.t2b:v 1.mu0:t 1.t1b:v 1.tsa:v 1.mu1:t 1.ul0:a 1.mu2:t 1.tsb:v 1.ola:v 1.mu3:t 1.ur0:a 1.olb:v 1.ul2:a 1.ul1:a 1.x00:v 1.ul3:a 1.ur2:a 1.ur1:a 1.ur3:a 1.x02:v 1.x03:v 1.x01:v 1.x10:v 1.aq0:v 1.x11:v 1.my0:t 1.oc0:y 1.x12:v 1.x13:v 1.yb0:a 1.aq1:v 1.y0:y 1.osc0:a 1.my1:t 1.osc1:y 1.osc3:a 1.oc1:a 1.osc2:a 1.yb1:v 1.y1:a
+"""
 
 
 def _bits(es):
@@ -82,20 +84,14 @@ def _helper_program(g, core, T, topo, rank, side):
     g.wait_ge(T.sem.sent, 2 * ROUNDS * FAR)
 
 
-def rank_program(g, core, T, topo):
-    rank = T.rank_of(core)
-    helpers = _helpers(T, topo)
-    if rank is None:
-        for (r, side), h in helpers.items():
-            if h == core:
-                _helper_program(g, core, T, topo, r, side)
-        return
+def _meet(u, v):
+    return u[0] == v[0] and u[1] < v[2] and v[1] < u[2] and not (u[3] == v[3] and (u[1] - v[1]) % u[3])
+
+
+def _calls(g, core, T, topo, rank, helpers):
     N = len(T.cores)
-    Q = {"v": g.vector, "a": g.scalar, "t": g.tensor, "g": g, "y": g.sync}
-    SEM = {"v": T.sem.nv, "a": T.sem.na, "t": T.sem.nt, "g": T.sem.ng}
-    cnt = {"v": 0, "a": 0, "t": 0, "g": 0}
-    seen = {}
-    hist = {}
+    ops = []
+    tag = [""]
 
     def vw(name, a=0, b=None, s=1, rev=False):
         t = T[name]
@@ -103,7 +99,7 @@ def rank_program(g, core, T, topo):
             b = t.shape[1]
         if rev:
             e = a + (b - 1 - a) // s * s
-            p = t[:, e::-s] if a == 0 else t[:, e:a - 1:-s]
+            p = t[:, e::-s] if a < s else t[:, e:a - 1:-s]
         else:
             p = t[:, a:b:s] if s != 1 else t[:, a:b]
         if name == "ps":
@@ -113,357 +109,375 @@ def rank_program(g, core, T, topo):
     def ind(w, o):
         return (w[0].indirect(o[0]), w[1] + o[1])
 
-    def need(q, key, val):
-        if seen.get((q, key), 0) < val:
-            seen[(q, key)] = val
-            Q[q].wait_ge(SEM[key] if key in SEM else T.sem[key], val)
-
-    def order(q, outs, ins):
-        want = {}
-        for views, wr in ((outs, True), (ins, False)):
-            for v in views:
-                if isinstance(v, tuple):
-                    for name, a, b, s in v[1]:
-                        for (x, y, z, k, n, w) in hist.get(name, []):
-                            if x < b and a < y and not (z == s and (x - a) % s) and not (k == "t" and q == "t"):
-                                if w or wr or (name == "ps" and k != q):
-                                    want[k] = max(want.get(k, 0), n)
-        for k in want:
-            need(q, k, want[k])
-
-    def run(q, outs, ins, fn):
-        order(q, outs, ins)
-        cnt[q] += 1
-        fn().then_inc(SEM[q], 1)
-        for views, wr in ((outs, True), (ins, False)):
-            for v in views:
-                if isinstance(v, tuple):
-                    for name, a, b, s in v[1]:
-                        hist.setdefault(name, []).append((a, b, s, q, cnt[q], wr))
+    def op(name, fns, outs, ins, sem=None):
+        cols = [[c for v in vs if isinstance(v, tuple) for c in v[1]] for vs in (outs, ins)]
+        ops.append((tag[0] + name, fns, cols[0], cols[1], sem))
 
     def ap(x):
         return x[0] if isinstance(x, tuple) else x
 
-    def ts(o, i, s1, op0, s2=None, op1=None):
+    def ts(n, o, i, s1, op0, s2=None, op1=None):
         if op1 is None:
-            run("v", [o], [i, s1], lambda: g.vector.tensor_scalar(o[0], i[0], ap(s1), None, op0))
+            op(n, {"v": lambda: g.vector.tensor_scalar(o[0], i[0], ap(s1), None, op0)}, [o], [i, s1])
         else:
-            run("v", [o], [i, s1, s2], lambda: g.vector.tensor_scalar(o[0], i[0], ap(s1), ap(s2), op0, op1))
+            op(n, {"v": lambda: g.vector.tensor_scalar(o[0], i[0], ap(s1), ap(s2), op0, op1)}, [o], [i, s1, s2])
 
-    def tt(o, a, b, op):
-        run("v", [o], [a, b], lambda: g.vector.tensor_tensor(o[0], a[0], b[0], op))
+    def tt(n, o, a, b, f):
+        op(n, {"v": lambda: g.vector.tensor_tensor(o[0], a[0], b[0], f)}, [o], [a, b])
 
-    def cp(o, i):
-        run("v", [o], [i], lambda: g.vector.tensor_copy(o[0], i[0]))
+    def cp(n, o, i):
+        op(n, {"v": lambda: g.vector.tensor_copy(o[0], i[0])}, [o], [i])
 
-    def scan(o, d0, d1, op0, op1):
-        run("v", [o], [d0, d1], lambda: g.vector.tensor_tensor_scan(o[0], d0[0], d1[0], 0.0, op0, op1))
+    def mv(n, o, i):
+        op(n, {"a": lambda: g.scalar.activation(o[0], i[0], F.Copy), "v": lambda: g.vector.tensor_copy(o[0], i[0])}, [o], [i])
 
-    def tr(o, i):
-        run("v", [o], [i], lambda: g.vector.transpose(o[0], i[0]))
-
-    def qz(o, s, i):
-        run("v", [o, s], [i], lambda: g.vector.quantize_mx(o[0], s[0], i[0]))
-
-    def act(o, i, f=F.Copy, scale=None, bias=None):
-        if bias is not None:
-            h = F.Identity if f == F.Copy else f
-            run("a", [o], [i, bias], lambda: g.scalar.activation(o[0], i[0], h, bias=ap(bias), scale=scale))
-        elif scale is not None:
-            run("a", [o], [i], lambda: g.scalar.activation(o[0], i[0], f, scale=scale))
+    def lin(n, o, i, scale, bias=None):
+        if bias is None:
+            op(n, {"a": lambda: g.scalar.activation(o[0], i[0], F.Copy, scale=scale),
+                   "v": lambda: g.vector.tensor_scalar(o[0], i[0], scale, None, A.mult)}, [o], [i])
         else:
-            run("a", [o], [i], lambda: g.scalar.activation(o[0], i[0], f))
+            op(n, {"a": lambda: g.scalar.activation(o[0], i[0], F.Identity, bias=ap(bias), scale=scale),
+                   "v": lambda: g.vector.tensor_scalar(o[0], i[0], scale, ap(bias), A.mult, A.add)}, [o], [i, bias])
 
-    def count(o, signs, i, bias):
-        run("a", [o, signs], [i, bias],
-            lambda: g.scalar.activation(signs[0], i[0], F.Sign, bias=bias[0], scale=1.0, accum_out=o[0]))
+    def fill(n, o, c, k):
+        fns = {"v": lambda: g.vector.memset(o[0], c)}
+        if n != "zero" and k > 1:
+            fns["a"] = lambda: g.scalar.activation(o[0], T.zero[:, 0:k], F.Identity, bias=c, scale=1.0)
+        if c == int(c):
+            fns["g"] = lambda: g.iota(o[0], [[0, k]], int(c), 0, allow_small_or_imprecise_dtypes=True)
+        op(n, fns, [o], [] if n == "zero" else [vw("zero")])
 
-    def mm(o, l, ls, r, rs):
-        run("t", [o], [l, ls, r, rs], lambda: g.tensor.matmul_mx(o[0], l[0], ls[0], r[0], rs[0], True, True))
+    def scan(n, o, d0, d1, op0, op1, init=0.0):
+        op(n, {"v": lambda: g.vector.tensor_tensor_scan(o[0], d0[0], d1[0], init, op0, op1)}, [o], [d0, d1])
 
-    def iota(o, pat, base=0, cm=0, whole=False):
+    def tr(n, o, i):
+        op(n, {"v": lambda: g.vector.transpose(o[0], i[0])}, [o], [i])
+
+    def qz(n, o, s, i):
+        op(n, {"v": lambda: g.vector.quantize_mx(o[0], s[0], i[0])}, [o, s], [i])
+
+    def act(n, o, i, f, scale, bias):
+        op(n, {"a": lambda: g.scalar.activation(o[0], i[0], f, bias=ap(bias), scale=ap(scale))}, [o], [i, scale, bias])
+
+    def count(n, o, signs, i, scale, bias):
+        op(n, {"a": lambda: g.scalar.activation(signs[0], i[0], F.Sign, bias=bias[0], scale=scale, accum_out=o[0])},
+           [o, signs], [i, bias])
+
+    def mm(n, o, l, ls, r, rs):
+        op(n, {"t": lambda: g.tensor.matmul_mx(o[0], l[0], ls[0], r[0], rs[0], True, True)}, [o], [l, ls, r, rs])
+
+    def iota(n, o, pat, base=0, cm=0, whole=False):
         if whole:
-            run("g", [o], [], lambda: g.iota(o[0], pat, base, cm))
+            op(n, {"g": lambda: g.iota(o[0], pat, base, cm)}, [o], [])
         else:
-            run("g", [o], [], lambda: g.iota(o[0], pat, base, cm, allow_small_or_imprecise_dtypes=True))
+            op(n, {"g": lambda: g.iota(o[0], pat, base, cm, allow_small_or_imprecise_dtypes=True)}, [o], [])
 
-    def sel(o, pat, base, fill, cm=0):
-        n = o[1][0][2] - o[1][0][1]
-        run("g", [o], [vw("zero")], lambda: g.affine_select(o[0], T.zero[:, 0:n], pat, A.not_equal, fill, base, cm))
+    def dma(n, o, i, outs, ins, sem):
+        op(n, {"y": lambda: g.sync.dma_start(o, i), "a": lambda: g.scalar.dma_start(o, i)}, outs, ins, sem)
 
-    g.sync.dma_start(T.xb[:, 0:4 * HALF], T.x[:, 0:4 * HALF]).then_inc(T.sem.lx, 16)
-    g.sync.dma_start(T.xb[:, 4 * HALF:4 * C], T.x[:, 4 * HALF:4 * C]).then_inc(T.sem.lx2, 16)
-    g.scalar.dma_start(T.ub[:], T.u[:]).then_inc(T.sem.lu, 16)
-    g.sync.dma_start(T.wq[:].bitcast(dt.uint8), T.wc[:]).then_inc(T.sem.lw, 16)
-    g.sync.dma_start(T.wsc[:], T.ws[:]).then_inc(T.sem.lw, 16)
-    g.sync.dma_start(T.vb[:], T.v[:]).then_inc(T.sem.lv, 16)
+    for n, (a, e) in zip("ab", PIECES):
+        dma("lx" + n, T.xb[:, 4 * a:4 * e], T.x[:, 4 * a:4 * e], [vw("xb", 4 * a, 4 * e)], [], "lx" + n)
+    dma("lu", T.ub[:], T.u[:], [vw("ub")], [], "lu")
+    dma("lw", T.wq[:].bitcast(dt.uint8), T.wc[:], [vw("wq")], [], "lw")
+    dma("ls", T.wsc[:], T.ws[:], [vw("wsc")], [], "ls")
+    dma("lv", T.vb[:], T.v[:], [vw("vb")], [], "lv")
 
     def col(i):
         return vw("cf", i, i + 1)
-    TC, HC, PAR, T15, W16, EA, EB, EDG, HN, NA, NEH, PN, TH = [col(i) for i in range(13)]
+    TC, HC, PAR, T15, PN, NA, BS, BO, B1, B2, HN, W16, TINY, SQ, TH = [col(i) for i in range(15)]
     TCB = vw("cb", 0, 1)
-    Z = vw("zero", 0, C)
-    run("v", [vw("zero")], [], lambda: g.vector.memset(T.zero[:], 0.0))
-    order("y", [], [vw("zero")])
-    for b in range(4):
-        g.sync.dma_start(T.eb[:, 512 * b:512 * b + 512], T.zero[:]).then_inc(T.sem.le, 16)
-    iota(vw("ci", 0, 1), [[0, 1]], 0, 1, True)
-    iota(vw("upi"), [[16, 8]], 0, 0, True)
-    iota(vw("r4"), [[0, 25], [1, 16]])
-    iota(vw("k8"), [[8, 4]])
-    for name, lo, hi in (("uv", 0, 1), ("uv", 385, 399), ("uv", 783, 784), ("hr", 0, 1), ("yy", DL + 2 * C, DL + 2 * C + 1)):
-        iota(vw(name, lo, hi), [[0, hi - lo]])
-    iota(vw("kk2"), [[16, 4], [1024, 2], [1, 16]])
+    fill("zero", vw("zero"), 0.0, 800)
+    for n, (name, a, e) in enumerate((("k16", 0, 800), ("br", 0, 800), ("br", 800, 1168), ("rb", 0, 48), ("rb", 1200, 1248))):
+        dma("z%d" % n, T[name][:, a:e], T.zero[:, 0:e - a], [vw(name, a, e)], [vw("zero")], "z%d" % n)
+    iota("ci", vw("ci", 0, 1), [[0, 1]], 0, 1, True)
+    iota("upi", vw("upi"), [[16, 8]], 0, 0, True)
+    iota("r4", vw("r4"), [[0, 24], [1, 16]])
+    iota("kc0", vw("kc", 0, 4), [[16, 4]], -48)
+    iota("kc1", vw("kc", 4, 8), [[-16, 4]])
+    iota("kk0", vw("kk2", 0, 128), [[-16, 4], [2048, 2], [1, 16]], 48)
+    iota("kk1", vw("kk2", 128, 256), [[16, 4], [2048, 2], [1, 16]])
+    iota("hi", vw("hi"), [[0, 4], [1, 2], [0, 16]])
     at = 0
     for a in range(12):
-        iota(vw("yf", at, at + 25 - 2 * a), [[1, 25 - 2 * a]], 33 * a)
+        iota("yf%d" % a, vw("yf", at, at + 25 - 2 * a), [[1, 25 - 2 * a]], 33 * a)
         at += 25 - 2 * a
-    iota(vw("yf", at, 176), [[0, 176 - at]], 384)
-    iota(vw("c24"), [[1, 24]])
-    iota(vw("posi"), [[1, 192]], 8)
-    sel(vw("ta", 0, 96), [[0, 2], [1, 3], [0, 16]], -1, -1.0)
-    sel(vw("tb", 48, 144), [[0, 2], [1, 3], [0, 16]], -2, 1.0)
-    sel(vw("idm"), [[-1, 128]], 0, 1.0, 1)
-    iota(vw("sh", 48, 49), [[0, 1]], 0, 0, True)
-    for name, lo, hi, c in (("tm", 48, 96, -64), ("pa", 0, 1, 0), ("pb", 24, 25, 1), ("ec", 175, 176, 0), ("rb", 0, 32, 0), ("rb", 800, 832, 0)):
-        iota(vw(name, lo, hi), [[0, hi - lo]], c)
+    iota("yf12", vw("yf", at, 176), [[0, 176 - at]], 13 * 32)
+    iota("nb", vw("f1", 0, 96, 4), [[-1, 24]])
+    iota("posi", vw("posi"), [[1, 192]], P0 // 2 - 32)
+    iota("vi", vw("vi"), [[1, 32], [0, 2]])
+    op("eb", {"g": lambda: g.affine_select(T.eb[:], T.zero[:, 0:528], [[-1, 528]], A.not_equal, 1.0, 3, 4)},
+       [vw("eb")], [vw("zero")])
+    for n, (name, a, e, s, c) in enumerate((
+            ("dv", 192, 193, 1, 0.0), ("ar", 1, 2, 1, -2.0), ("br", 1153, 1154, 1, 2.0), ("k16", 0, 800, 16, -256.0),
+            ("vl", 24, 25, 1, 1000.0), ("vr", 0, 1, 1, 1000.0), ("ar", 0, 1156, 3, 64.0), ("ar", 2, 1156, 3, -64.0),
+            ("arow", 0, 16, 1, 77.0),
+            ("rsf", 176, 192, 1, 0.0), ("e0", 0, 96, 4, 0.0), ("e0", 1, 96, 4, 1.0), ("e0", 3, 96, 4, -1.0),
+            ("f0", 0, 96, 4, -1e6), ("f0", 3, 96, 4, 0.0), ("f1", 1, 96, 4, -1e6),
+            ("cf", 12, 13, 1, 1e-37), ("cf", 13, 14, 1, -204.5))):
+        fill("f%d" % n, vw(name, a, e, s), c, len(range(a, e, s)))
+    for c in (0, 64, 65, 66, 67, P0 + C, P0 + C + 1):
+        fill("zz%d" % c, vw("zz", c, 4 * ROUNDS * ZW, ZW), 0.0, 4 * ROUNDS)
 
-    ts(vw("ci", 1, 2), vw("ci", 0, 1), 15, A.bitwise_and)
-    ts(vw("ci", 2, 3), vw("ci", 0, 1), 4, A.logical_shift_right, 1, A.bitwise_and)
-    ts(vw("ci", 3, 4), vw("ci", 0, 1), 1, A.bitwise_and)
-    cp(vw("upl"), vw("upi"))
-    cp(vw("cf", 0, 3), vw("ci", 1, 4))
-    cp(TCB, vw("ci", 1, 2))
+    ts("c1", vw("ci", 1, 2), vw("ci", 0, 1), 15, A.bitwise_and)
+    ts("c2", vw("ci", 2, 3), vw("ci", 0, 1), 4, A.logical_shift_right, 1, A.bitwise_and)
+    ts("c3", vw("ci", 3, 4), vw("ci", 0, 1), 1, A.bitwise_and)
+    cp("upl", vw("upl"), vw("upi"))
+    cp("cf", vw("cf", 0, 3), vw("ci", 1, 4))
+    cp("cb", TCB, vw("ci", 1, 2))
     if rank == 0 or rank == N - 1:
         lo = 0 if rank == 0 else 128
         for t in range(ROUNDS):
-            qz(vw("lq%d" % t, lo, lo + 128), vw("ls%d" % t, lo, lo + 128), vw("zero"))
-    ts(T15, TC, -1.0, A.mult, 15.0, A.add)
-    ts(PN, PAR, -1.0, A.mult, 1.0, A.add)
-    ts(EA, TC, 0.0, A.is_equal, 16.0, A.mult)
-    ts(EB, TC, 15.0, A.is_equal, 32.0, A.mult)
-    ts(NA, PAR, HC, A.not_equal, 400.0, A.mult)
-    ts(EDG, EA, EB, A.add, 48.0, A.add)
-    ts(vw("kh", 0, 400), vw("r4"), TCB, A.is_equal, -512.0, A.mult)
-    ts(vw("kh", 400, 784), vw("r4", 0, C), TCB, A.is_equal, -512.0, A.mult)
-    ts(vw("e3"), vw("r4", 0, 48), TCB, A.is_equal, 64.0, A.mult)
-    act(vw("ns", 0, 2 * C, 2), Z)
-    act(vw("hr", 1, 2 * C, 2), Z)
-    act(vw("k32"), vw("zero", 0, 256), scale=1.0, bias=1.0)
+            qz("zq%d" % t, vw("lq%d" % t, lo, lo + 128), vw("ls%d" % t, lo, lo + 128), vw("zero", 0, 512))
+    lin("t15", T15, TC, -1.0, 15.0)
+    lin("pn", PN, PAR, -1.0, 65.0)
+    ts("na", NA, PAR, HC, A.not_equal)
+    lin("bs", BS, TC, -0.5, 7.25)
+    lin("bo", BO, TC, -1.0, 15.5)
+    lin("b1", B1, TC, -1.0 / 16, 192.0 - 17.0 / 32)
+    lin("b2", B2, TC, 1.0 / 16, -192.0 - 15.0 / 32)
+    lin("hn", HN, HC, -2048.0, 0.25)
+    lin("w16", W16, TC, 16.0)
+    lin("thc", TH, TC, -1.0, -0.5)
+    lin("kc", vw("kc"), vw("kc"), 1.0, TH)
+    ts("kh", vw("kh"), vw("r4"), TCB, A.is_equal, 1024.0, A.mult)
+    lin("kd", vw("kd"), vw("kh"), 1.0, -1.0)
+    lin("kd2", vw("kd2"), vw("kh"), 1.0, -2.0)
+    r16 = vw("r4", 0, 64)
+    for name, vo, vc in (("ta", 64.0, -2.0), ("tb", 2.0, -64.0)):
+        ts(name + "o", vw(name, 1, 128, 2), r16, TCB, A.is_equal, vo, A.mult)
+        ts(name + "c", vw(name, 0, 128, 2), r16, TCB, A.is_equal, vc, A.mult)
+    for e in range(2):
+        ts("tm%d" % e, vw("tm", e, 128, 2), r16, TCB, A.not_equal, -5.0, A.mult)
+    lin("tm", vw("tm"), vw("tm"), 1.0, 4.0)
+    act("thr", vw("thr"), vw("kk2"), F.Abs, 1.0, HN)
+    ts("ka", vw("ka"), vw("hi"), HC, A.is_equal, 1.0 / 16, A.mult)
+    lin("kb", vw("kb"), vw("ka"), -1.0)
+    fill("ka1", vw("ka", 31, 128, 32), 64.0, 4)
+    fill("kb1", vw("kb", 0, 128, 32), -64.0, 4)
+    scan("yd", vw("yf", 176, 352), vw("kd", 0, 176), vw("yf", 0, 176), A.add, A.min)
+    lin("ari", vw("ga"), vw("yf", 0, 176), 1.0 / 32, 192.0 - 0.49)
+    lin("arow", vw("arow", 16, 192), vw("ga"), 1.0, -192.0)
+    tt("rsf", vw("rsf", 0, 176), vw("arow", 16, 192), vw("arow", 15, 191), A.is_equal)
+    lin("rsb", vw("rsb"), vw("rsf", 1, 177), -8.0, 8.0)
+    ts("gi0", vw("gi", 0, 11), vw("yf", 191, 352, 16), T15, A.add)
+    ts("gi1", vw("gi", 12, 23), vw("gi", 0, 11), 31, A.bitwise_and)
+    cp("gl0", vw("gl", 0, 11), vw("gi", 12, 23))
+    ts("gl1", vw("gl", 12, 23), vw("gi", 12, 23), 48.0, A.mult, 1.0, A.add)
+    for e in range(2):
+        lin("pos%d" % e, vw("pos", e, C, 2), vw("posi"), 1.0 / 256)
+    ts("sf0", vw("sf", 0, 1), NA, 272.0, A.mult, W16, A.add)
+    ts("sf1", vw("sf", 1, 2), NA, -144.0, A.mult, W16, A.add)
+    ts("sl0", vw("sl", 0, 1), vw("sf", 0, 1), 15.0, A.add)
+    ts("sl1", vw("sl", 2, 3), vw("sf", 1, 2), 687.0, A.add, 799.0, A.min)
+    fill("vt0", vw("vt", 0, GF, 2), 1.0 / 256, GF // 2)
+    fill("vt1", vw("vt", 1, GF, 2), 194.0 / 256, GF // 2)
+    lin("vt2", vw("vt", 2, 4, 2), vw("vi", 0, 1), 1.0 / 256, -32.0 / 256)
+    lin("vt3", vw("vt", 4, 130, 2), vw("vi", 0, 63), 1.0 / 256, -31.0 / 256)
+    lin("vt4", vw("vt", 1, 128, 2), vw("vi"), 1.0 / 256, 195.0 / 256)
     for b in range(4):
-        act(vw("zz", ZW * b, ZW * b + 16), vw("zero", 0, 16))
-        act(vw("zz", ZW * b + 400, ZW * b + 416), vw("zero", 0, 16))
-    act(vw("k32", 0, 256, 32), vw("zero", 0, 8))
-    act(W16, TC, F.Copy, 16.0)
-    act(TH, TC, scale=0.5, bias=0.25)
-    act(HN, HC, F.Copy, -512.0)
-    act(vw("kd"), vw("kh", 0, C), scale=-1.0, bias=-0.5)
-    act(vw("b8", 0, 4), vw("k8"), scale=1.0, bias=TH)
-    act(vw("kb"), Z)
-    act(vw("b8", 4, 8), vw("b8", 0, 4), F.Copy, -1.0)
-    act(vw("kb", 0, C, 16), vw("zero", 0, 24), scale=1.0, bias=512.0)
-    for e in range(3):
-        act(vw("ta", 96 + 16 * e, 112 + 16 * e), vw("e3", 0, 16), scale=1.0, bias=-1.0 * (e == 1))
-        act(vw("tb", 16 * e, 16 + 16 * e), vw("e3", 0, 16), scale=-1.0, bias=1.0 * (e == 2))
-    act(vw("tm", 0, 48), vw("e3"), scale=1.0, bias=-64.0)
-    act(vw("tm", 96, 144), vw("e3"), scale=1.0, bias=-64.0)
-    need("v", "lu", 16)
-    qz(vw("uq"), vw("us"), vw("ub"))
-    run("v", [vw("uq2")], [vw("uq"), vw("upl")],
-        lambda: g.vector.tensor_copy(T.uq2[:, 0:128].bitcast(dt.uint32), T.uq[:, 0:128].bitcast(dt.uint32).indirect(T.upl[:, 0:8])))
-    run("v", [vw("us2")], [vw("us"), vw("upl")],
-        lambda: g.vector.tensor_copy(T.us2[:, 0:128], T.us[:, 0:128].indirect(T.upl[:, 0:8])))
-    act(vw("thr2", 128, 256), vw("kk2"), F.Abs, 0.5, HN)
-    act(vw("thr2", 0, 128), vw("thr2", 128, 256), F.Copy, -1.0)
-    need("v", "lx", 16)
-    qz(vw("aq0", 0, HALF), vw("as0", 0, HALF), vw("xb", 0, 4 * HALF))
-    need("v", "lx2", 16)
-    qz(vw("aq0", HALF, C), vw("as0", HALF, C), vw("xb", 4 * HALF, 4 * C))
-    ts(NEH, NA, W16, A.add, 15.0, A.add)
+        qz("eq%d" % b, vw("eq", 128 * b, 128 * b + 128), vw("es", 128 * b, 128 * b + 128), vw("eb", 3 - b, 515 - b))
+    qz("uq", vw("uq"), vw("us"), vw("ub"))
+    op("uq2", {"v": lambda: g.vector.tensor_copy(T.uq2[:, 0:128].bitcast(dt.uint32),
+                                                 T.uq[:, 0:128].bitcast(dt.uint32).indirect(T.upl[:, 0:8]))},
+       [vw("uq2")], [vw("uq"), vw("upl")])
+    mv("us2", vw("us2", 0, 128), ind(vw("us", 0, 128), vw("upl", 0, 8)))
+    qz("vq", vw("vq"), vw("vs"), vw("vb"))
+    for n, (a, e) in zip("ab", PIECES):
+        qz("xq" + n, vw("aq0", a, e), vw("as0", a, e), vw("xb", 4 * a, 4 * e))
 
     sides = [s for s in (0, 1) if (rank, s) in helpers]
-    sent = [0]
 
-    def send(t):
-        for kind, sem in (("q", "ha%d"), ("s", "hb%d")):
-            xs = []
-            for s in sides:
-                h = helpers[(rank, s)]
-                rid, pid = topo.addr(h, core)
-                es = topo.engines(core, h)
-                src, dst = T["m%s%d" % (kind, t)][:, TM * s:TM * s + TM], T["h%s%d" % (kind, t)][:]
-                if kind == "q":
-                    src, dst = src.bitcast(dt.uint8), dst.bitcast(dt.uint8)
-                xs.append(RemoteDMATransfer(dst_ids=[DstId(rid=rid, pnc=pid)], dma_engine_mask=_bits(es[NEAR * s:NEAR * s + NEAR]),
-                                            remote_sem=T.sem[sem % t], src=src, dst=dst))
-                sent[0] += NEAR
-            g.remote_dma_fused(xs, local_sem=T.sem.sent)
+    def send(t, kind, sem):
+        xs = []
+        for s in sides:
+            h = helpers[(rank, s)]
+            rid, pid = topo.addr(h, core)
+            es = topo.engines(core, h)
+            src, dst = T["m%s%d" % (kind, t)][:, TM * s:TM * s + TM], T["h%s%d" % (kind, t)][:]
+            if kind == "q":
+                src, dst = src.bitcast(dt.uint8), dst.bitcast(dt.uint8)
+            xs.append(RemoteDMATransfer(dst_ids=[DstId(rid=rid, pnc=pid)], dma_engine_mask=_bits(es[NEAR * s:NEAR * s + NEAR]),
+                                        remote_sem=T.sem[sem % t], src=src, dst=dst))
+        op("send" + kind, {"g": lambda: g.remote_dma_fused(xs, local_sem=T.sem.sent)}, [(None, [("sent%d" % t, 0, 1, 1)])],
+           [vw("m%s%d" % (kind, t))], "sent")
 
-    arrive = 2 * FAR * len(sides)
+    def sm(i):
+        return vw("sm", 24 * i, 24 * i + 24)
 
-    def sm(i, k=1):
-        return vw("sm", 24 * i, 24 * (i + k))
+    def sb(i, n):
+        return vw("sb", 32 * i, 32 * i + n)
 
-    def bank(b, n):
-        return vw("ps", 512 * b, 512 * b + n)
-
-    def plane(b, a, e):
-        return vw("zz", ZW * b + a, ZW * b + e)
-
-    def lay(b):
-        act(plane(b, 16, 400), bank(b + 1, C), F.Copy, 0.0625)
-
-    def again(b):
-        act(vw("pp", C * b, C * b + C), plane(b, 16, 400))
-
-    def leave(t):
-        mq, msc = vw("mq%d" % t), vw("ms%d" % t)
-        qz(mq, msc, vw("mt"))
-        order("g", [], [mq, msc])
-        send(t)
+    def bank(b, n, a=0):
+        return vw("ps", 512 * b + a, 512 * b + n)
 
     for t in range(ROUNDS):
-        aq, asc = vw("aq%d" % t), vw("as%d" % t)
-        mm(bank(0, C), vw("uq2"), vw("us2"), aq, asc)
-        if t == 0:
-            need("t", "lw", 32)
-        for b in range(4):
-            mm(bank(b + 1, C), vw("wq", 128 * b, 128 * b + 128), vw("wsc", 128 * b, 128 * b + 128), aq, asc)
-        if t > 0:
-            need("v", "lv", 16)
-            qz(vw("vq"), vw("vs"), vw("vb"))
-        S, Sr = vw("sg"), vw("sg", rev=True)
-        ts(S, bank(0, C), 0.0, A.is_ge, -0.5, A.add)
-        if t > 0:
-            lay(0)
-        act(vw("ns", 1, 2 * C, 2), S)
-        lay(t)
-        scan(vw("dr"), S, Z, A.add, A.add)
-        scan(vw("rr", rev=True), Sr, Z, A.add, A.add)
-        scan(vw("uv", 1, 385), vw("dr"), Z, A.min, A.min)
-        scan(vw("uv", 399, 783, rev=True), vw("rr", rev=True), Z, A.max, A.max)
-        for i in range(8):
-            ends = vw("uv", 16, 385, 16) if i < 4 else vw("uv", 399, 783, 16)
-            count(vw("n1", i, i + 1), vw("jk", 24 * i, 24 * i + 24), ends, vw("b8", i, i + 1))
-        lay(t + 1)
-        act(vw("off", 0, 4), vw("n1", 0, 4), scale=8.0, bias=191.0)
-        act(vw("off", 4, 8), vw("n1", 4, 8), scale=8.0, bias=192.0)
-        for b in range(t + 2, 4):
-            lay(b)
-        scan(vw("hr", 2, 2 * C + 2, 2), S, Z, A.add, A.max)
-        scan(vw("hb", 1, 785), vw("kh"), vw("uv", 0, 784), A.add, A.max)
-        scan(vw("yy", DL, DL + 2 * C, rev=True), vw("ns", rev=True), vw("hr", 0, 2 * C, rev=True), A.subtract, A.min)
-        act(vw("lim", 0, 1), vw("uv", 384, 385), F.Relu, 1.0, 32.0)
-        act(vw("lim", 1, 2), vw("uv", 399, 400), F.Relu, -1.0, 32.0)
-        act(vw("ee", 0, 24), vw("hb", 16, 400, 16), scale=-2.0, bias=416.0)
-        act(vw("ee", 24, 48), vw("hb", 416, 785, 16), scale=2.0, bias=480.0)
-        ts(vw("o16", 0, 16, 2), vw("n1"), 8.0, A.mult, 192.0, A.add)
-        ts(vw("o16", 1, 16, 2), vw("n1"), 8.0, A.mult, 192.0, A.add)
-        tt(vw("c2", 0, 128), ind(vw("hb", 16, 401), vw("o16", 0, 8)), vw("thr2", 0, 128), A.is_ge)
-        tt(vw("c2", 128, 256), ind(vw("hb", 400, 785), vw("o16", 8, 16)), vw("thr2", 128, 256), A.is_gt)
-        tr(vw("t2"), vw("c2"))
-        scan(vw("n2"), vw("k32"), vw("t2"), A.mult, A.add)
-        tt(vw("mi"), vw("n2", 31, 256, 32), vw("off"), A.add)
-        cp(vw("ml"), vw("mi"))
-        for b in range(4):
-            (cp if b < VM[t] else act)(vw("mt", b, 512, 4), ind(plane(b, 0, 416), vw("ml")))
-        if VM[t]:
-            leave(t)
-        after = vw("yy", DL + 2, DL + 2 + 2 * C, 2)
-        scan(vw("xx", 0, C), vw("kd"), after, A.add, A.min)
-        scan(vw("yy", 0, 2 * C, 2), vw("kd"), vw("yy", DL, DL + 2 * C, 2), A.add, A.min)
-        if t == 0:
-            scan(vw("yf", 176, 352), vw("kd", 0, 176), vw("yf", 0, 176), A.add, A.min)
-            ts(vw("arow"), vw("yf", 0, 176), 1.0 / 32, A.mult, -0.49, A.add)
-            ts(vw("gi", 0, 11), vw("yf", 191, 352, 16), 2.0, A.mult, T15, A.add)
-            act(vw("pos", 0, C, 2), vw("posi"), F.Copy, 1.0 / 256)
-            act(vw("pos", 1, C, 2), vw("posi"), F.Copy, 1.0 / 256)
-            act(vw("sf"), vw("c24", 0, 2), scale=256.0, bias=NEH)
-            act(vw("cl", 0, 24), vw("c24"), scale=8.0 / 256, bias=8.0 / 256)
-            act(vw("cl", 24, 48), vw("c24"), scale=8.0 / 256, bias=15.0 / 256)
-        scan(vw("xx", C, 2 * C), vw("kb"), after, A.add, A.min)
-        tt(sm(2), vw("xx", 15, C, 16), vw("yy", 30, 2 * C, 32), A.subtract)
-        tt(sm(0, 2), vw("xx", 15, 2 * C, 16), vw("yy", 30, 4 * C, 32), A.min)
-        ts(sm(3), sm(2), 96.0, A.mult, EDG, A.add)
-        ts(vw("li"), sm(0, 2), 2.0, A.mult, T15, A.add)
-        act(sm(6), sm(2), scale=177.0, bias=88.5)
-        ts(vw("cc", 0, 24), vw("hb", 16, 400, 16), 32.0, A.add, vw("lim", 0, 1), A.is_gt)
-        ts(vw("ri"), vw("li", 0, 24), 15, A.bitwise_and)
-        ts(vw("sh", 0, 48), vw("li"), 4, A.logical_shift_right)
-        tt(sm(4), sm(3), vw("ri"), A.add)
-        ts(sm(10), sm(2), 0.0, A.is_equal)
-        cp(vw("o1"), sm(4))
-        if not VM[t]:
-            leave(t)
-        if t == 0:
-            ts(vw("gi", 12, 23), vw("gi", 0, 11), 1, A.logical_shift_right, 31, A.bitwise_and)
-            ts(vw("sl"), vw("sf"), 799.0, A.min)
-            ts(vw("gl", 12, 23), vw("gi", 12, 23), 7.0, A.add)
-            cp(vw("gl", 0, 11), vw("gi", 12, 23))
-            iota(vw("xm", 0, 2 * C, 2), [[0, C]], 256)
-            for a in (0, 400):
-                sel(vw("k16", a, a + 400), [[0, 25], [1, 16]], 0, -256.0)
-        act(vw("xa"), ind(vw("ta"), vw("o1")))
-        act(vw("xc"), ind(vw("tb"), vw("o1")))
-        GL = vw("gl", 0, 11)
-        tt(vw("ea"), ind(vw("sh", 16, 49), vw("gl", 12, 23)), vw("arow"), A.is_equal)
-        ts(sm(5), vw("sh", 0, 24), -1.0, A.mult, 25.0, A.add)
-        tt(sm(8), sm(6), vw("c24"), A.add)
-        tt(sm(7), sm(5), vw("sh", 0, 24), A.mult)
-        scan(vw("ar"), vw("xa"), vw("pos"), A.add, A.min)
-        tt(sm(9), sm(7), sm(8), A.add)
-        tt(vw("pa", 1, 25), vw("ar", 15, C, 16), vw("cl", 0, 24), A.max)
-        ts(vw("cc", 24, 48), vw("hb", 416, 785, 16), vw("lim", 1, 2), A.add, 32.0, A.is_lt)
-        act(vw("ec", 0, 175), vw("ea", 1, 176), scale=-1.0, bias=1.0)
-        act(vw("ga"), ind(vw("pa", 0, 25), GL))
-        scan(vw("br", 1, 2 * C, 2, rev=True), vw("xc", rev=True), vw("pos", rev=True), A.add, A.max)
-        cp(vw("og"), sm(9))
-        tt(vw("pb", 0, 24), vw("br", 1, 2 * C, 32), vw("cl", 24, 48), A.min)
-        act(vw("gb"), ind(vw("pb", 0, 25), GL))
-        act(vw("xm", 1, 2 * C, 2), ind(vw("tm"), vw("o1")))
-        if t == 0:
-            need("a", "le", 64)
-            for b in range(4):
-                act(vw("eb", 512 * b + b, 512 * b + 512, 4), vw("idm"))
-        for b in range(4):
-            again(b)
-        scan(vw("grid", 0, 176), vw("ea"), vw("ga"), A.add, A.min)
-        tt(vw("ff"), vw("cc"), vw("ee"), A.mult)
-        scan(vw("grid", 176, 352, rev=True), vw("ec", rev=True), vw("gb", rev=True), A.mult, A.max)
-        tt(sm(12), vw("ff", 0, 24), vw("ff", 24, 48), A.add)
-        tt(vw("br", 0, 2 * C, 2), ind(vw("grid"), vw("og")), vw("ar"), A.max)
-        scan(vw("rb", 32, 800), vw("xm"), vw("br"), A.add, A.min)
-        tt(sm(13), sm(12), sm(10), A.mult)
-        if t == 0:
-            qz(vw("eq"), vw("es"), vw("eb"))
-        need("t", "arr%d" % t, arrive)
-        for b in range(4):
-            mm(bank(b + 1, 128), vw("eq", 128 * b, 128 * b + 128), vw("es", 128 * b, 128 * b + 128),
-               vw("lq%d" % t, 64, 192), vw("ls%d" % t, 64, 192))
-        for b in range(4):
-            act(plane(b, 416, ZW), bank(b + 1, 128))
-        tr(vw("tt", 0, C), vw("rb", 33, 800, 2))
-        tr(vw("tt", C, 800), vw("rb", 1, 832, 2))
-        scan(vw("ts"), vw("k16"), vw("tt"), A.add, A.max)
-        ts(vw("pt"), ind(vw("ts"), vw("sl")), 512.0, A.mult, PN, A.add)
-        tt(sm(15), vw("pt", 0, 24), sm(13), A.max)
-        cp(vw("ol"), sm(15))
-        aq, asc = "aq%d" % (t + 1), "as%d" % (t + 1)
-        for n, (a, e) in enumerate(((0, C),) if t < ROUNDS - 1 else ((0, HALF), (HALF, C))):
-            for b in range(4):
-                tt(vw("xt", 4 * a + b, 4 * e, 4), ind(plane(b, 0, ZW), vw("ol", a // 16, e // 16)), vw("pp", C * b + a, C * b + e), A.add)
-            qz(vw(aq, a, e), vw(asc, a, e), vw("xt", 4 * a, 4 * e))
-            if t == ROUNDS - 1:
-                mm(bank(5 * n, e - a), vw("vq"), vw("vs"), vw(aq, a, e), vw(asc, a, e))
-                order("y", [], [vw(aq, a, e), vw(asc, a, e)])
-                g.sync.dma_start(T.oc[:, 4 * a:4 * e], T[aq][:, a:e].bitcast(dt.uint8)).then_inc(T.sem.st, 16)
-                (cp if n else act)(vw("yb", a, e), bank(5 * n, e - a))
-                order("a", [], [vw("yb", a, e)])
-                g.scalar.dma_start(T.y[:, a:e], T.yb[:, a:e]).then_inc(T.sem.st, 16)
+        tag[0] = "%d." % t
 
+        def plane(b, a, e, t=t):
+            return vw("zz", ZW * (4 * t + b) + a, ZW * (4 * t + b) + e)
+
+        for n, (a, e) in enumerate(PIECES):
+            aq, asc = vw("aq%d" % t, a, e), vw("as%d" % t, a, e)
+            mm("ms%d" % n, bank(n, e - a), vw("uq2"), vw("us2"), aq, asc)
+            act("sg%d" % n, vw("sg", a, e), bank(n, e - a), F.Sign, 1.0, TINY)
+        for n, (a, e) in enumerate(PIECES):
+            aq, asc = vw("aq%d" % t, a, e), vw("as%d" % t, a, e)
+            for b in range(4):
+                k = (2 + 4 * n + b) % 8
+                mm("mp%d%d" % (n, b), bank(k, e - a), vw("wq", 128 * b, 128 * b + 128), vw("wsc", 128 * b, 128 * b + 128), aq, asc)
+                lin("lay%d%d" % (n, b), plane(b, P0 + a, P0 + e), bank(k, e - a), 0.0625)
+        for b in range(4):
+            dma("pp%d" % b, T.pp[:, C * b:C * b + C], plane(b, P0, P0 + C)[0], [vw("pp", C * b, C * b + C)],
+                [plane(b, P0, P0 + C)], "p%d" % b)
+        S = vw("sg")
+        scan("dl", vw("dv", 0, 192, rev=True), vw("zero", 0, 192), vw("sg", 0, 192, rev=True), A.add, A.subtract)
+        scan("dr", vw("dv", 193, 385), vw("sg", 192, C), vw("zero", 0, 192), A.add, A.add)
+        D, Dr = vw("dv", 0, 385), vw("dv", 0, 385, rev=True)
+        D0, DE = vw("dv", 0, 1), vw("dv", C, C + 1)
+        scan("L", vw("lr", 0, 385), D, D, A.min, A.min, 999.0)
+        scan("R", vw("rr", 0, 385, rev=True), Dr, Dr, A.min, A.min, 999.0)
+        scan("sd", vw("sd"), vw("kd2"), S, A.add, A.min)
+        scan("dd", vw("dd"), vw("kd"), vw("dv", 1, 385), A.add, A.min)
+        SR, RAW, HV, OPEN = vw("sd", 15, C, 16), vw("dd", 15, C, 16), vw("e1", 3, 96, 4), vw("e0", 2, 96, 4)
+        lin("s1", sm(0), SR, -0.25, BS)
+        lin("open", OPEN, SR, 0.5, BO)
+        lin("qb", sb(0, 24), vw("dv", 8, C, 16), 1.0 / 16, 192.0)
+        lin("q16", sm(1), sb(0, 24), -16.0, 3072.0)
+        tt("s2", sm(2), sm(0), sm(1), A.add)
+        tt("hr", sm(3), RAW, sm(2), A.add)
+        ts("o1", vw("o1"), sm(3), 2.0, A.mult, 64.0, A.add)
+        tt("hv", HV, RAW, sm(0), A.add)
+        lin("nd", vw("al", 1, 2), D0, -1.0)
+        lin("th0", vw("th", 0, 4), vw("kc", 0, 4), -1.0, vw("al", 1, 2))
+        lin("th1", vw("th", 4, 8), vw("kc", 4, 8), 1.0, DE)
+        for i in range(8):
+            ends = vw("lr", 16, 385, 16) if i < 4 else vw("rr", 0, C, 16)
+            count("n%d" % i, vw("n1", i, i + 1), vw("jk", 24 * i, 24 * i + 24), ends, 1.0 if i < 4 else -1.0, vw("th", i, i + 1))
+        lin("vl", vw("vl", 0, 24), HV, -1.0, D0)
+        lin("vr", vw("vr", 1, 25), HV, -1.0, DE)
+        for e in range(2):
+            ts("o16%d" % e, vw("o16", e, 16, 2), vw("n1"), 0.5, A.mult, 12.0, A.add)
+        lin("of0", vw("off", 0, 4), vw("n1", 0, 4, rev=True), 0.5, 12.25)
+        lin("of1", vw("off", 4, 8), vw("n1", 4, 8), 0.5, 11.25 - 1.0 / 16)
+        tt("c20", vw("c2", 0, 128), ind(vw("vl", 0, 25), vw("o16", 0, 8)), vw("thr", 0, 128), A.is_lt)
+        tt("c21", vw("c2", 128, 256), ind(vw("vr", 0, 25), vw("o16", 8, 16)), vw("thr", 128, 256), A.is_ge)
+        for i in range(2):
+            tr("t2%d" % i, vw("t2", 128 * i, 128 * i + 128), vw("c2", 128 * i, 128 * i + 128))
+        scan("n20", vw("n2", 0, 128), vw("ka", rev=True), vw("t2", 0, 128, rev=True), A.add, A.min)
+        scan("n21", vw("n2", 128, 256), vw("kb"), vw("t2", 128, 256), A.add, A.max)
+        tt("mi", vw("mi"), vw("n2", 31, 256, 32), vw("off"), A.add)
+        ts("ml", vw("ml"), vw("mi"), 16.0, A.mult)
+        for b in range(4):
+            mv("mt%d" % b, vw("mt", b, 512, 4), ind(plane(b, 64, DR), vw("ml")))
+        qz("mq", vw("mq%d" % t), vw("ms%d" % t), vw("mt"))
+        send(t, "q", "ha%d")
+        send(t, "s", "hb%d")
+        op("arr", {}, [vw("lq%d" % t, 64, 192), vw("ls%d" % t, 64, 192)], [(None, [("sent%d" % t, 0, 1, 1)])], "arr%d" % t)
+        mv("xa", vw("xa"), ind(vw("ta"), vw("o1")))
+        mv("xc", vw("xc"), ind(vw("tb"), vw("o1")))
+        mv("xm", vw("br", 5, 5 + 3 * C, 3), ind(vw("tm"), vw("o1")))
+        scan("ar", vw("ar", 4, 4 + 3 * C, 3), vw("xa"), vw("pos"), A.add, A.min, -2.0)
+        scan("br", vw("br", 1, 1 + 3 * C, 3, rev=True), vw("xc", rev=True), vw("pos", rev=True), A.add, A.max, 2.0)
+        BASE = vw("e1", 2, 100, 4)
+        tt("base", BASE, vw("lr", 0, 385, 16), vw("rr", 0, 385, 16), A.max)
+        lin("q1", sb(1, 25), vw("dv", 0, 385, 16), 1.0 / 16, B1)
+        lin("q2", sb(2, 25), BASE, -1.0 / 16, B2)
+        tt("cc", sb(3, 25), sb(1, 25), sb(2, 25), A.add)
+        tt("ea", vw("ea"), ind(sb(3, 25), vw("gl", 0, 11)), vw("arow", 16, 192), A.is_equal)
+        lin("ec", vw("ec"), vw("ea"), -4.0, 4.0)
+        tt("ga", vw("ga"), ind(vw("ar", 0, 1156), vw("gl", 12, 23)), vw("ea"), A.mult)
+        tt("gb", vw("gb"), ind(vw("br"), vw("gl", 12, 23)), vw("ec"), A.max)
+        scan("gf", vw("vt", GF, GF + 176), vw("rsf", 0, 176), vw("ga"), A.mult, A.max)
+        scan("gr", vw("vt", GF + 176, GF + 352, rev=True), vw("rsb", rev=True), vw("gb", rev=True), A.add, A.min)
+        lin("b0", vw("e1", 0, 96, 4), vw("e1", 6, 100, 4), 1.0)
+        lin("bn", vw("e1", 1, 96, 4), vw("e1", 2, 96, 4), -1.0)
+        scan("de", vw("e2"), vw("e0"), vw("e1", 0, 96), A.mult, A.add)
+        DL = vw("e2", 3, 96, 4)
+        lin("ab", sb(4, 24), DL, 1.0 / 16, 192.0 - 31.0 / 64)
+        act("sq", vw("f0", 2, 96, 4), sb(4, 24), F.Square, 1.0, SQ)
+        lin("rp", vw("f1", 2, 96, 4), DL, -1e5, -2.5e4)
+        lin("ow", vw("f0", 1, 96, 4), OPEN, 177.0, GF + 156.25)
+        lin("al", vw("al", 0, 1), D0, -1.0, DE)
+        act("es", sm(4), OPEN, F.Identity, vw("al", 0, 1), D0)
+        tt("vi", sm(5), sm(4), HV, A.subtract)
+        lin("v2", vw("f1", 3, 96, 4), sm(5), 2.0)
+        scan("ogs", vw("f2"), vw("f0"), vw("f1"), A.subtract, A.max)
+        cp("og", vw("og"), vw("f2", 3, 96, 4))
+        for n, (a, e) in enumerate(((0, 288), (288, C))):
+            mv("lk%d" % n, vw("br", 3 + 3 * a, 3 + 3 * e, 3), ind(vw("vt"), vw("og", a // 16, e // 16)))
+            scan("rb%d" % n, vw("rb", 48 + 3 * a, 48 + 3 * e), vw("ar", 3 * a, 3 * e), vw("br", 3 + 3 * a, 3 + 3 * e), A.max, A.min)
+        tr("t1a", vw("tt", 0, 256), vw("rb", 50, 816, 3))
+        tr("t2a", vw("tt", 256, 544), vw("rb", 2, 864, 3))
+        scan("tsa", vw("ts", 0, 544), vw("k16", 0, 544), vw("tt", 0, 544), A.add, A.max)
+        ts("ola", vw("ol", 0, 16), ind(vw("ts", 0, 544), vw("sl", 0, 1)), 512.0, A.mult, PN, A.add)
+        tr("t2b", vw("tt", 544, 672), vw("rb", 866, 1248, 3))
+        tr("t1b", vw("tt", 672, 800), vw("rb", 818, 1200, 3))
+        scan("tsb", vw("ts", 544, 800), vw("k16", 544, 800), vw("tt", 544, 800), A.add, A.max)
+        ts("olb", vw("ol", 16, 32), ind(vw("ts"), vw("sl", 2, 3)), 512.0, A.mult, PN, A.add)
+        for b in range(4):
+            mm("mu%d" % b, bank(2 + b, 128), vw("eq", 128 * b, 128 * b + 128), vw("es", 128 * b, 128 * b + 128),
+               vw("lq%d" % t, 64, 192), vw("ls%d" % t, 64, 192))
+            mv("ul%d" % b, plane(b, 1, 65), bank(2 + b, 64))
+            mv("ur%d" % b, plane(b, DR, DR + TM), bank(2 + b, 128, 64))
+        aq, asc = "aq%d" % (t + 1), "as%d" % (t + 1)
+        for n, (a, e) in enumerate(PIECES):
+            for b in range(4):
+                tt("x%d%d" % (n, b), vw("xt", 4 * a + b, 4 * e, 4), ind(plane(b, 0, DR + TM), vw("ol", a // 16, e // 16)),
+                   vw("pp", C * b + a, C * b + e), A.add)
+            qz("aq%d" % n, vw(aq, a, e), vw(asc, a, e), vw("xt", 4 * a, 4 * e))
+            if t == ROUNDS - 1:
+                mm("my%d" % n, bank(n, e - a), vw("vq"), vw("vs"), vw(aq, a, e), vw(asc, a, e))
+                dma("oc%d" % n, T.oc[:, 4 * a:4 * e], T[aq][:, a:e].bitcast(dt.uint8), [], [vw(aq, a, e)], "st")
+                mv("yb%d" % n, vw("yb", a, e), bank(n, e - a))
+                dma("y%d" % n, T.y[:, a:e], T.yb[:, a:e], [], [vw("yb", a, e)], "st")
     for k in range(4):
-        g.sync.dma_start(T.osc[4 * k:4 * k + 4, :], T[asc][32 * k:32 * k + 4, :]).then_inc(T.sem.st, 16)
-    g.wait_ge(T.sem.sent, sent[0])
+        dma("osc%d" % k, T.osc[4 * k:4 * k + 4, :], T[asc][32 * k:32 * k + 4, :], [], [vw(asc)], "st")
+    return ops, len(sides)
+
+
+def rank_program(g, core, T, topo):
+    rank = T.rank_of(core)
+    helpers = _helpers(T, topo)
+    if rank is None:
+        for (r, side), h in helpers.items():
+            if h == core:
+                _helper_program(g, core, T, topo, r, side)
+        return
+    ops, sides = _calls(g, core, T, topo, rank, helpers)
+    byname = {o[0]: o for o in ops}
+    plan = [(byname[w[:-2]], w[-1] if w[-1] != "-" else None) for w in PLAN.split() if w[:-2] in byname]
+    assert len(plan) == len(ops)
+    Q = {"v": g.vector, "a": g.scalar, "t": g.tensor, "g": g, "y": g.sync}
+    cnt, seen, hist = {}, {}, []
+
+    def need(q, key, val):
+        if seen.get((q, key), 0) < val:
+            seen[(q, key)] = val
+            Q[q].wait_ge(T.sem[key], val)
+
+    for (name, fns, outs, ins, sem), q in plan:
+        if q is None:
+            key, cnt[sem] = sem, 2 * FAR * sides
+        else:
+            want = {}
+            for cols, wr in ((outs, True), (ins, False)):
+                for c in cols:
+                    for (d, k, n, w) in hist:
+                        if _meet(c, d) and not (k == "nt" and q == "t") and k != "sent":
+                            if w or wr or (c[0] == "ps" and k != "n" + q):
+                                want[k] = max(want.get(k, 0), n)
+            for k in want:
+                need(q, k, want[k])
+            key = sem or "n" + q
+            step = NEAR * sides if sem == "sent" else 16 if sem else 1
+            cnt[key] = cnt.get(key, 0) + step
+            call = fns[q]()
+            if sem != "sent":
+                call.then_inc(T.sem[key], step)
+        for cols, wr in ((outs, True), (ins, False)):
+            for c in cols:
+                hist.append((c, key, cnt[key], wr))
+    g.wait_ge(T.sem.sent, cnt["sent"])
     for k in cnt:
-        need("y", k, cnt[k])
-    g.sync.wait_ge(T.sem.st, 16 * 8)
+        if k != "sent":
+            need("y", k, cnt[k])

@@ -1,52 +1,33 @@
+import math
 from concourse.bass import DstId, RemoteDMATransfer
 from concourse.mybir import dt, AluOpType as A, ActivationFunctionType as F
 
 C, TM, ROUNDS = 384, 64, 2
 ZW = 528
-P0, DR = 68, 454
+P0, DR = 68, 456
 GF = 784
+TW = 416
+BR = 1200
 NEAR, FAR = 8, 8
 HALF = 256
 PIECES = ((0, HALF), (HALF, C))
 X4, U8, BF, F32, I32, U16 = "float8_e4m3fn_x4", "uint8", "bfloat16", "float32", "int32", "uint16"
-
-
-def _sb(n, d):
-    return ("sbuf", [128, n], d)
-
-
-SCRATCH = {
-    "xb": _sb(4 * C, BF), "ub": _sb(512, BF), "vb": _sb(512, BF),
-    "aq0": _sb(C, X4), "as0": _sb(C, U8), "aq1": _sb(C, X4), "as1": _sb(C, U8), "aq2": _sb(C, X4), "as2": _sb(C, U8),
-    "uq": _sb(128, X4), "us": _sb(128, U8), "uq2": _sb(128, X4), "us2": _sb(128, U8),
-    "vq": _sb(128, X4), "vs": _sb(128, U8), "wq": _sb(512, X4), "wsc": _sb(512, U8),
-    "eb": _sb(528, BF), "eq": _sb(512, X4), "es": _sb(512, U8),
-    "zz": _sb(ROUNDS * 4 * ZW, BF), "xt": _sb(4 * C, BF), "mt": _sb(512, BF), "yb": _sb(C, F32), "pp": _sb(4 * C, BF),
-    "mq0": _sb(128, X4), "ms0": _sb(128, U8), "mq1": _sb(128, X4), "ms1": _sb(128, U8),
-    "hq0": _sb(64, X4), "hs0": _sb(64, U8), "hq1": _sb(64, X4), "hs1": _sb(64, U8),
-    "lq0": _sb(256, X4), "ls0": _sb(256, U8), "lq1": _sb(256, X4), "ls1": _sb(256, U8),
-    "ps": ("psum", [128, 512 * 8], F32),
-    "zero": _sb(800, BF), "ci": _sb(16, I32), "cf": _sb(24, F32), "cb": _sb(2, BF), "r4": _sb(C, BF),
-    "kh": _sb(C, BF), "kd": _sb(C, BF), "kd2": _sb(C, BF), "k16": _sb(800, BF), "hi": _sb(128, BF),
-    "ka": _sb(128, BF), "kb": _sb(128, BF), "kc": _sb(8, F32), "kk2": _sb(256, F32), "thr": _sb(256, BF),
-    "upi": _sb(8, I32), "upl": _sb(8, U16), "yf": _sb(352, F32), "arow": _sb(192, BF),
-    "gi": _sb(24, I32), "gl": _sb(24, U16), "posi": _sb(192, BF), "pos": _sb(C, BF),
-    "ta": _sb(128, BF), "tb": _sb(128, BF), "tm": _sb(128, BF), "rsf": _sb(192, BF), "rsb": _sb(176, BF),
-    "sf": _sb(4, F32), "sl": _sb(4, U16), "vi": _sb(64, BF),
-    "sg": _sb(C, BF), "dv": _sb(400, BF), "lr": _sb(400, BF), "rr": _sb(400, BF), "sd": _sb(C, BF), "dd": _sb(C, BF),
-    "th": _sb(8, F32), "jk": _sb(192, BF), "n1": _sb(8, F32), "o16": _sb(16, U16), "off": _sb(8, F32),
-    "vl": _sb(32, F32), "vr": _sb(32, F32), "c2": _sb(256, BF), "t2": _sb(256, BF), "n2": _sb(256, BF),
-    "mi": _sb(8, F32), "ml": _sb(8, U16), "sm": _sb(24 * 8, F32), "sb": _sb(32 * 5, BF), "al": _sb(2, F32),
-    "e0": _sb(96, F32), "e1": _sb(104, F32), "e2": _sb(96, F32), "f0": _sb(96, F32), "f1": _sb(96, F32), "f2": _sb(96, F32),
-    "o1": _sb(24, U16), "og": _sb(24, U16), "ol": _sb(32, U16),
-    "xa": _sb(C, BF), "xc": _sb(C, BF), "ar": _sb(1168, BF), "br": _sb(1168, BF),
-    "ea": _sb(176, BF), "ec": _sb(176, BF), "ga": _sb(176, BF), "gb": _sb(176, BF), "vt": _sb(GF + 352, BF),
-    "rb": _sb(1248, BF), "tt": _sb(800, BF), "ts": _sb(800, BF),
-}
-DMAS = ["lxa", "lxb", "lu", "lw", "ls", "lv", "z0", "z1", "z2", "z3", "z4", "p0", "p1", "p2", "p3"]
-SEMAPHORES = ["nv", "na", "nt", "ng", "st", "sent", "ha0", "hb0", "ha1", "hb1", "arr0", "arr1"] + DMAS
+SCRATCH = {"ps": ("psum", [128, 512 * 8], F32)}
+for _d, _s in ((X4, "aq0 384 aq1 384 aq2 384 uq 128 uq2 128 vq 128 wq 512 eq 512 mq0 128 mq1 128 hq0 64 hq1 64 lq0 256 lq1 256"),
+               (U8, "as0 384 as1 384 as2 384 us 128 us2 128 vs 128 wsc 512 es 512 ms0 128 ms1 128 hs0 64 hs1 64 ls0 256 ls1 256"),
+               (BF, "xb 1536 ub 512 vb 512 eb 528 zz 4224 xt 1536 mt 512 pp 1536 da 512 db 512 zero 528 cb 2 r4 416 kh 416 kd 384 "
+                    "k16 544 ta 832 tb 832 tm 832 kk 288 cap 176 cpt 32 arow 352 pos 384 sg 400 ns 208 ev 400 lr 400 rr 400 sd 384 "
+                    "dd 416 jk 200 c2 160 t2 288 n2 288 sb 128 xa 384 xc 384 ab 2368 ga 352 vt 1136 rb 1248 tt 800 ts 800"),
+               (F32, "yb 384 cf 24 c9 2 kc 8 k2 64 thr 128 sf 4 th 8 n1 8 off 8 mk 16 sm 24 al 2 cc 32 key 56 "
+                     "e0 96 e1 96 e2 96 f0 96 f1 96 f2 96 bs 32 yf 352"),
+               (I32, "ci 16 upi 8 gi 24"), (U16, "upl 8 gl 24 sl 8 o16 8 ml 32 o1 24 og 24 ol 32")):
+    _w = _s.split()
+    for _i in range(0, len(_w), 2):
+        SCRATCH[_w[_i]] = ("sbuf", [128, int(_w[_i + 1])], _d)
+DMAS = ["lxa", "lxb", "lu", "lw", "ls", "lv", "p0", "p1", "p2", "p3"]
+SEMAPHORES = ["nv", "na", "nt", "ng", "st", "sent", "ha0", "ha1", "arr0", "arr1"] + DMAS
 PLAN = """
-zero:v lxa:y ci:g lu:y lxb:y r4:g lw:y ls:y c1:v c2:v c3:v zz67:a z3:y zz65:v z0:y zz64:a f4:v z2:y f9:a z4:y cb:v f8:a z1:y f1:v f13:a cf:v upi:g hn:v pn:a zz452:a hi:g kh:v f17:v tm1:v thc:v kd2:a kk0:g na:v f16:v f14:v ka:v upl:v zz66:v t15:a yf5:g tm0:v f10:a kd:v kb:a yf3:g bo:a xqa:v b1:a yf8:g w16:a yf11:g uq:v kc1:g f12:v yf6:g uq2:v us2:a kk1:g zq0:v ka1:a b2:a zz453:a kc0:g xqb:v 0.ms0:t yf9:g thr:a sf1:v f11:v yf7:g tao:v 0.ms1:t tm:v tac:v f5:g f0:v 0.sg0:a tbo:v yf1:g tbc:v f15:v yf12:g bs:v 0.sg1:a yf0:g kc:a 0.dl:v zz0:a 0.mp00:t kb1:a 0.dr:v yf10:g 0.sd:v 0.nd:a nb:g 0.th1:a 0.mp11:t 0.R:v 0.qb:a yf2:g 0.lay00:a 0.mp02:t 0.L:v yf4:g posi:g 0.s1:v 0.n5:a 0.th0:v 0.n7:a 0.mp10:t 0.q16:v 0.n6:a 0.dd:v 0.n4:a 0.mp12:t 0.n3:a 0.base:v 0.n0:a 0.s2:v 0.mp03:t f2:g 0.n2:a 0.al:v 0.hv:v 0.n1:a eb:g yd:v 0.lay02:a 0.mp13:t 0.o160:v 0.o161:v 0.vl:a 0.bn:v 0.mp01:t 0.q2:a 0.vr:v ari:a 0.hr:v 0.c20:v 0.b0:a 0.of0:a 0.open:a 0.c21:v 0.q1:a 0.lay10:a 0.ow:a 0.of1:v 0.lay12:a 0.t20:v 0.t21:v 0.lay01:a vi:g gi0:v 0.n20:v 0.pp2:y 0.n21:v arow:v 0.lay13:a f7:g gi1:v 0.es:a 0.mi:v 0.lay11:a 0.o1:v pos0:v 0.lay03:a 0.ml:v 0.de:v 0.pp1:y 0.cc:v lv:y 0.mt2:a gl1:v 0.vi:v gl0:v 0.pp3:y pos1:v 0.pp0:y 0.mt3:a 0.ab:v f6:g 0.mt1:v 0.mt0:a 0.ea:v 0.xa:a 0.mq:v rsf:v 0.sendq:g 0.xc:v 0.rp:a 0.v2:a 0.xm:a 0.ec:v 0.ar:v rsb:a 0.sends:g 0.br:v 0.sq:a vt0:a 0.ga:v 0.arr:- vt1:a 0.gb:v 0.ogs:v vt2:a 0.gf:v 0.gr:v vt4:a vt3:a 0.og:v eq3:v 0.lk0:a sf0:v eq0:v eq1:v sl0:v eq2:v 0.lk1:a sl1:v 0.rb0:v f3:a 0.rb1:v 0.t2a:v 0.t1a:v 0.mu1:t 0.t2b:v 0.t1b:v 0.mu3:t 0.tsa:v 0.ul1:a 0.mu0:t 0.tsb:v 0.mu2:t 0.ur1:a 0.ola:v 0.ul0:a 0.ul3:a 0.olb:v 0.x01:v 0.ur0:a 0.ur3:a 0.ul2:a 0.ur2:a 0.x11:v 0.x03:v 0.x00:v 0.x02:v 0.x13:v 0.aq0:v 0.x12:v 1.ms0:t 0.x10:v 1.mp00:t 1.sg0:a 0.aq1:v vq:v 1.ms1:t 1.lay00:a 1.dl:v 1.mp11:t 1.sg1:a 1.nd:v 1.mp02:t 1.th0:a 1.dr:v 1.mp10:t 1.sd:v 1.th1:a 1.mp01:t 1.L:v 1.q1:a 1.al:a 1.open:a 1.R:v 1.s1:a 1.qb:a 1.mp13:t 1.n3:a 1.dd:v 1.n2:a 1.mp03:t 1.n1:a zq1:v 1.n6:a 1.n5:a 1.q16:v 1.n4:a 1.hv:v 1.mp12:t 1.n7:a 1.base:v 1.lay11:v 1.n0:a 1.es:a 1.vl:v 1.vr:a 1.of1:a 1.o160:v 1.q2:a 1.o161:v 1.bn:a 1.vi:v 1.lay01:a 1.b0:v 1.c20:v 1.lay12:a 1.c21:v 1.of0:a 1.pp1:y 1.ow:a 1.lay02:a 1.t20:v 1.de:v 1.t21:v 1.lay10:a 1.n20:v 1.s2:v 1.ab:a 1.pp2:y 1.lay03:a 1.n21:v 1.hr:v 1.mi:v 1.lay13:a 1.rp:v 1.sq:a 1.ml:v 1.v2:a 1.o1:v 1.pp3:y 1.cc:v 1.pp0:y 1.mt0:a 1.mt2:v 1.xa:v 1.mt3:a 1.mt1:a 1.xc:a 1.mq:v 1.ea:v 1.sendq:g 1.ar:v 1.xm:a 1.br:v 1.sends:g 1.ogs:v 1.ec:v 1.ga:v 1.arr:- 1.gb:v 1.og:v 1.gf:v 1.gr:v 1.lk1:a 1.lk0:v 1.rb1:v 1.rb0:v 1.t1a:v 1.t2a:v 1.t2b:v 1.mu0:t 1.t1b:v 1.tsa:v 1.mu1:t 1.ul0:a 1.mu2:t 1.tsb:v 1.ola:v 1.mu3:t 1.ur0:a 1.olb:v 1.ul2:a 1.ul1:a 1.x00:v 1.ul3:a 1.ur2:a 1.ur1:a 1.ur3:a 1.x02:v 1.x03:v 1.x01:v 1.x10:v 1.aq0:v 1.x11:v 1.my0:t 1.oc0:y 1.x12:v 1.x13:v 1.yb0:a 1.aq1:v 1.y0:y 1.osc0:a 1.my1:t 1.osc1:y 1.osc3:a 1.oc1:a 1.osc2:a 1.yb1:v 1.y1:a
+lu:a zero:v f30:a ci:g c1:v f18:a c3:v f26:v c2:v f20:a upi:g f2:v zz455:a f13:v cf:v cb:v lxa:y r4:g yf3:g mk:g f25:v t2c:a f14:v yf10:g zq0:v kc0:g upl:v yf11:g f4:a uq:v f21:a b1a:a kh:v lxb:y uq2:v xqa:v mk0:v xqb:v ls:y coa:a c0:a b2:a a0:a k20:g zz64:a zz0:g yf2:g lw:y us2:a 0.ms0:t a1:a na:v kd:v yf5:g w16:a f24:g yf4:g c91:a kc:a c90:v co:a zz65:g yf9:g yf8:g sn1:v ta0:a 0.ms1:t yf0:g 0.ns:a 0.sg1:a ta1:v 0.dl:v mk1:v zz67:v yf6:g 0.sg0:a k2:v 0.L0:v yf12:g sf2:a 0.nd:a f22:a 0.dr:v ho:a c1c:a yf1:g 0.mp11:t f15:v zz453:a yf7:g zz66:v 0.mp00:t f23:g 0.mp01:t 0.th1:a 0.tr0:a 0.tr1:a zz452:g 0.th0:v 0.L1:v 0.n3:a sn0:v f19:g 0.R0:v 0.n1:a 0.n0:a 0.n2:a 0.n5:a 0.n6:a 0.mp13:t tb1:v f8:g sl2:v 0.dd:v eb:g sl3:v yd:v 0.mp02:t 0.n7:a 0.n4:a 0.o16:v 0.of0:v 0.base:v 0.of1:v 0.lay00:a 0.mp10:t 0.cm:v 0.mp12:t 0.o1:v 0.j1:v 0.j0:v pos:g 0.mp03:t 0.t21:v 0.t20:v 0.lay10:a gi0:v 0.lay13:v 0.lay02:a 0.nn:v cpt:g 0.sd:v lv:y 0.ml0:v 0.lay12:a nb:g 0.ml1:v 0.lay03:v 0.mt0:v 0.lay01:a 0.mt3:v f0:v gi1:v 0.lay11:a 0.xa:a 0.mt2:a 0.mt1:a b1:v 0.q2:a tb0:a 0.mq:v bo:v 0.bn:v 0.q1:v 0.b0:a f7:g 0.hv:v f9:v 0.ar:v ari:a 0.pp2:y f1:v sf0:v 0.bp:a 0.sendq:g 0.sends:g f29:v vt0:g 0.open:a arp:v 0.pp3:y eq3:v vt1:g 0.xc:a 0.de:v tm0:v 0.cc:v 0.al:a f12:a sf1:a 0.ab:a f10:a arn:v 0.br:v 0.arr:- 0.kf:v gl0:v gl1:v 0.kb:v 0.es:a f11:a 0.v2:v 0.sq:a f5:g 0.pp0:y 0.rp:v 0.ow:v 0.ga:v 0.ogs:v tm1:a sl1:v cap:a 0.gf:v 0.xm:a 0.gr:v 0.og:v 0.lk0:a eq2:v zq1:v 0.lk1:a 0.lk2:a f6:v sl0:v eq1:v f17:a f16:a f28:a f3:a pn:a eq0:v 0.rb0:v 0.lb1:a 0.mu1:t 0.rb1:v 0.mu3:t 0.rb2:v 0.mu0:t 0.lb3:a 0.t1a:v 0.t2a:v 0.mu2:t 0.t1b:v 0.pp1:y 0.t2b:v 0.tsa:v f27:a 0.ul1:a 0.ur1:a 0.ul3:a 0.tsb:v 0.ur3:a 0.ul0:a 0.ur0:a 0.ur2:a 0.ola:v 0.ul2:a 0.olb:v 0.x01:v 0.x03:v 0.xg3:a 0.x00:v 0.x02:v 0.xg1:a 0.xs:v 0.aq0:v 1.ms0:t 1.ns:a 1.sg0:a 0.x12:v 0.x10:v 0.aq1:v vq:v 1.mp03:t 1.dl:v 1.lay03:v 1.tr0:v 1.L0:v 1.ms1:t 1.sg1:a 1.dr:v 1.mp01:t 1.nd:a 1.lay01:a 1.sd:v 1.mp11:t 1.L1:v 1.R0:v 1.mp12:t 1.dd:v 1.q1:v 1.mp13:t 1.mp00:t 1.lay11:v 1.th0:a 1.tr1:a 1.base:v 1.o1:v 1.th1:a 1.lay00:v 1.hv:v 1.bp:v 1.bn:v 1.mp10:t 1.n1:a 1.n2:a 1.n3:a 1.n5:a 1.n7:a 1.n0:a 1.of0:v 1.n4:a 1.n6:a 1.o16:v 1.q2:a 1.lay10:v 1.of1:v 1.cm:v 1.open:v 1.j1:v 1.j0:v 1.pp0:y 1.xa:a 1.b0:a 1.xc:a 1.t20:v 1.t21:v 1.mp02:t 1.lay13:v 1.de:v 1.nn:v 1.ar:v 1.ml0:v 1.ml1:v 1.cc:v 1.br:v 1.mt1:v 1.lay12:a 1.lay02:a 1.mt2:v 1.mt3:a 1.mt0:a 1.ab:a 1.kf:v 1.ow:a 1.pp2:y 1.al:a 1.kb:v 1.lb3:a 1.es:a 1.mq:v 1.lb1:a 1.sendq:g 1.sends:g 1.ga:v 1.sq:a 1.arr:- 1.rp:a 1.xm:a 1.v2:v 1.ogs:v 1.gr:v 1.gf:v 1.og:v 1.lk1:a 1.lk2:a 1.lk0:v 1.rb1:v 1.rb0:v 1.mu0:t 1.pp3:y 1.rb2:v 1.ur0:a 1.t1a:v 1.mu2:t 1.ul0:a 1.ul2:a 1.t2a:v 1.mu3:t 1.t1b:v 1.ur2:a 1.t2b:v 1.tsa:v 1.mu1:t 1.tsb:v 1.ola:v 1.ur3:a 1.ul3:a 1.ur1:a 1.olb:v 1.x00:v 1.pp1:y 1.xg3:a 1.x02:v 1.ul1:a 1.x03:v 1.x01:v 1.xg1:a 1.xs:v 1.aq0:v 1.oc0:a 1.x10:v 1.x12:v 1.aq1:v 1.my0:t 1.yb0:a 1.my1:t 1.oc1:y 1.osc3:y 1.osc1:a 1.y0:a 1.yb1:v 1.osc2:y 1.y1:a 1.osc0:y
 """
 
 
@@ -61,7 +42,7 @@ def _helpers(T, topo):
     out = {}
     for r, c in enumerate(T.cores):
         used = []
-        for side, n in ((0, r - 1), (1, r + 1)):
+        for side, n in ((0, r - 1), (1, r + 1), (2, r - 1), (3, r + 1)):
             if 0 <= n < len(T.cores):
                 ok = [h for h in topo.cores_of(c) if T.rank_of(h) is None and h not in used and topo.may_write(h, T.cores[n])]
                 ok.sort(key=lambda h: topo.die(h) != topo.die(c))
@@ -71,27 +52,29 @@ def _helpers(T, topo):
 
 
 def _helper_program(g, core, T, topo, rank, side):
-    dst = T.cores[rank - 1 if side == 0 else rank + 1]
+    dst = T.cores[rank - 1 + 2 * (side % 2)]
     rid, pid = topo.addr(dst, core)
     m = _bits(topo.engines(core, dst)[:FAR])
-    lo = 128 - TM * side
+    lo = 128 - TM * (side % 2)
     for t in range(ROUNDS):
         g.wait_ge(T.sem["ha%d" % t], NEAR)
-        g.remote_dma(T["lq%d" % t][:, lo:lo + TM].bitcast(dt.uint8), T["hq%d" % t][:].bitcast(dt.uint8),
-                     T.sem["arr%d" % t], T.sem.sent, pid, rid, m)
-        g.wait_ge(T.sem["hb%d" % t], NEAR)
-        g.remote_dma(T["ls%d" % t][:, lo:lo + TM], T["hs%d" % t][:], T.sem["arr%d" % t], T.sem.sent, pid, rid, m)
-    g.wait_ge(T.sem.sent, 2 * ROUNDS * FAR)
+        if side < 2:
+            g.remote_dma(T["lq%d" % t][:, lo:lo + TM].bitcast(dt.uint8), T["hq%d" % t][:].bitcast(dt.uint8),
+                         T.sem["arr%d" % t], T.sem.sent, pid, rid, m)
+        else:
+            g.remote_dma(T["ls%d" % t][:, lo:lo + TM], T["hs%d" % t][:], T.sem["arr%d" % t], T.sem.sent, pid, rid, m)
+    g.wait_ge(T.sem.sent, ROUNDS * FAR)
 
 
 def _meet(u, v):
-    return u[0] == v[0] and u[1] < v[2] and v[1] < u[2] and not (u[3] == v[3] and (u[1] - v[1]) % u[3])
+    return u[0] == v[0] and u[1] < v[2] and v[1] < u[2] and not (u[1] - v[1]) % math.gcd(u[3], v[3])
 
 
 def _calls(g, core, T, topo, rank, helpers):
     N = len(T.cores)
     ops = []
     tag = [""]
+    V, S = g.vector, g.scalar
 
     def vw(name, a=0, b=None, s=1, rev=False):
         t = T[name]
@@ -118,49 +101,45 @@ def _calls(g, core, T, topo, rank, helpers):
 
     def ts(n, o, i, s1, op0, s2=None, op1=None):
         if op1 is None:
-            op(n, {"v": lambda: g.vector.tensor_scalar(o[0], i[0], ap(s1), None, op0)}, [o], [i, s1])
+            op(n, {"v": lambda: V.tensor_scalar(o[0], i[0], ap(s1), None, op0)}, [o], [i, s1])
         else:
-            op(n, {"v": lambda: g.vector.tensor_scalar(o[0], i[0], ap(s1), ap(s2), op0, op1)}, [o], [i, s1, s2])
+            op(n, {"v": lambda: V.tensor_scalar(o[0], i[0], ap(s1), ap(s2), op0, op1)}, [o], [i, s1, s2])
 
     def tt(n, o, a, b, f):
-        op(n, {"v": lambda: g.vector.tensor_tensor(o[0], a[0], b[0], f)}, [o], [a, b])
+        op(n, {"v": lambda: V.tensor_tensor(o[0], a[0], b[0], f)}, [o], [a, b])
 
     def cp(n, o, i):
-        op(n, {"v": lambda: g.vector.tensor_copy(o[0], i[0])}, [o], [i])
+        op(n, {"v": lambda: V.tensor_copy(o[0], i[0])}, [o], [i])
 
     def mv(n, o, i):
-        op(n, {"a": lambda: g.scalar.activation(o[0], i[0], F.Copy), "v": lambda: g.vector.tensor_copy(o[0], i[0])}, [o], [i])
+        op(n, {"a": lambda: S.activation(o[0], i[0], F.Copy), "v": lambda: V.tensor_copy(o[0], i[0])}, [o], [i])
 
-    def lin(n, o, i, scale, bias=None):
-        if bias is None:
-            op(n, {"a": lambda: g.scalar.activation(o[0], i[0], F.Copy, scale=scale),
-                   "v": lambda: g.vector.tensor_scalar(o[0], i[0], scale, None, A.mult)}, [o], [i])
-        else:
-            op(n, {"a": lambda: g.scalar.activation(o[0], i[0], F.Identity, bias=ap(bias), scale=scale),
-                   "v": lambda: g.vector.tensor_scalar(o[0], i[0], scale, ap(bias), A.mult, A.add)}, [o], [i, bias])
+    def lin(n, o, i, scale, bias=0.0):
+        op(n, {"a": lambda: S.activation(o[0], i[0], F.Identity, bias=ap(bias), scale=ap(scale)),
+               "v": lambda: V.tensor_scalar(o[0], i[0], ap(scale), ap(bias), A.mult, A.add)}, [o], [i, scale, bias])
 
     def fill(n, o, c, k):
-        fns = {"v": lambda: g.vector.memset(o[0], c)}
-        if n != "zero" and k > 1:
-            fns["a"] = lambda: g.scalar.activation(o[0], T.zero[:, 0:k], F.Identity, bias=c, scale=1.0)
-        if c == int(c):
+        fns = {"v": lambda: V.memset(o[0], c)}
+        if n != "zero" and 1 < k <= 528:
+            fns["a"] = lambda: S.activation(o[0], T.zero[:, 0:k], F.Identity, bias=c, scale=1.0)
+        if c == int(c) and abs(c) < 1e7:
             fns["g"] = lambda: g.iota(o[0], [[0, k]], int(c), 0, allow_small_or_imprecise_dtypes=True)
         op(n, fns, [o], [] if n == "zero" else [vw("zero")])
 
     def scan(n, o, d0, d1, op0, op1, init=0.0):
-        op(n, {"v": lambda: g.vector.tensor_tensor_scan(o[0], d0[0], d1[0], init, op0, op1)}, [o], [d0, d1])
+        op(n, {"v": lambda: V.tensor_tensor_scan(o[0], d0[0], d1[0], ap(init), op0, op1)}, [o], [d0, d1, init])
 
     def tr(n, o, i):
-        op(n, {"v": lambda: g.vector.transpose(o[0], i[0])}, [o], [i])
+        op(n, {"v": lambda: V.transpose(o[0], i[0])}, [o], [i])
 
     def qz(n, o, s, i):
-        op(n, {"v": lambda: g.vector.quantize_mx(o[0], s[0], i[0])}, [o, s], [i])
+        op(n, {"v": lambda: V.quantize_mx(o[0], s[0], i[0])}, [o, s], [i])
 
     def act(n, o, i, f, scale, bias):
-        op(n, {"a": lambda: g.scalar.activation(o[0], i[0], f, bias=ap(bias), scale=ap(scale))}, [o], [i, scale, bias])
+        op(n, {"a": lambda: S.activation(o[0], i[0], f, bias=ap(bias), scale=ap(scale))}, [o], [i, scale, bias])
 
     def count(n, o, signs, i, scale, bias):
-        op(n, {"a": lambda: g.scalar.activation(signs[0], i[0], F.Sign, bias=bias[0], scale=scale, accum_out=o[0])},
+        op(n, {"a": lambda: S.activation(signs[0], i[0], F.Sign, bias=bias[0], scale=scale, accum_out=o[0])},
            [o, signs], [i, bias])
 
     def mm(n, o, l, ls, r, rs):
@@ -173,50 +152,51 @@ def _calls(g, core, T, topo, rank, helpers):
             op(n, {"g": lambda: g.iota(o[0], pat, base, cm, allow_small_or_imprecise_dtypes=True)}, [o], [])
 
     def dma(n, o, i, outs, ins, sem):
-        op(n, {"y": lambda: g.sync.dma_start(o, i), "a": lambda: g.scalar.dma_start(o, i)}, outs, ins, sem)
+        op(n, {"y": lambda: g.sync.dma_start(o, i), "a": lambda: S.dma_start(o, i)}, outs, ins, sem)
 
+    dma("lu", T.ub[:], T.u[:], [vw("ub")], [], "lu")
     for n, (a, e) in zip("ab", PIECES):
         dma("lx" + n, T.xb[:, 4 * a:4 * e], T.x[:, 4 * a:4 * e], [vw("xb", 4 * a, 4 * e)], [], "lx" + n)
-    dma("lu", T.ub[:], T.u[:], [vw("ub")], [], "lu")
     dma("lw", T.wq[:].bitcast(dt.uint8), T.wc[:], [vw("wq")], [], "lw")
     dma("ls", T.wsc[:], T.ws[:], [vw("wsc")], [], "ls")
     dma("lv", T.vb[:], T.v[:], [vw("vb")], [], "lv")
 
     def col(i):
         return vw("cf", i, i + 1)
-    TC, HC, PAR, T15, PN, NA, BS, BO, B1, B2, HN, W16, TINY, SQ, TH = [col(i) for i in range(15)]
+    TC, HC, PAR, PN, NA, BO, HO, B1, B2, W16, TINY, NTINY, SQ, CO, A0, A1, C0, C1, T2, GB, GC = [col(i) for i in range(21)]
     TCB = vw("cb", 0, 1)
-    fill("zero", vw("zero"), 0.0, 800)
-    for n, (name, a, e) in enumerate((("k16", 0, 800), ("br", 0, 800), ("br", 800, 1168), ("rb", 0, 48), ("rb", 1200, 1248))):
-        dma("z%d" % n, T[name][:, a:e], T.zero[:, 0:e - a], [vw(name, a, e)], [vw("zero")], "z%d" % n)
+    fill("zero", vw("zero"), 0.0, 528)
     iota("ci", vw("ci", 0, 1), [[0, 1]], 0, 1, True)
     iota("upi", vw("upi"), [[16, 8]], 0, 0, True)
-    iota("r4", vw("r4"), [[0, 24], [1, 16]])
-    iota("kc0", vw("kc", 0, 4), [[16, 4]], -48)
-    iota("kc1", vw("kc", 4, 8), [[-16, 4]])
-    iota("kk0", vw("kk2", 0, 128), [[-16, 4], [2048, 2], [1, 16]], 48)
-    iota("kk1", vw("kk2", 128, 256), [[16, 4], [2048, 2], [1, 16]])
-    iota("hi", vw("hi"), [[0, 4], [1, 2], [0, 16]])
+    iota("r4", vw("r4"), [[0, 26], [1, 16]])
+    iota("kc0", vw("kc"), [[-1, 2], [32, 4]], 2)
+    iota("k20", vw("k2"), [[-2, 64]], -31)
     at = 0
-    for a in range(12):
-        iota("yf%d" % a, vw("yf", at, at + 25 - 2 * a), [[1, 25 - 2 * a]], 33 * a)
-        at += 25 - 2 * a
-    iota("yf12", vw("yf", at, 176), [[0, 176 - at]], 13 * 32)
+    for a in range(13):
+        k = 25 - 2 * a if a < 12 else 176 - at
+        iota("yf%d" % a, vw("yf", at, at + k), [[1 if a < 12 else 0, k]], 33 * a if a < 12 else 13 * 32)
+        at += k
+    iota("cpt", vw("cpt"), [[8, 32]], 1)
     iota("nb", vw("f1", 0, 96, 4), [[-1, 24]])
-    iota("posi", vw("posi"), [[1, 192]], P0 // 2 - 32)
-    iota("vi", vw("vi"), [[1, 32], [0, 2]])
+    iota("pos", vw("pos"), [[1, 192], [0, 2]], P0 // 2 - 32)
     op("eb", {"g": lambda: g.affine_select(T.eb[:], T.zero[:, 0:528], [[-1, 528]], A.not_equal, 1.0, 3, 4)},
        [vw("eb")], [vw("zero")])
     for n, (name, a, e, s, c) in enumerate((
-            ("dv", 192, 193, 1, 0.0), ("ar", 1, 2, 1, -2.0), ("br", 1153, 1154, 1, 2.0), ("k16", 0, 800, 16, -256.0),
-            ("vl", 24, 25, 1, 1000.0), ("vr", 0, 1, 1, 1000.0), ("ar", 0, 1156, 3, 64.0), ("ar", 2, 1156, 3, -64.0),
-            ("arow", 0, 16, 1, 77.0),
-            ("rsf", 176, 192, 1, 0.0), ("e0", 0, 96, 4, 0.0), ("e0", 1, 96, 4, 1.0), ("e0", 3, 96, 4, -1.0),
+            ("ab", 1, 2, 1, -512.0), ("ab", BR + 1153, BR + 1154, 1, 512.0), ("k16", 0, 544, 1, 0.0), ("k16", 0, 544, 16, -2048.0),
+            ("kk", 0, 288, 2, 0.0), ("ab", 0, 1152, 3, 1024.0), ("ab", 2, 1152, 3, -1024.0),
+            ("e0", 0, 96, 4, 0.0), ("e0", 1, 96, 4, 1.0), ("e0", 3, 96, 4, -1.0),
             ("f0", 0, 96, 4, -1e6), ("f0", 3, 96, 4, 0.0), ("f1", 1, 96, 4, -1e6),
-            ("cf", 12, 13, 1, 1e-37), ("cf", 13, 14, 1, -204.5))):
+            ("cf", 10, 11, 1, 1e-37), ("cf", 11, 12, 1, -1e-37), ("cf", 12, 13, 1, -204.5),
+            ("rb", 0, 48, 1, 0.0), ("rb", 1200, 1248, 1, 0.0), ("c2", 0, 160, 1, 0.0), ("kk", 0, 288, 144, -64.0),
+            ("kk", 1, 288, 2, 0.125), ("kk", 65, 128, 2, -0.125), ("kk", 209, 288, 2, -0.125), ("zz", P0 + C + 2, 4224, ZW, 0.0),
+            ("sg", C, C + 1, 1, 1.0), ("ns", 0, 1, 1, 1.0), ("ns", 193, 194, 1, 0.0),
+            ("da", 0, 512, 2, 1e29), ("db", 1, 512, 2, 1e29), ("vt", 132, GF, 2, 1.0), ("vt", 129, GF, 2, 194.0))):
         fill("f%d" % n, vw(name, a, e, s), c, len(range(a, e, s)))
-    for c in (0, 64, 65, 66, 67, P0 + C, P0 + C + 1):
+    for c in (0, 64, 65, 66, 67, P0 + C, P0 + C + 1, P0 + C + 3):
         fill("zz%d" % c, vw("zz", c, 4 * ROUNDS * ZW, ZW), 0.0, 4 * ROUNDS)
+    iota("vt0", vw("vt", 0, 132, 2), [[1, 33], [0, 2]], -32)
+    iota("vt1", vw("vt", 1, 128, 2), [[1, 32], [0, 2]], 196)
+    iota("mk", vw("mk", 0, 8), [[0, 4], [1, 2]])
 
     ts("c1", vw("ci", 1, 2), vw("ci", 0, 1), 15, A.bitwise_and)
     ts("c2", vw("ci", 2, 3), vw("ci", 0, 1), 4, A.logical_shift_right, 1, A.bitwise_and)
@@ -228,57 +208,54 @@ def _calls(g, core, T, topo, rank, helpers):
         lo = 0 if rank == 0 else 128
         for t in range(ROUNDS):
             qz("zq%d" % t, vw("lq%d" % t, lo, lo + 128), vw("ls%d" % t, lo, lo + 128), vw("zero", 0, 512))
-    lin("t15", T15, TC, -1.0, 15.0)
     lin("pn", PN, PAR, -1.0, 65.0)
     ts("na", NA, PAR, HC, A.not_equal)
-    lin("bs", BS, TC, -0.5, 7.25)
     lin("bo", BO, TC, -1.0, 15.5)
-    lin("b1", B1, TC, -1.0 / 16, 192.0 - 17.0 / 32)
-    lin("b2", B2, TC, 1.0 / 16, -192.0 - 15.0 / 32)
-    lin("hn", HN, HC, -2048.0, 0.25)
+    lin("ho", HO, TC, -2.0, 30.0)
+    lin("t2c", T2, TC, 2.0)
+    lin("b2", B2, TC, 16.0, -49152.0 - 120.0)
+    lin("b1a", GB, PAR, 16.0)
+    lin("b1", B1, B2, -1.0, GB)
     lin("w16", W16, TC, 16.0)
-    lin("thc", TH, TC, -1.0, -0.5)
-    lin("kc", vw("kc"), vw("kc"), 1.0, TH)
+    lin("coa", GC, TC, -1.0, 223.0)
+    lin("co", CO, PAR, float(TW), GC)
+    for n, c, s, b in (("a0", A0, -16896.0, 16384.0), ("a1", A1, 16896.0, -512.0), ("c0", C0, -16896.0, 512.0), ("c1c", C1, 16896.0, -16384.0)):
+        lin(n, c, PAR, s / 1024, b / 1024)
+    lin("kc", vw("kc"), vw("kc"), 1.0, T2)
+    lin("k2", vw("k2"), vw("k2"), 1.0, T2)
     ts("kh", vw("kh"), vw("r4"), TCB, A.is_equal, 1024.0, A.mult)
-    lin("kd", vw("kd"), vw("kh"), 1.0, -1.0)
-    lin("kd2", vw("kd2"), vw("kh"), 1.0, -2.0)
-    r16 = vw("r4", 0, 64)
-    for name, vo, vc in (("ta", 64.0, -2.0), ("tb", 2.0, -64.0)):
-        ts(name + "o", vw(name, 1, 128, 2), r16, TCB, A.is_equal, vo, A.mult)
-        ts(name + "c", vw(name, 0, 128, 2), r16, TCB, A.is_equal, vc, A.mult)
-    for e in range(2):
-        ts("tm%d" % e, vw("tm", e, 128, 2), r16, TCB, A.not_equal, -5.0, A.mult)
-    lin("tm", vw("tm"), vw("tm"), 1.0, 4.0)
-    act("thr", vw("thr"), vw("kk2"), F.Abs, 1.0, HN)
-    ts("ka", vw("ka"), vw("hi"), HC, A.is_equal, 1.0 / 16, A.mult)
-    lin("kb", vw("kb"), vw("ka"), -1.0)
-    fill("ka1", vw("ka", 31, 128, 32), 64.0, 4)
-    fill("kb1", vw("kb", 0, 128, 32), -64.0, 4)
+    lin("kd", vw("kd"), vw("kh", 0, C), 1.0, -2.0)
+    for h, (x, y) in enumerate(((A0, C0), (A1, C1))):
+        lin("ta%d" % h, vw("ta", TW * h, TW * h + TW), vw("kh"), x)
+        lin("tb%d" % h, vw("tb", TW * h, TW * h + TW), vw("kh"), y)
+        lin("tm%d" % h, vw("tm", TW * h, TW * h + TW), vw("kh"), 0.5, -64.0)
+    lin("ari", vw("ga", 0, 176), vw("yf", 0, 176), 8.0, 32768.0 + 160.0)
+    lin("arp", vw("arow", 0, 176), vw("ga", 0, 176), 1.0, -32768.0)
+    lin("arn", vw("arow", 176, 352), vw("ga", 0, 176), -1.0, 32768.0)
     scan("yd", vw("yf", 176, 352), vw("kd", 0, 176), vw("yf", 0, 176), A.add, A.min)
-    lin("ari", vw("ga"), vw("yf", 0, 176), 1.0 / 32, 192.0 - 0.49)
-    lin("arow", vw("arow", 16, 192), vw("ga"), 1.0, -192.0)
-    tt("rsf", vw("rsf", 0, 176), vw("arow", 16, 192), vw("arow", 15, 191), A.is_equal)
-    lin("rsb", vw("rsb"), vw("rsf", 1, 177), -8.0, 8.0)
-    ts("gi0", vw("gi", 0, 11), vw("yf", 191, 352, 16), T15, A.add)
+    ts("gi0", vw("gi", 0, 11), vw("yf", 191, 352, 16), HO, A.add)
     ts("gi1", vw("gi", 12, 23), vw("gi", 0, 11), 31, A.bitwise_and)
     cp("gl0", vw("gl", 0, 11), vw("gi", 12, 23))
-    ts("gl1", vw("gl", 12, 23), vw("gi", 12, 23), 48.0, A.mult, 1.0, A.add)
-    for e in range(2):
-        lin("pos%d" % e, vw("pos", e, C, 2), vw("posi"), 1.0 / 256)
-    ts("sf0", vw("sf", 0, 1), NA, 272.0, A.mult, W16, A.add)
-    ts("sf1", vw("sf", 1, 2), NA, -144.0, A.mult, W16, A.add)
+    ts("gl1", vw("gl", 11, 22), vw("gi", 12, 23), 25.0, A.add)
+    mv("cap", vw("cap"), ind(vw("cpt"), vw("gl", 0, 11)))
+    lin("sf0", vw("sf", 0, 1), NA, 272.0, W16)
+    lin("sf1", vw("sf", 1, 2), NA, -144.0, W16)
+    lin("sf2", vw("sf", 2, 3), NA, 144.0, W16)
     ts("sl0", vw("sl", 0, 1), vw("sf", 0, 1), 15.0, A.add)
     ts("sl1", vw("sl", 2, 3), vw("sf", 1, 2), 687.0, A.add, 799.0, A.min)
-    fill("vt0", vw("vt", 0, GF, 2), 1.0 / 256, GF // 2)
-    fill("vt1", vw("vt", 1, GF, 2), 194.0 / 256, GF // 2)
-    lin("vt2", vw("vt", 2, 4, 2), vw("vi", 0, 1), 1.0 / 256, -32.0 / 256)
-    lin("vt3", vw("vt", 4, 130, 2), vw("vi", 0, 63), 1.0 / 256, -31.0 / 256)
-    lin("vt4", vw("vt", 1, 128, 2), vw("vi"), 1.0 / 256, 195.0 / 256)
+    ts("sl2", vw("sl", 4, 5), vw("sf", 2, 3), -176.0, A.add)
+    ts("sl3", vw("sl", 6, 7), vw("sf", 2, 3), 80.0, A.add, 287.0, A.min)
+    ts("mk0", vw("mk", 0, 8), vw("mk", 0, 8), HC, A.not_equal, -100.0, A.mult)
+    lin("mk1", vw("mk", 8, 16), vw("mk", 0, 8), -1.0, -100.0)
+    lin("sn0", vw("dd", 15, 16), vw("kh", 15, 16), 4.0, -1000.0)
+    lin("sn1", vw("dd", 415, 416), vw("kh", 0, 1), 4.0, -1000.0)
+    lin("c90", vw("c9", 0, 1), PAR, -1.0, 436.0)
+    lin("c91", vw("c9", 1, 2), PAR, 1.0, -45.0)
     for b in range(4):
         qz("eq%d" % b, vw("eq", 128 * b, 128 * b + 128), vw("es", 128 * b, 128 * b + 128), vw("eb", 3 - b, 515 - b))
     qz("uq", vw("uq"), vw("us"), vw("ub"))
-    op("uq2", {"v": lambda: g.vector.tensor_copy(T.uq2[:, 0:128].bitcast(dt.uint32),
-                                                 T.uq[:, 0:128].bitcast(dt.uint32).indirect(T.upl[:, 0:8]))},
+    op("uq2", {"v": lambda: V.tensor_copy(T.uq2[:, 0:128].bitcast(dt.uint32),
+                                          T.uq[:, 0:128].bitcast(dt.uint32).indirect(T.upl[:, 0:8]))},
        [vw("uq2")], [vw("uq"), vw("upl")])
     mv("us2", vw("us2", 0, 128), ind(vw("us", 0, 128), vw("upl", 0, 8)))
     qz("vq", vw("vq"), vw("vs"), vw("vb"))
@@ -290,7 +267,7 @@ def _calls(g, core, T, topo, rank, helpers):
     def send(t, kind, sem):
         xs = []
         for s in sides:
-            h = helpers[(rank, s)]
+            h = helpers[(rank, s if kind == "q" else s + 2)]
             rid, pid = topo.addr(h, core)
             es = topo.engines(core, h)
             src, dst = T["m%s%d" % (kind, t)][:, TM * s:TM * s + TM], T["h%s%d" % (kind, t)][:]
@@ -301,14 +278,14 @@ def _calls(g, core, T, topo, rank, helpers):
         op("send" + kind, {"g": lambda: g.remote_dma_fused(xs, local_sem=T.sem.sent)}, [(None, [("sent%d" % t, 0, 1, 1)])],
            [vw("m%s%d" % (kind, t))], "sent")
 
-    def sm(i):
-        return vw("sm", 24 * i, 24 * i + 24)
-
     def sb(i, n):
         return vw("sb", 32 * i, 32 * i + n)
 
     def bank(b, n, a=0):
         return vw("ps", 512 * b + a, 512 * b + n)
+
+    def br(a, e, s=1, rev=False):
+        return vw("ab", BR + a, BR + e, s, rev)
 
     for t in range(ROUNDS):
         tag[0] = "%d." % t
@@ -317,103 +294,101 @@ def _calls(g, core, T, topo, rank, helpers):
             return vw("zz", ZW * (4 * t + b) + a, ZW * (4 * t + b) + e)
 
         for n, (a, e) in enumerate(PIECES):
-            aq, asc = vw("aq%d" % t, a, e), vw("as%d" % t, a, e)
-            mm("ms%d" % n, bank(n, e - a), vw("uq2"), vw("us2"), aq, asc)
+            mm("ms%d" % n, bank(n, e - a), vw("uq2"), vw("us2"), vw("aq%d" % t, a, e), vw("as%d" % t, a, e))
+        act("ns", vw("ns", 1, 193), bank(0, 192), F.Sign, -1.0, NTINY)
+        for n, (a, e) in enumerate(PIECES):
             act("sg%d" % n, vw("sg", a, e), bank(n, e - a), F.Sign, 1.0, TINY)
         for n, (a, e) in enumerate(PIECES):
-            aq, asc = vw("aq%d" % t, a, e), vw("as%d" % t, a, e)
             for b in range(4):
                 k = (2 + 4 * n + b) % 8
-                mm("mp%d%d" % (n, b), bank(k, e - a), vw("wq", 128 * b, 128 * b + 128), vw("wsc", 128 * b, 128 * b + 128), aq, asc)
+                mm("mp%d%d" % (n, b), bank(k, e - a), vw("wq", 128 * b, 128 * b + 128), vw("wsc", 128 * b, 128 * b + 128),
+                   vw("aq%d" % t, a, e), vw("as%d" % t, a, e))
                 lin("lay%d%d" % (n, b), plane(b, P0 + a, P0 + e), bank(k, e - a), 0.0625)
+                if n and b % 2:
+                    lin("lb%d" % b, vw("db", b - 1, 512, 4), bank(k, e - a), 0.0625)
         for b in range(4):
-            dma("pp%d" % b, T.pp[:, C * b:C * b + C], plane(b, P0, P0 + C)[0], [vw("pp", C * b, C * b + C)],
-                [plane(b, P0, P0 + C)], "p%d" % b)
-        S = vw("sg")
-        scan("dl", vw("dv", 0, 192, rev=True), vw("zero", 0, 192), vw("sg", 0, 192, rev=True), A.add, A.subtract)
-        scan("dr", vw("dv", 193, 385), vw("sg", 192, C), vw("zero", 0, 192), A.add, A.add)
-        D, Dr = vw("dv", 0, 385), vw("dv", 0, 385, rev=True)
-        D0, DE = vw("dv", 0, 1), vw("dv", C, C + 1)
-        scan("L", vw("lr", 0, 385), D, D, A.min, A.min, 999.0)
-        scan("R", vw("rr", 0, 385, rev=True), Dr, Dr, A.min, A.min, 999.0)
-        scan("sd", vw("sd"), vw("kd2"), S, A.add, A.min)
-        scan("dd", vw("dd"), vw("kd"), vw("dv", 1, 385), A.add, A.min)
-        SR, RAW, HV, OPEN = vw("sd", 15, C, 16), vw("dd", 15, C, 16), vw("e1", 3, 96, 4), vw("e0", 2, 96, 4)
-        lin("s1", sm(0), SR, -0.25, BS)
-        lin("open", OPEN, SR, 0.5, BO)
-        lin("qb", sb(0, 24), vw("dv", 8, C, 16), 1.0 / 16, 192.0)
-        lin("q16", sm(1), sb(0, 24), -16.0, 3072.0)
-        tt("s2", sm(2), sm(0), sm(1), A.add)
-        tt("hr", sm(3), RAW, sm(2), A.add)
-        ts("o1", vw("o1"), sm(3), 2.0, A.mult, 64.0, A.add)
-        tt("hv", HV, RAW, sm(0), A.add)
-        lin("nd", vw("al", 1, 2), D0, -1.0)
-        lin("th0", vw("th", 0, 4), vw("kc", 0, 4), -1.0, vw("al", 1, 2))
-        lin("th1", vw("th", 4, 8), vw("kc", 4, 8), 1.0, DE)
+            e = HALF if b % 2 else C
+            dma("pp%d" % b, T.pp[:, C * b:C * b + e], plane(b, P0, P0 + e)[0], [vw("pp", C * b, C * b + e)],
+                [plane(b, P0, P0 + e)], "p%d" % b)
+        scan("dl", vw("ev", 0, 193, rev=True), vw("ns", 1, 194, rev=True), vw("ns", 0, 193, rev=True), A.add, A.add, -1.0)
+        scan("dr", vw("ev", 193, 386), vw("sg", 191, C), vw("sg", 192, C + 1), A.add, A.add, vw("ev", 192, 193))
+        E0, EE = vw("ev", 0, 1), vw("ev", 385, 386)
+        for n, a, e, i in (("L0", 0, 193, 999.0), ("L1", 193, 385, vw("lr", 192, 193))):
+            scan(n, vw("lr", a, e), vw("ev", a, e), vw("ev", a, e), A.min, A.min, i)
+        scan("R0", vw("rr", 1, 386, rev=True), vw("ev", 1, 386, rev=True), vw("ev", 1, 386, rev=True), A.min, A.min, 999.0)
+        scan("dd", vw("dd", 16, 400), vw("kd"), vw("ev", 1, 385), A.add, A.min)
+        scan("sd", vw("sd"), vw("kd"), vw("sg", 0, C), A.add, A.min)
+        SR, RAW, HV, OPEN = vw("sd", 15, C, 16), vw("dd", 31, 400, 16), vw("e1", 3, 96, 4), vw("e0", 2, 96, 4)
+        LV, RV = vw("lr", 0, 385, 16), vw("rr", 1, 386, 16)
+        ND, AL = vw("al", 1, 2), vw("al", 0, 1)
+        lin("nd", ND, E0, -1.0, -1.0)
+        lin("th0", vw("th", 0, 4), vw("kc", 0, 4), 1.0, ND)
+        lin("th1", vw("th", 4, 8), vw("kc", 4, 8), -1.0, EE)
+        lin("tr0", vw("thr", 0, 64), vw("k2"), 1.0, E0)
+        lin("tr1", vw("thr", 64, 128), vw("k2"), 1.0, EE)
         for i in range(8):
-            ends = vw("lr", 16, 385, 16) if i < 4 else vw("rr", 0, C, 16)
-            count("n%d" % i, vw("n1", i, i + 1), vw("jk", 24 * i, 24 * i + 24), ends, 1.0 if i < 4 else -1.0, vw("th", i, i + 1))
-        lin("vl", vw("vl", 0, 24), HV, -1.0, D0)
-        lin("vr", vw("vr", 1, 25), HV, -1.0, DE)
-        for e in range(2):
-            ts("o16%d" % e, vw("o16", e, 16, 2), vw("n1"), 0.5, A.mult, 12.0, A.add)
-        lin("of0", vw("off", 0, 4), vw("n1", 0, 4, rev=True), 0.5, 12.25)
-        lin("of1", vw("off", 4, 8), vw("n1", 4, 8), 0.5, 11.25 - 1.0 / 16)
-        tt("c20", vw("c2", 0, 128), ind(vw("vl", 0, 25), vw("o16", 0, 8)), vw("thr", 0, 128), A.is_lt)
-        tt("c21", vw("c2", 128, 256), ind(vw("vr", 0, 25), vw("o16", 8, 16)), vw("thr", 128, 256), A.is_ge)
-        for i in range(2):
-            tr("t2%d" % i, vw("t2", 128 * i, 128 * i + 128), vw("c2", 128 * i, 128 * i + 128))
-        scan("n20", vw("n2", 0, 128), vw("ka", rev=True), vw("t2", 0, 128, rev=True), A.add, A.min)
-        scan("n21", vw("n2", 128, 256), vw("kb"), vw("t2", 128, 256), A.add, A.max)
-        tt("mi", vw("mi"), vw("n2", 31, 256, 32), vw("off"), A.add)
-        ts("ml", vw("ml"), vw("mi"), 16.0, A.mult)
+            count("n%d" % i, vw("n1", i, i + 1), vw("jk", 25 * i, 25 * i + 25), LV if i < 4 else RV, 1.0 if i < 4 else -1.0,
+                  vw("th", i, i + 1))
+        ts("o16", vw("o16"), vw("n1"), 8.0, A.mult, 215.0, A.add)
+        lin("of0", vw("off", 0, 4), vw("n1", 0, 4), -0.5, 13.5)
+        lin("of1", vw("off", 4, 8), vw("n1", 4, 8), 0.5, 14.5)
+        tt("j0", vw("kk", 16, 144, 16), vw("off"), vw("mk", 0, 8), A.add)
+        tt("j1", vw("kk", 160, 288, 16), vw("off"), vw("mk", 8, 16), A.add)
+        tt("cm", vw("c2", 16, 144), ind(vw("dd"), vw("o16")), vw("thr"), A.is_lt)
+        tr("t20", vw("t2", 0, 128), vw("c2", 16, 144))
+        tr("t21", vw("t2", 128, 288), vw("c2"))
+        scan("nn", vw("n2"), vw("kk"), vw("t2"), A.add, A.max)
+        ts("ml0", vw("ml", 0, 16), ind(vw("n2"), vw("sl", 4, 5)), -16.0, A.mult, vw("c9", 0, 1), A.add)
+        ts("ml1", vw("ml", 16, 32), ind(vw("n2"), vw("sl", 6, 7)), 16.0, A.mult, vw("c9", 1, 2), A.add)
         for b in range(4):
-            mv("mt%d" % b, vw("mt", b, 512, 4), ind(plane(b, 64, DR), vw("ml")))
+            mv("mt%d" % b, vw("mt", b, 512, 4), ind(plane(b, 64, DR), vw("ml", 12, 20)))
         qz("mq", vw("mq%d" % t), vw("ms%d" % t), vw("mt"))
         send(t, "q", "ha%d")
-        send(t, "s", "hb%d")
+        send(t, "s", "ha%d")
         op("arr", {}, [vw("lq%d" % t, 64, 192), vw("ls%d" % t, 64, 192)], [(None, [("sent%d" % t, 0, 1, 1)])], "arr%d" % t)
+        ts("o1", vw("o1"), RAW, 0.5, A.mult, CO, A.add)
         mv("xa", vw("xa"), ind(vw("ta"), vw("o1")))
         mv("xc", vw("xc"), ind(vw("tb"), vw("o1")))
-        mv("xm", vw("br", 5, 5 + 3 * C, 3), ind(vw("tm"), vw("o1")))
-        scan("ar", vw("ar", 4, 4 + 3 * C, 3), vw("xa"), vw("pos"), A.add, A.min, -2.0)
-        scan("br", vw("br", 1, 1 + 3 * C, 3, rev=True), vw("xc", rev=True), vw("pos", rev=True), A.add, A.max, 2.0)
-        BASE = vw("e1", 2, 100, 4)
-        tt("base", BASE, vw("lr", 0, 385, 16), vw("rr", 0, 385, 16), A.max)
-        lin("q1", sb(1, 25), vw("dv", 0, 385, 16), 1.0 / 16, B1)
-        lin("q2", sb(2, 25), BASE, -1.0 / 16, B2)
-        tt("cc", sb(3, 25), sb(1, 25), sb(2, 25), A.add)
-        tt("ea", vw("ea"), ind(sb(3, 25), vw("gl", 0, 11)), vw("arow", 16, 192), A.is_equal)
-        lin("ec", vw("ec"), vw("ea"), -4.0, 4.0)
-        tt("ga", vw("ga"), ind(vw("ar", 0, 1156), vw("gl", 12, 23)), vw("ea"), A.mult)
-        tt("gb", vw("gb"), ind(vw("br"), vw("gl", 12, 23)), vw("ec"), A.max)
-        scan("gf", vw("vt", GF, GF + 176), vw("rsf", 0, 176), vw("ga"), A.mult, A.max)
-        scan("gr", vw("vt", GF + 176, GF + 352, rev=True), vw("rsb", rev=True), vw("gb", rev=True), A.add, A.min)
-        lin("b0", vw("e1", 0, 96, 4), vw("e1", 6, 100, 4), 1.0)
-        lin("bn", vw("e1", 1, 96, 4), vw("e1", 2, 96, 4), -1.0)
-        scan("de", vw("e2"), vw("e0"), vw("e1", 0, 96), A.mult, A.add)
+        mv("xm", br(5, 5 + 3 * C, 3), ind(vw("tm"), vw("o1")))
+        scan("ar", vw("ab", 4, 4 + 3 * C, 3), vw("xa"), vw("pos"), A.add, A.min, -512.0)
+        scan("br", br(1, 1 + 3 * C, 3, True), vw("xc", rev=True), vw("pos", rev=True), A.add, A.max, 512.0)
+        BASE = vw("bs", 0, 25)
+        tt("base", BASE, LV, RV, A.max)
+        lin("q1", sb(1, 25), vw("ev", 1, 386, 16), 8.0, B1)
+        lin("q2", sb(2, 25), BASE, -8.0, B2)
+        tt("cc", vw("cc", 0, 25), sb(1, 25), sb(2, 25), A.add)
+        tt("kf", vw("key", 0, 25), vw("ab", 1, 1156, 48), vw("cc", 0, 25), A.subtract)
+        tt("kb", vw("key", 25, 50), br(1, 1156, 48), vw("cc", 0, 25), A.add)
+        tt("ga", vw("ga"), ind(vw("key", 0, 50), vw("gl", 0, 22)), vw("arow"), A.add)
+        scan("gf", vw("vt", GF, GF + 176), vw("ga", 0, 176), vw("cap"), A.max, A.min)
+        scan("gr", vw("vt", GF + 176, GF + 352, rev=True), vw("ga", 176, 352, rev=True), vw("cap", rev=True), A.min, A.max, 512.0)
+        lin("open", OPEN, SR, 0.5, BO)
+        lin("hv", HV, RAW, 1.0, HO)
+        lin("b0", vw("e1", 0, 96, 4), vw("bs", 1, 25), 1.0)
+        lin("bn", vw("e1", 1, 96, 4), vw("bs", 0, 24), -1.0)
+        lin("bp", vw("e1", 2, 96, 4), vw("bs", 0, 24), 1.0)
+        scan("de", vw("e2"), vw("e0"), vw("e1"), A.mult, A.add)
         DL = vw("e2", 3, 96, 4)
-        lin("ab", sb(4, 24), DL, 1.0 / 16, 192.0 - 31.0 / 64)
-        act("sq", vw("f0", 2, 96, 4), sb(4, 24), F.Square, 1.0, SQ)
+        lin("ab", sb(0, 24), DL, 1.0 / 32, 192.0 - 15.0 / 32)
+        act("sq", vw("f0", 2, 96, 4), sb(0, 24), F.Square, 1.0, SQ)
         lin("rp", vw("f1", 2, 96, 4), DL, -1e5, -2.5e4)
         lin("ow", vw("f0", 1, 96, 4), OPEN, 177.0, GF + 156.25)
-        lin("al", vw("al", 0, 1), D0, -1.0, DE)
-        act("es", sm(4), OPEN, F.Identity, vw("al", 0, 1), D0)
-        tt("vi", sm(5), sm(4), HV, A.subtract)
-        lin("v2", vw("f1", 3, 96, 4), sm(5), 2.0)
+        lin("al", AL, EE, 1.0, ND)
+        act("es", vw("sm"), OPEN, F.Identity, AL, E0)
+        tt("v2", vw("f1", 3, 96, 4), vw("sm"), HV, A.subtract)
         scan("ogs", vw("f2"), vw("f0"), vw("f1"), A.subtract, A.max)
         cp("og", vw("og"), vw("f2", 3, 96, 4))
-        for n, (a, e) in enumerate(((0, 288), (288, C))):
-            mv("lk%d" % n, vw("br", 3 + 3 * a, 3 + 3 * e, 3), ind(vw("vt"), vw("og", a // 16, e // 16)))
-            scan("rb%d" % n, vw("rb", 48 + 3 * a, 48 + 3 * e), vw("ar", 3 * a, 3 * e), vw("br", 3 + 3 * a, 3 + 3 * e), A.max, A.min)
+        for n, (a, e) in enumerate(((0, 160), (160, 288), (288, C))):
+            mv("lk%d" % n, br(3 + 3 * a, 3 + 3 * e, 3), ind(vw("vt"), vw("og", a // 16, e // 16)))
+            scan("rb%d" % n, vw("rb", 48 + 3 * a, 48 + 3 * e), vw("ab", 3 * a, 3 * e), br(3 + 3 * a, 3 + 3 * e), A.max, A.min)
         tr("t1a", vw("tt", 0, 256), vw("rb", 50, 816, 3))
         tr("t2a", vw("tt", 256, 544), vw("rb", 2, 864, 3))
-        scan("tsa", vw("ts", 0, 544), vw("k16", 0, 544), vw("tt", 0, 544), A.add, A.max)
-        ts("ola", vw("ol", 0, 16), ind(vw("ts", 0, 544), vw("sl", 0, 1)), 512.0, A.mult, PN, A.add)
+        scan("tsa", vw("ts", 0, 544), vw("k16"), vw("tt", 0, 544), A.add, A.max)
+        ts("ola", vw("ol", 0, 16), ind(vw("ts", 0, 544), vw("sl", 0, 1)), 2.0, A.mult, PN, A.add)
         tr("t2b", vw("tt", 544, 672), vw("rb", 866, 1248, 3))
         tr("t1b", vw("tt", 672, 800), vw("rb", 818, 1200, 3))
-        scan("tsb", vw("ts", 544, 800), vw("k16", 544, 800), vw("tt", 544, 800), A.add, A.max)
-        ts("olb", vw("ol", 16, 32), ind(vw("ts"), vw("sl", 2, 3)), 512.0, A.mult, PN, A.add)
+        scan("tsb", vw("ts", 544, 800), vw("k16", 0, 256), vw("tt", 544, 800), A.add, A.max)
+        ts("olb", vw("ol", 16, 32), ind(vw("ts"), vw("sl", 2, 3)), 2.0, A.mult, PN, A.add)
         for b in range(4):
             mm("mu%d" % b, bank(2 + b, 128), vw("eq", 128 * b, 128 * b + 128), vw("es", 128 * b, 128 * b + 128),
                vw("lq%d" % t, 64, 192), vw("ls%d" % t, 64, 192))
@@ -421,7 +396,11 @@ def _calls(g, core, T, topo, rank, helpers):
             mv("ur%d" % b, plane(b, DR, DR + TM), bank(2 + b, 128, 64))
         aq, asc = "aq%d" % (t + 1), "as%d" % (t + 1)
         for n, (a, e) in enumerate(PIECES):
-            for b in range(4):
+            if n:
+                for b in (1, 3):
+                    mv("xg%d" % b, vw("da", b, 512, 4), ind(plane(b, 0, DR + TM), vw("ol", a // 16, e // 16)))
+                scan("xs", vw("xt", 4 * a, 4 * e), vw("da"), vw("db"), A.add, A.min)
+            for b in ((0, 2) if n else range(4)):
                 tt("x%d%d" % (n, b), vw("xt", 4 * a + b, 4 * e, 4), ind(plane(b, 0, DR + TM), vw("ol", a // 16, e // 16)),
                    vw("pp", C * b + a, C * b + e), A.add)
             qz("aq%d" % n, vw(aq, a, e), vw(asc, a, e), vw("xt", 4 * a, 4 * e))

@@ -4,7 +4,7 @@ from concourse.mybir import dt, AluOpType as A, ActivationFunctionType as F
 
 C, TM, ROUNDS = 384, 64, 2
 ZW = 528
-P0, DR = 68, 456
+P0, DR = 68, 454
 GF = 784
 TW = 416
 BR = 1200
@@ -15,19 +15,18 @@ X4, U8, BF, F32, I32, U16 = "float8_e4m3fn_x4", "uint8", "bfloat16", "float32", 
 SCRATCH = {"ps": ("psum", [128, 512 * 8], F32)}
 for _d, _s in ((X4, "aq0 384 aq1 384 aq2 384 uq 128 uq2 128 vq 128 wq 512 eq 512 mq0 128 mq1 128 hq0 64 hq1 64 lq0 256 lq1 256"),
                (U8, "as0 384 as1 384 as2 384 us 128 us2 128 vs 128 wsc 512 es 512 ms0 128 ms1 128 hs0 64 hs1 64 ls0 256 ls1 256"),
-               (BF, "xb 1536 ub 512 vb 512 eb 528 zz 4224 xt 1536 mt 512 pp 1536 da 512 db 512 zero 528 cb 2 r4 416 kh 416 kd 384 "
-                    "k16 544 ta 832 tb 832 tm 832 kk 288 cap 176 cpt 32 arow 352 pos 384 sg 400 ns 208 ev 400 lr 400 rr 400 sd 384 "
-                    "dd 416 jk 200 c2 160 t2 288 n2 288 sb 128 xa 384 xc 384 ab 2368 ga 352 vt 1136 rb 1248 tt 800 ts 800"),
-               (F32, "yb 384 cf 24 c9 2 kc 8 k2 64 thr 128 sf 4 th 8 n1 8 off 8 mk 16 sm 24 al 2 cc 32 key 56 "
-                     "e0 96 e1 96 e2 96 f0 96 f1 96 f2 96 bs 32 yf 352"),
-               (I32, "ci 16 upi 8 gi 24"), (U16, "upl 8 gl 24 sl 8 o16 8 ml 32 o1 24 og 24 ol 32")):
+               (BF, "xb 1536 ub 512 vb 512 eb 528 zz 4224 xt 1536 mt 512 pp 1536 da 512 db 512 zero 528 cb 4 r4 416 kh 416 kd 384 "
+                    "k16 544 ta 832 cap 176 cpt 32 arow 352 pos 384 sg 400 ev 400 lr 400 rr 400 sd 384 "
+                    "dd 384 jk 1536 sb 128 xa 384 xc 384 ab 2368 ga 352 vt 1136 rb 1248 tt 800 ts 800"),
+               (F32, "yb 384 cf 24 c9 2 kc 8 sf 4 th 8 n1 8 sm 24 al 2 cc 32 key 56 e0 96 e1 104 e2 96 f0 96 f1 96 f2 96 yf 352"),
+               (I32, "ci 16 upi 8 gi 24"), (U16, "upl 8 gl 24 sl 4 ml 8 o1 24 og 24 ol 32")):
     _w = _s.split()
     for _i in range(0, len(_w), 2):
         SCRATCH[_w[_i]] = ("sbuf", [128, int(_w[_i + 1])], _d)
 DMAS = ["lxa", "lxb", "lu", "lw", "ls", "lv", "p0", "p1", "p2", "p3"]
 SEMAPHORES = ["nv", "na", "nt", "ng", "st", "sent", "ha0", "ha1", "arr0", "arr1"] + DMAS
 PLAN = """
-lu:a zero:v f30:a ci:g c1:v f18:a c3:v f26:v c2:v f20:a upi:g f2:v zz455:a f13:v cf:v cb:v lxa:y r4:g yf3:g mk:g f25:v t2c:a f14:v yf10:g zq0:v kc0:g upl:v yf11:g f4:a uq:v f21:a b1a:a kh:v lxb:y uq2:v xqa:v mk0:v xqb:v ls:y coa:a c0:a b2:a a0:a k20:g zz64:a zz0:g yf2:g lw:y us2:a 0.ms0:t a1:a na:v kd:v yf5:g w16:a f24:g yf4:g c91:a kc:a c90:v co:a zz65:g yf9:g yf8:g sn1:v ta0:a 0.ms1:t yf0:g 0.ns:a 0.sg1:a ta1:v 0.dl:v mk1:v zz67:v yf6:g 0.sg0:a k2:v 0.L0:v yf12:g sf2:a 0.nd:a f22:a 0.dr:v ho:a c1c:a yf1:g 0.mp11:t f15:v zz453:a yf7:g zz66:v 0.mp00:t f23:g 0.mp01:t 0.th1:a 0.tr0:a 0.tr1:a zz452:g 0.th0:v 0.L1:v 0.n3:a sn0:v f19:g 0.R0:v 0.n1:a 0.n0:a 0.n2:a 0.n5:a 0.n6:a 0.mp13:t tb1:v f8:g sl2:v 0.dd:v eb:g sl3:v yd:v 0.mp02:t 0.n7:a 0.n4:a 0.o16:v 0.of0:v 0.base:v 0.of1:v 0.lay00:a 0.mp10:t 0.cm:v 0.mp12:t 0.o1:v 0.j1:v 0.j0:v pos:g 0.mp03:t 0.t21:v 0.t20:v 0.lay10:a gi0:v 0.lay13:v 0.lay02:a 0.nn:v cpt:g 0.sd:v lv:y 0.ml0:v 0.lay12:a nb:g 0.ml1:v 0.lay03:v 0.mt0:v 0.lay01:a 0.mt3:v f0:v gi1:v 0.lay11:a 0.xa:a 0.mt2:a 0.mt1:a b1:v 0.q2:a tb0:a 0.mq:v bo:v 0.bn:v 0.q1:v 0.b0:a f7:g 0.hv:v f9:v 0.ar:v ari:a 0.pp2:y f1:v sf0:v 0.bp:a 0.sendq:g 0.sends:g f29:v vt0:g 0.open:a arp:v 0.pp3:y eq3:v vt1:g 0.xc:a 0.de:v tm0:v 0.cc:v 0.al:a f12:a sf1:a 0.ab:a f10:a arn:v 0.br:v 0.arr:- 0.kf:v gl0:v gl1:v 0.kb:v 0.es:a f11:a 0.v2:v 0.sq:a f5:g 0.pp0:y 0.rp:v 0.ow:v 0.ga:v 0.ogs:v tm1:a sl1:v cap:a 0.gf:v 0.xm:a 0.gr:v 0.og:v 0.lk0:a eq2:v zq1:v 0.lk1:a 0.lk2:a f6:v sl0:v eq1:v f17:a f16:a f28:a f3:a pn:a eq0:v 0.rb0:v 0.lb1:a 0.mu1:t 0.rb1:v 0.mu3:t 0.rb2:v 0.mu0:t 0.lb3:a 0.t1a:v 0.t2a:v 0.mu2:t 0.t1b:v 0.pp1:y 0.t2b:v 0.tsa:v f27:a 0.ul1:a 0.ur1:a 0.ul3:a 0.tsb:v 0.ur3:a 0.ul0:a 0.ur0:a 0.ur2:a 0.ola:v 0.ul2:a 0.olb:v 0.x01:v 0.x03:v 0.xg3:a 0.x00:v 0.x02:v 0.xg1:a 0.xs:v 0.aq0:v 1.ms0:t 1.ns:a 1.sg0:a 0.x12:v 0.x10:v 0.aq1:v vq:v 1.mp03:t 1.dl:v 1.lay03:v 1.tr0:v 1.L0:v 1.ms1:t 1.sg1:a 1.dr:v 1.mp01:t 1.nd:a 1.lay01:a 1.sd:v 1.mp11:t 1.L1:v 1.R0:v 1.mp12:t 1.dd:v 1.q1:v 1.mp13:t 1.mp00:t 1.lay11:v 1.th0:a 1.tr1:a 1.base:v 1.o1:v 1.th1:a 1.lay00:v 1.hv:v 1.bp:v 1.bn:v 1.mp10:t 1.n1:a 1.n2:a 1.n3:a 1.n5:a 1.n7:a 1.n0:a 1.of0:v 1.n4:a 1.n6:a 1.o16:v 1.q2:a 1.lay10:v 1.of1:v 1.cm:v 1.open:v 1.j1:v 1.j0:v 1.pp0:y 1.xa:a 1.b0:a 1.xc:a 1.t20:v 1.t21:v 1.mp02:t 1.lay13:v 1.de:v 1.nn:v 1.ar:v 1.ml0:v 1.ml1:v 1.cc:v 1.br:v 1.mt1:v 1.lay12:a 1.lay02:a 1.mt2:v 1.mt3:a 1.mt0:a 1.ab:a 1.kf:v 1.ow:a 1.pp2:y 1.al:a 1.kb:v 1.lb3:a 1.es:a 1.mq:v 1.lb1:a 1.sendq:g 1.sends:g 1.ga:v 1.sq:a 1.arr:- 1.rp:a 1.xm:a 1.v2:v 1.ogs:v 1.gr:v 1.gf:v 1.og:v 1.lk1:a 1.lk2:a 1.lk0:v 1.rb1:v 1.rb0:v 1.mu0:t 1.pp3:y 1.rb2:v 1.ur0:a 1.t1a:v 1.mu2:t 1.ul0:a 1.ul2:a 1.t2a:v 1.mu3:t 1.t1b:v 1.ur2:a 1.t2b:v 1.tsa:v 1.mu1:t 1.tsb:v 1.ola:v 1.ur3:a 1.ul3:a 1.ur1:a 1.olb:v 1.x00:v 1.pp1:y 1.xg3:a 1.x02:v 1.ul1:a 1.x03:v 1.x01:v 1.xg1:a 1.xs:v 1.aq0:v 1.oc0:a 1.x10:v 1.x12:v 1.aq1:v 1.my0:t 1.yb0:a 1.my1:t 1.oc1:y 1.osc3:y 1.osc1:a 1.y0:a 1.yb1:v 1.osc2:y 1.y1:a 1.osc0:y
+zero:v ci:g c2:v c1:v c3:v upi:g r4:g zq0:v f17:a cpt:g upl:v cf:v lu:y f7:a kc0:g pos:g f23:a zz65:a f14:v zz64:a zz452:a coa:a zz66:g zz453:a f12:v a3:a f18:g a2:a cb:v nb:g c91:v na:v yf2:g f9:a t2c:a a1:a a0:a uq:v yf3:g b1a:v c90:a b2:a us2:a f8:a f15:a f11:v yf6:g u1:a uq2:v kc:a lxa:y b1:a vt0:g xqa:v lxb:y co:a bo:a kh:v ls:y lw:y 0.ms0:t f10:a zz67:a f6:a bo0:a w16:a zz0:a xqb:v f13:v kd:v 0.ms1:t yf9:g f1:g ta1:v u0:v 0.mp01:t yf12:g 0.ns:a 0.sg0:a 0.dl:v 0.sd0:v 0.mp00:t yf1:g 0.sg1:a 0.dr:v yf10:g ta0:a 0.mp11:t 0.nd:v 0.mp03:t 0.sd1:v yf0:g 0.lay01:a 0.L0:v yf4:g 0.mp13:t 0.th1:a 0.th0:a 0.mp12:t 0.lay00:a 0.dd:v 0.n1:a 0.n3:a 0.R0:v 0.n7:a 0.n4:a 0.lay11:v 0.n0:a 0.n2:a 0.o1:v 0.lay03:v 0.xa:v 0.lay13:v 0.mp02:t 0.n5:a eb:g 0.mp10:t 0.n6:a sf0:a yf5:g 0.lay12:a yf11:g yf7:g 0.lay10:v 0.ml0:v 0.lay02:v 0.mt00:a 0.mt01:a 0.base:v 0.ml1:v 0.mt03:v 0.mt11:a 0.mt02:v 0.mt10:a 0.mt12:v 0.mt13:v ho:a 0.xc:v 0.op0:a 0.al:a 0.q1:a yf8:g 0.op1:a 0.b0:a 0.mq:v yd:v 0.br:v gi0:v 0.bn:a 0.q2:a u2:a ari:a 0.ar:v 0.hv:a gi1:v 0.es:a pn:a vt1:g 0.cc:v 0.de:v f0:g 0.ow:a arn:a f20:a gl0:v 0.kf:v arp:a 0.ab:a 0.sendq:g 0.sends:g gl1:v f4:g 0.rp:a 0.pp2:y f22:a 0.kb:v sf1:a lv:y 0.sq:a eq2:v 0.v2:v f2:g cap:a 0.ga:v 0.ogs:v f16:a 0.xm:v 0.gf:v f3:g u3:a 0.og:v f5:a f19:a 0.gr:v 0.pp0:y 0.lk0:a eq0:v 0.lk1:v eq1:v sl1:v 0.pp3:y 0.arr:- 0.lk2:a 0.rb1:v 0.mu0:t 0.rb0:v 0.ul0:a 0.ur0:a eq3:v 0.mu3:t 0.rb2:v 0.mu1:t 0.ur1:a 0.pp1:y 0.t2a:v 0.t1a:v 0.t2b:v 0.mu2:t 0.t1b:v sl0:v 0.tsa:v 0.ur3:a 0.ul1:a 0.ul3:a f21:a 0.lb3:a 0.tsb:v 0.ola:v 0.olb:v 0.ul2:a 0.ur2:a 0.x00:v 0.x03:v 0.x01:v 0.x02:v 0.xg3:a 0.xg1:a 0.lb1:a 0.xs:v 0.aq0:v 1.ms0:t 0.x12:v 1.mp02:t 1.mp01:t 1.ns:a 0.x10:v 0.aq1:v 1.ms1:t 1.sg0:a 1.lay02:a 1.mp10:t 1.sg1:a vq:v zq1:v 1.dl:v 1.sd0:v 1.nd:v 1.L0:v 1.mp12:t 1.mp03:t 1.op0:v 1.dr:v 1.sd1:v 1.L1:v 1.lay01:a 1.lay12:a 1.R0:v 1.lay10:a 1.dd:v 1.th0:a 1.th1:a 1.lay03:v 1.q1:a 1.op1:a 1.mp13:t 1.lay13:a 1.pp3:y 1.o1:v 1.mp00:t 1.lay00:v 1.mp11:t 1.xa:v 1.base:v 1.n2:a 1.n5:a 1.n6:a 1.n7:a 1.n4:a 1.ml1:v 1.n3:a 1.n1:a 1.lay11:v 1.xc:v 1.mt12:v 1.n0:a 1.ml0:v 1.q2:a 1.mt10:a 1.br:v 1.mt11:a 1.mt13:a 1.cc:v 1.mt00:a 1.mt03:v 1.mt01:v 1.mt02:a 1.ar:v 1.al:a 1.kb:v 1.mq:v 1.b0:a 1.hv:a 1.kf:v 1.bn:a 1.de:v 1.sendq:g 1.sends:g 1.es:a 1.pp2:y 1.lb1:a 1.v2:v 1.ab:a 1.pp1:y 1.arr:- 1.ow:a 1.ga:v 1.rp:a 1.sq:a 1.ogs:v 1.gf:v 1.gr:v 1.og:v 1.xm:v 1.lk1:v 1.mu0:t 1.lk0:a 1.lk2:a 1.rb1:v 1.ul0:a 1.rb0:v 1.ur0:a 1.rb2:v 1.mu3:t 1.mu1:t 1.t2a:v 1.t1a:v 1.pp0:y 1.lb3:a 1.t1b:v 1.mu2:t 1.t2b:v 1.tsa:v 1.ur1:a 1.ur3:a 1.tsb:v 1.ola:v 1.ul3:a 1.ur2:a 1.olb:v 1.ul1:a 1.ul2:a 1.x00:v 1.xg3:a 1.x03:v 1.x01:v 1.x02:v 1.xg1:a 1.xs:v 1.aq0:v 1.x12:v 1.x10:v 1.oc0:y 1.aq1:v 1.my0:t 1.yb0:v 1.osc2:a 1.my1:t 1.yb1:v 1.oc1:y 1.y0:y 1.osc3:y 1.osc0:y 1.osc1:a 1.y1:a
 """
 
 
@@ -163,14 +162,13 @@ def _calls(g, core, T, topo, rank, helpers):
 
     def col(i):
         return vw("cf", i, i + 1)
-    TC, HC, PAR, PN, NA, BO, HO, B1, B2, W16, TINY, NTINY, SQ, CO, A0, A1, C0, C1, T2, GB, GC = [col(i) for i in range(21)]
+    TC, HC, PAR, PN, NA, BO, HO, B1, B2, W16, TINY, NTINY, SQ, CO, A0, A1, C0, T2, GB, GC = [col(i) for i in range(20)]
     TCB = vw("cb", 0, 1)
     fill("zero", vw("zero"), 0.0, 528)
     iota("ci", vw("ci", 0, 1), [[0, 1]], 0, 1, True)
     iota("upi", vw("upi"), [[16, 8]], 0, 0, True)
     iota("r4", vw("r4"), [[0, 26], [1, 16]])
     iota("kc0", vw("kc"), [[-1, 2], [32, 4]], 2)
-    iota("k20", vw("k2"), [[-2, 64]], -31)
     at = 0
     for a in range(13):
         k = 25 - 2 * a if a < 12 else 176 - at
@@ -182,21 +180,21 @@ def _calls(g, core, T, topo, rank, helpers):
     op("eb", {"g": lambda: g.affine_select(T.eb[:], T.zero[:, 0:528], [[-1, 528]], A.not_equal, 1.0, 3, 4)},
        [vw("eb")], [vw("zero")])
     for n, (name, a, e, s, c) in enumerate((
-            ("ab", 1, 2, 1, -512.0), ("ab", BR + 1153, BR + 1154, 1, 512.0), ("k16", 0, 544, 1, 0.0), ("k16", 0, 544, 16, -2048.0),
-            ("kk", 0, 288, 2, 0.0), ("ab", 0, 1152, 3, 1024.0), ("ab", 2, 1152, 3, -1024.0),
+            ("ab", 1, 2, 1, -1.0), ("ab", BR + 1153, BR + 1154, 1, 1.0), ("k16", 0, 544, 1, 0.0), ("k16", 0, 544, 16, -4.0),
+            ("ab", 0, 1152, 3, 2.0), ("ab", 2, 1152, 3, -2.0),
             ("e0", 0, 96, 4, 0.0), ("e0", 1, 96, 4, 1.0), ("e0", 3, 96, 4, -1.0),
             ("f0", 0, 96, 4, -1e6), ("f0", 3, 96, 4, 0.0), ("f1", 1, 96, 4, -1e6),
             ("cf", 10, 11, 1, 1e-37), ("cf", 11, 12, 1, -1e-37), ("cf", 12, 13, 1, -204.5),
-            ("rb", 0, 48, 1, 0.0), ("rb", 1200, 1248, 1, 0.0), ("c2", 0, 160, 1, 0.0), ("kk", 0, 288, 144, -64.0),
-            ("kk", 1, 288, 2, 0.125), ("kk", 65, 128, 2, -0.125), ("kk", 209, 288, 2, -0.125), ("zz", P0 + C + 2, 4224, ZW, 0.0),
-            ("sg", C, C + 1, 1, 1.0), ("ns", 0, 1, 1, 1.0), ("ns", 193, 194, 1, 0.0),
-            ("da", 0, 512, 2, 1e29), ("db", 1, 512, 2, 1e29), ("vt", 132, GF, 2, 1.0), ("vt", 129, GF, 2, 194.0))):
+            ("rb", 0, 48, 1, 0.0), ("rb", 1200, 1248, 1, 0.0),
+            ("sg", 0, 387, 386, 1.0), ("sg", 193, 194, 1, 0.0), ("da", 0, 256, 2, 1e29),
+            ("da", 256, 512, 2, 1e29), ("db", 1, 512, 2, 1e29), ("vt", 132, GF, 2, 1.0 / 512), ("vt", 129, GF, 2, 194.0 / 512))):
         fill("f%d" % n, vw(name, a, e, s), c, len(range(a, e, s)))
-    for c in (0, 64, 65, 66, 67, P0 + C, P0 + C + 1, P0 + C + 3):
+    for c in (0, 64, 65, 66, 67, P0 + C, P0 + C + 1):
         fill("zz%d" % c, vw("zz", c, 4 * ROUNDS * ZW, ZW), 0.0, 4 * ROUNDS)
     iota("vt0", vw("vt", 0, 132, 2), [[1, 33], [0, 2]], -32)
-    iota("vt1", vw("vt", 1, 128, 2), [[1, 32], [0, 2]], 196)
-    iota("mk", vw("mk", 0, 8), [[0, 4], [1, 2]])
+    iota("vt1", vw("vt", 1, 128, 2), [[1, 32], [0, 2]], 195)
+    for n, x in (("u0", vw("pos")), ("u1", vw("cpt")), ("u2", vw("vt", 0, 132, 2)), ("u3", vw("vt", 1, 128, 2))):
+        lin(n, x, x, 1.0 / 512)
 
     ts("c1", vw("ci", 1, 2), vw("ci", 0, 1), 15, A.bitwise_and)
     ts("c2", vw("ci", 2, 3), vw("ci", 0, 1), 4, A.logical_shift_right, 1, A.bitwise_and)
@@ -211,27 +209,27 @@ def _calls(g, core, T, topo, rank, helpers):
     lin("pn", PN, PAR, -1.0, 65.0)
     ts("na", NA, PAR, HC, A.not_equal)
     lin("bo", BO, TC, -1.0, 15.5)
+    lin("bo0", C0, TC, 1.0, -14.5)
     lin("ho", HO, TC, -2.0, 30.0)
     lin("t2c", T2, TC, 2.0)
-    lin("b2", B2, TC, 16.0, -49152.0 - 120.0)
-    lin("b1a", GB, PAR, 16.0)
+    lin("b2", B2, TC, 16.0 / 512, -96.0 - 120.0 / 512)
+    lin("b1a", GB, PAR, 16.0 / 512)
     lin("b1", B1, B2, -1.0, GB)
     lin("w16", W16, TC, 16.0)
     lin("coa", GC, TC, -1.0, 223.0)
     lin("co", CO, PAR, float(TW), GC)
-    for n, c, s, b in (("a0", A0, -16896.0, 16384.0), ("a1", A1, 16896.0, -512.0), ("c0", C0, -16896.0, 512.0), ("c1c", C1, 16896.0, -16384.0)):
+    for n, c, s, b in (("a0", A0, -33.0, 32.0), ("a1", A1, 33.0, -1.0), ("a2", vw("cb", 1, 2), -33.0, 32.0), ("a3", vw("cb", 2, 3), 33.0, -1.0)):
         lin(n, c, PAR, s / 1024, b / 1024)
     lin("kc", vw("kc"), vw("kc"), 1.0, T2)
-    lin("k2", vw("k2"), vw("k2"), 1.0, T2)
     ts("kh", vw("kh"), vw("r4"), TCB, A.is_equal, 1024.0, A.mult)
     lin("kd", vw("kd"), vw("kh", 0, C), 1.0, -2.0)
-    for h, (x, y) in enumerate(((A0, C0), (A1, C1))):
-        lin("ta%d" % h, vw("ta", TW * h, TW * h + TW), vw("kh"), x)
-        lin("tb%d" % h, vw("tb", TW * h, TW * h + TW), vw("kh"), y)
-        lin("tm%d" % h, vw("tm", TW * h, TW * h + TW), vw("kh"), 0.5, -64.0)
+    for h in range(2):
+        o, x, y = vw("ta", TW * h, TW * h + TW), (A0, A1)[h], vw("cb", 1 + h, 2 + h)
+        op("ta%d" % h, {"a": lambda o=o, x=x: S.activation(o[0], T.kh[:], F.Identity, scale=x[0]),
+                        "v": lambda o=o, y=y: V.tensor_scalar(o[0], T.kh[:], y[0], None, A.mult)}, [o], [vw("kh"), x, y])
     lin("ari", vw("ga", 0, 176), vw("yf", 0, 176), 8.0, 32768.0 + 160.0)
-    lin("arp", vw("arow", 0, 176), vw("ga", 0, 176), 1.0, -32768.0)
-    lin("arn", vw("arow", 176, 352), vw("ga", 0, 176), -1.0, 32768.0)
+    lin("arp", vw("arow", 0, 176), vw("ga", 0, 176), 1.0 / 512, -64.0)
+    lin("arn", vw("arow", 176, 352), vw("ga", 0, 176), -1.0 / 512, 64.0)
     scan("yd", vw("yf", 176, 352), vw("kd", 0, 176), vw("yf", 0, 176), A.add, A.min)
     ts("gi0", vw("gi", 0, 11), vw("yf", 191, 352, 16), HO, A.add)
     ts("gi1", vw("gi", 12, 23), vw("gi", 0, 11), 31, A.bitwise_and)
@@ -240,17 +238,10 @@ def _calls(g, core, T, topo, rank, helpers):
     mv("cap", vw("cap"), ind(vw("cpt"), vw("gl", 0, 11)))
     lin("sf0", vw("sf", 0, 1), NA, 272.0, W16)
     lin("sf1", vw("sf", 1, 2), NA, -144.0, W16)
-    lin("sf2", vw("sf", 2, 3), NA, 144.0, W16)
     ts("sl0", vw("sl", 0, 1), vw("sf", 0, 1), 15.0, A.add)
     ts("sl1", vw("sl", 2, 3), vw("sf", 1, 2), 687.0, A.add, 799.0, A.min)
-    ts("sl2", vw("sl", 4, 5), vw("sf", 2, 3), -176.0, A.add)
-    ts("sl3", vw("sl", 6, 7), vw("sf", 2, 3), 80.0, A.add, 287.0, A.min)
-    ts("mk0", vw("mk", 0, 8), vw("mk", 0, 8), HC, A.not_equal, -100.0, A.mult)
-    lin("mk1", vw("mk", 8, 16), vw("mk", 0, 8), -1.0, -100.0)
-    lin("sn0", vw("dd", 15, 16), vw("kh", 15, 16), 4.0, -1000.0)
-    lin("sn1", vw("dd", 415, 416), vw("kh", 0, 1), 4.0, -1000.0)
-    lin("c90", vw("c9", 0, 1), PAR, -1.0, 436.0)
-    lin("c91", vw("c9", 1, 2), PAR, 1.0, -45.0)
+    lin("c90", vw("c9", 0, 1), PAR, 1.0, 196.0)
+    lin("c91", vw("c9", 1, 2), PAR, -1.0, 195.0)
     for b in range(4):
         qz("eq%d" % b, vw("eq", 128 * b, 128 * b + 128), vw("es", 128 * b, 128 * b + 128), vw("eb", 3 - b, 515 - b))
     qz("uq", vw("uq"), vw("us"), vw("ub"))
@@ -295,9 +286,9 @@ def _calls(g, core, T, topo, rank, helpers):
 
         for n, (a, e) in enumerate(PIECES):
             mm("ms%d" % n, bank(n, e - a), vw("uq2"), vw("us2"), vw("aq%d" % t, a, e), vw("as%d" % t, a, e))
-        act("ns", vw("ns", 1, 193), bank(0, 192), F.Sign, -1.0, NTINY)
-        for n, (a, e) in enumerate(PIECES):
-            act("sg%d" % n, vw("sg", a, e), bank(n, e - a), F.Sign, 1.0, TINY)
+        act("ns", vw("sg", 1, 193), bank(0, 192), F.Sign, -1.0, NTINY)
+        act("sg0", vw("sg", 194, HALF + 2), bank(0, HALF, 192), F.Sign, 1.0, TINY)
+        act("sg1", vw("sg", HALF + 2, C + 2), bank(1, C - HALF), F.Sign, 1.0, TINY)
         for n, (a, e) in enumerate(PIECES):
             for b in range(4):
                 k = (2 + 4 * n + b) % 8
@@ -310,64 +301,54 @@ def _calls(g, core, T, topo, rank, helpers):
             e = HALF if b % 2 else C
             dma("pp%d" % b, T.pp[:, C * b:C * b + e], plane(b, P0, P0 + e)[0], [vw("pp", C * b, C * b + e)],
                 [plane(b, P0, P0 + e)], "p%d" % b)
-        scan("dl", vw("ev", 0, 193, rev=True), vw("ns", 1, 194, rev=True), vw("ns", 0, 193, rev=True), A.add, A.add, -1.0)
-        scan("dr", vw("ev", 193, 386), vw("sg", 191, C), vw("sg", 192, C + 1), A.add, A.add, vw("ev", 192, 193))
+        scan("dl", vw("ev", 0, 193, rev=True), vw("sg", 1, 194, rev=True), vw("sg", 0, 193, rev=True), A.add, A.add, -1.0)
+        scan("dr", vw("ev", 193, 386), vw("sg", 193, C + 2), vw("sg", 194, C + 3), A.add, A.add, -1.0)
         E0, EE = vw("ev", 0, 1), vw("ev", 385, 386)
-        for n, a, e, i in (("L0", 0, 193, 999.0), ("L1", 193, 385, vw("lr", 192, 193))):
+        for n, a, e, i in (("L0", 0, 193, 999.0), ("L1", 193, 385, vw("lr", 192, 193))) if t else (("L0", 0, 385, 999.0),):
             scan(n, vw("lr", a, e), vw("ev", a, e), vw("ev", a, e), A.min, A.min, i)
         scan("R0", vw("rr", 1, 386, rev=True), vw("ev", 1, 386, rev=True), vw("ev", 1, 386, rev=True), A.min, A.min, 999.0)
-        scan("dd", vw("dd", 16, 400), vw("kd"), vw("ev", 1, 385), A.add, A.min)
-        scan("sd", vw("sd"), vw("kd"), vw("sg", 0, C), A.add, A.min)
-        SR, RAW, HV, OPEN = vw("sd", 15, C, 16), vw("dd", 31, 400, 16), vw("e1", 3, 96, 4), vw("e0", 2, 96, 4)
+        scan("dd", vw("dd"), vw("kd"), vw("ev", 1, 385), A.add, A.min)
+        scan("sd0", vw("sd", 0, 192), vw("kd", 0, 192), vw("sg", 1, 193), A.add, A.min)
+        scan("sd1", vw("sd", 192, C), vw("kd", 0, 192), vw("sg", 194, C + 2), A.add, A.min)
+        RAW, HV, OPEN = vw("dd", 15, C, 16), vw("e1", 3, 96, 4), vw("e0", 2, 96, 4)
         LV, RV = vw("lr", 0, 385, 16), vw("rr", 1, 386, 16)
         ND, AL = vw("al", 1, 2), vw("al", 0, 1)
         lin("nd", ND, E0, -1.0, -1.0)
         lin("th0", vw("th", 0, 4), vw("kc", 0, 4), 1.0, ND)
         lin("th1", vw("th", 4, 8), vw("kc", 4, 8), -1.0, EE)
-        lin("tr0", vw("thr", 0, 64), vw("k2"), 1.0, E0)
-        lin("tr1", vw("thr", 64, 128), vw("k2"), 1.0, EE)
         for i in range(8):
-            count("n%d" % i, vw("n1", i, i + 1), vw("jk", 25 * i, 25 * i + 25), LV if i < 4 else RV, 1.0 if i < 4 else -1.0,
-                  vw("th", i, i + 1))
-        ts("o16", vw("o16"), vw("n1"), 8.0, A.mult, 215.0, A.add)
-        lin("of0", vw("off", 0, 4), vw("n1", 0, 4), -0.5, 13.5)
-        lin("of1", vw("off", 4, 8), vw("n1", 4, 8), 0.5, 14.5)
-        tt("j0", vw("kk", 16, 144, 16), vw("off"), vw("mk", 0, 8), A.add)
-        tt("j1", vw("kk", 160, 288, 16), vw("off"), vw("mk", 8, 16), A.add)
-        tt("cm", vw("c2", 16, 144), ind(vw("dd"), vw("o16")), vw("thr"), A.is_lt)
-        tr("t20", vw("t2", 0, 128), vw("c2", 16, 144))
-        tr("t21", vw("t2", 128, 288), vw("c2"))
-        scan("nn", vw("n2"), vw("kk"), vw("t2"), A.add, A.max)
-        ts("ml0", vw("ml", 0, 16), ind(vw("n2"), vw("sl", 4, 5)), -16.0, A.mult, vw("c9", 0, 1), A.add)
-        ts("ml1", vw("ml", 16, 32), ind(vw("n2"), vw("sl", 6, 7)), 16.0, A.mult, vw("c9", 1, 2), A.add)
-        for b in range(4):
-            mv("mt%d" % b, vw("mt", b, 512, 4), ind(plane(b, 64, DR), vw("ml", 12, 20)))
+            count("n%d" % i, vw("n1", i, i + 1), vw("jk", 192 * i, 192 * i + 192),
+                  vw("lr", 2, 385, 2) if i < 4 else vw("rr", 1, 385, 2), 1.0 if i < 4 else -1.0, vw("th", i, i + 1))
+        for s in range(2):
+            ts("ml%d" % s, vw("ml", 4 * s, 4 * s + 4), vw("n1", 4 * s, 4 * s + 4), vw("c9", s, s + 1), A.add)
+            for b in range(4):
+                mv("mt%d%d" % (s, b), vw("mt", 256 * s + b, 256 * s + 256, 4), ind(plane(b, 64, DR), vw("ml", 4 * s, 4 * s + 4)))
         qz("mq", vw("mq%d" % t), vw("ms%d" % t), vw("mt"))
         send(t, "q", "ha%d")
         send(t, "s", "ha%d")
         op("arr", {}, [vw("lq%d" % t, 64, 192), vw("ls%d" % t, 64, 192)], [(None, [("sent%d" % t, 0, 1, 1)])], "arr%d" % t)
         ts("o1", vw("o1"), RAW, 0.5, A.mult, CO, A.add)
         mv("xa", vw("xa"), ind(vw("ta"), vw("o1")))
-        mv("xc", vw("xc"), ind(vw("tb"), vw("o1")))
-        mv("xm", br(5, 5 + 3 * C, 3), ind(vw("tm"), vw("o1")))
-        scan("ar", vw("ab", 4, 4 + 3 * C, 3), vw("xa"), vw("pos"), A.add, A.min, -512.0)
-        scan("br", br(1, 1 + 3 * C, 3, True), vw("xc", rev=True), vw("pos", rev=True), A.add, A.max, 512.0)
-        BASE = vw("bs", 0, 25)
+        ts("xc", vw("xc"), vw("xa"), 32.0, A.mult, 1.0, A.min)
+        ts("xm", br(5, 5 + 3 * C, 3), vw("xa"), 0.0, A.not_equal, 0.5, A.subtract)
+        scan("ar", vw("ab", 4, 4 + 3 * C, 3), vw("xa"), vw("pos"), A.add, A.min, -1.0)
+        scan("br", br(1, 1 + 3 * C, 3, True), vw("xc", rev=True), vw("pos", rev=True), A.add, A.max, 1.0)
+        BASE = vw("e1", 2, 100, 4)
         tt("base", BASE, LV, RV, A.max)
-        lin("q1", sb(1, 25), vw("ev", 1, 386, 16), 8.0, B1)
-        lin("q2", sb(2, 25), BASE, -8.0, B2)
+        lin("q1", sb(1, 25), vw("ev", 1, 386, 16), 8.0 / 512, B1)
+        lin("q2", sb(2, 25), BASE, -8.0 / 512, B2)
         tt("cc", vw("cc", 0, 25), sb(1, 25), sb(2, 25), A.add)
         tt("kf", vw("key", 0, 25), vw("ab", 1, 1156, 48), vw("cc", 0, 25), A.subtract)
         tt("kb", vw("key", 25, 50), br(1, 1156, 48), vw("cc", 0, 25), A.add)
         tt("ga", vw("ga"), ind(vw("key", 0, 50), vw("gl", 0, 22)), vw("arow"), A.add)
         scan("gf", vw("vt", GF, GF + 176), vw("ga", 0, 176), vw("cap"), A.max, A.min)
-        scan("gr", vw("vt", GF + 176, GF + 352, rev=True), vw("ga", 176, 352, rev=True), vw("cap", rev=True), A.min, A.max, 512.0)
-        lin("open", OPEN, SR, 0.5, BO)
+        scan("gr", vw("vt", GF + 176, GF + 352, rev=True), vw("ga", 176, 352, rev=True), vw("cap", rev=True), A.min, A.max, 1.0)
+        lin("op0", vw("e0", 2, 48, 4), vw("sd", 15, 192, 16), -0.5, C0)
+        lin("op1", vw("e0", 50, 96, 4), vw("sd", 207, C, 16), 0.5, BO)
         lin("hv", HV, RAW, 1.0, HO)
-        lin("b0", vw("e1", 0, 96, 4), vw("bs", 1, 25), 1.0)
-        lin("bn", vw("e1", 1, 96, 4), vw("bs", 0, 24), -1.0)
-        lin("bp", vw("e1", 2, 96, 4), vw("bs", 0, 24), 1.0)
-        scan("de", vw("e2"), vw("e0"), vw("e1"), A.mult, A.add)
+        lin("b0", vw("e1", 0, 96, 4), vw("e1", 6, 100, 4), 1.0)
+        lin("bn", vw("e1", 1, 96, 4), vw("e1", 2, 96, 4), -1.0)
+        scan("de", vw("e2"), vw("e0"), vw("e1", 0, 96), A.mult, A.add)
         DL = vw("e2", 3, 96, 4)
         lin("ab", sb(0, 24), DL, 1.0 / 32, 192.0 - 15.0 / 32)
         act("sq", vw("f0", 2, 96, 4), sb(0, 24), F.Square, 1.0, SQ)
@@ -384,11 +365,11 @@ def _calls(g, core, T, topo, rank, helpers):
         tr("t1a", vw("tt", 0, 256), vw("rb", 50, 816, 3))
         tr("t2a", vw("tt", 256, 544), vw("rb", 2, 864, 3))
         scan("tsa", vw("ts", 0, 544), vw("k16"), vw("tt", 0, 544), A.add, A.max)
-        ts("ola", vw("ol", 0, 16), ind(vw("ts", 0, 544), vw("sl", 0, 1)), 2.0, A.mult, PN, A.add)
+        ts("ola", vw("ol", 0, 16), ind(vw("ts", 0, 544), vw("sl", 0, 1)), 1024.0, A.mult, PN, A.add)
         tr("t2b", vw("tt", 544, 672), vw("rb", 866, 1248, 3))
         tr("t1b", vw("tt", 672, 800), vw("rb", 818, 1200, 3))
         scan("tsb", vw("ts", 544, 800), vw("k16", 0, 256), vw("tt", 544, 800), A.add, A.max)
-        ts("olb", vw("ol", 16, 32), ind(vw("ts"), vw("sl", 2, 3)), 2.0, A.mult, PN, A.add)
+        ts("olb", vw("ol", 16, 32), ind(vw("ts"), vw("sl", 2, 3)), 1024.0, A.mult, PN, A.add)
         for b in range(4):
             mm("mu%d" % b, bank(2 + b, 128), vw("eq", 128 * b, 128 * b + 128), vw("es", 128 * b, 128 * b + 128),
                vw("lq%d" % t, 64, 192), vw("ls%d" % t, 64, 192))

import math
from concourse.bass import DstId, RemoteDMATransfer
from concourse.mybir import dt, AluOpType as A, ActivationFunctionType as F

C, TM, ROUNDS = 384, 64, 2
ZW = 528
P0, DR = 68, 454
GF = 784
TW = 416
BR = 1200
NEAR, FAR = 8, 8
HALF = 256
PIECES = ((0, HALF), (HALF, C))
X4, U8, BF, F32, I32, U16 = "float8_e4m3fn_x4", "uint8", "bfloat16", "float32", "int32", "uint16"
SCRATCH = {"ps": ("psum", [128, 512 * 8], F32)}
for _d, _s in ((X4, "aq0 384 aq1 384 aq2 384 uq 128 uq2 128 vq 128 wq 512 eq 512 mq0 128 mq1 128 hq0 64 hq1 64 lq0 256 lq1 256"),
               (U8, "as0 384 as1 384 as2 384 us 128 us2 128 vs 128 wsc 512 es 512 ms0 128 ms1 128 hs0 64 hs1 64 ls0 256 ls1 256"),
               (BF, "xb 1536 ub 512 vb 512 eb 528 zz 4224 xt 1536 mt 512 pp 1536 da 512 db 512 zero 528 cb 4 r4 416 kh 416 kd 384 "
                    "k16 544 ta 832 cap 176 cpt 32 arow 352 pos 384 sg 400 ev 400 lr 400 rr 400 sd 384 "
                    "dd 384 jk 1536 sb 128 xa 384 xc 384 ab 2368 ga 352 vt 1136 rb 1248 tt 800 ts 800"),
               (F32, "yb 384 cf 24 c9 2 kc 8 sf 4 th 8 n1 8 sm 24 al 2 cc 32 key 56 e0 96 e1 104 e2 96 f0 96 f1 96 f2 96 yf 352"),
               (I32, "ci 16 upi 8 gi 24"), (U16, "upl 8 gl 24 sl 4 ml 8 o1 24 og 24 ol 32")):
    _w = _s.split()
    for _i in range(0, len(_w), 2):
        SCRATCH[_w[_i]] = ("sbuf", [128, int(_w[_i + 1])], _d)
DMAS = ["lxa", "lxb", "lu", "lw", "ls", "lv", "p0", "p1", "p2", "p3"]
SEMAPHORES = ["nv", "na", "nt", "ng", "st", "sent", "ha0", "ha1", "arr0", "arr1"] + DMAS
PLAN = """
zero:v ci:g c2:v c1:v c3:v upi:g r4:g zq0:v f17:a cpt:g upl:v cf:v lu:y f7:a kc0:g pos:g f23:a zz65:a f14:v zz64:a zz452:a coa:a zz66:g zz453:a f12:v a3:a f18:g a2:a cb:v nb:g c91:v na:v yf2:g f9:a t2c:a a1:a a0:a uq:v yf3:g b1a:v c90:a b2:a us2:a f8:a f15:a f11:v yf6:g u1:a uq2:v kc:a lxa:y b1:a vt0:g xqa:v lxb:y co:a bo:a kh:v ls:y lw:y 0.ms0:t f10:a zz67:a f6:a bo0:a w16:a zz0:a xqb:v f13:v kd:v 0.ms1:t yf9:g f1:g ta1:v u0:v 0.mp01:t yf12:g 0.ns:a 0.sg0:a 0.dl:v 0.sd0:v 0.mp00:t yf1:g 0.sg1:a 0.dr:v yf10:g ta0:a 0.mp11:t 0.nd:v 0.mp03:t 0.sd1:v yf0:g 0.lay01:a 0.L0:v yf4:g 0.mp13:t 0.th1:a 0.th0:a 0.mp12:t 0.lay00:a 0.dd:v 0.n1:a 0.n3:a 0.R0:v 0.n7:a 0.n4:a 0.lay11:v 0.n0:a 0.n2:a 0.o1:v 0.lay03:v 0.xa:v 0.lay13:v 0.mp02:t 0.n5:a eb:g 0.mp10:t 0.n6:a sf0:a yf5:g 0.lay12:a yf11:g yf7:g 0.lay10:v 0.ml0:v 0.lay02:v 0.mt00:a 0.mt01:a 0.base:v 0.ml1:v 0.mt03:v 0.mt11:a 0.mt02:v 0.mt10:a 0.mt12:v 0.mt13:v ho:a 0.xc:v 0.op0:a 0.al:a 0.q1:a yf8:g 0.op1:a 0.b0:a 0.mq:v yd:v 0.br:v gi0:v 0.bn:a 0.q2:a u2:a ari:a 0.ar:v 0.hv:a gi1:v 0.es:a pn:a vt1:g 0.cc:v 0.de:v f0:g 0.ow:a arn:a f20:a gl0:v 0.kf:v arp:a 0.ab:a 0.sendq:g 0.sends:g gl1:v f4:g 0.rp:a 0.pp2:y f22:a 0.kb:v sf1:a lv:y 0.sq:a eq2:v 0.v2:v f2:g cap:a 0.ga:v 0.ogs:v f16:a 0.xm:v 0.gf:v f3:g u3:a 0.og:v f5:a f19:a 0.gr:v 0.pp0:y 0.lk0:a eq0:v 0.lk1:v eq1:v sl1:v 0.pp3:y 0.arr:- 0.lk2:a 0.rb1:v 0.mu0:t 0.rb0:v 0.ul0:a 0.ur0:a eq3:v 0.mu3:t 0.rb2:v 0.mu1:t 0.ur1:a 0.pp1:y 0.t2a:v 0.t1a:v 0.t2b:v 0.mu2:t 0.t1b:v sl0:v 0.tsa:v 0.ur3:a 0.ul1:a 0.ul3:a f21:a 0.lb3:a 0.tsb:v 0.ola:v 0.olb:v 0.ul2:a 0.ur2:a 0.x00:v 0.x03:v 0.x01:v 0.x02:v 0.xg3:a 0.xg1:a 0.lb1:a 0.xs:v 0.aq0:v 1.ms0:t 0.x12:v 1.mp02:t 1.mp01:t 1.ns:a 0.x10:v 0.aq1:v 1.ms1:t 1.sg0:a 1.lay02:a 1.mp10:t 1.sg1:a vq:v zq1:v 1.dl:v 1.sd0:v 1.nd:v 1.L0:v 1.mp12:t 1.mp03:t 1.op0:v 1.dr:v 1.sd1:v 1.L1:v 1.lay01:a 1.lay12:a 1.R0:v 1.lay10:a 1.dd:v 1.th0:a 1.th1:a 1.lay03:v 1.q1:a 1.op1:a 1.mp13:t 1.lay13:a 1.pp3:y 1.o1:v 1.mp00:t 1.lay00:v 1.mp11:t 1.xa:v 1.base:v 1.n2:a 1.n5:a 1.n6:a 1.n7:a 1.n4:a 1.ml1:v 1.n3:a 1.n1:a 1.lay11:v 1.xc:v 1.mt12:v 1.n0:a 1.ml0:v 1.q2:a 1.mt10:a 1.br:v 1.mt11:a 1.mt13:a 1.cc:v 1.mt00:a 1.mt03:v 1.mt01:v 1.mt02:a 1.ar:v 1.al:a 1.kb:v 1.mq:v 1.b0:a 1.hv:a 1.kf:v 1.bn:a 1.de:v 1.sendq:g 1.sends:g 1.es:a 1.pp2:y 1.lb1:a 1.v2:v 1.ab:a 1.pp1:y 1.arr:- 1.ow:a 1.ga:v 1.rp:a 1.sq:a 1.ogs:v 1.gf:v 1.gr:v 1.og:v 1.xm:v 1.lk1:v 1.mu0:t 1.lk0:a 1.lk2:a 1.rb1:v 1.ul0:a 1.rb0:v 1.ur0:a 1.rb2:v 1.mu3:t 1.mu1:t 1.t2a:v 1.t1a:v 1.pp0:y 1.lb3:a 1.t1b:v 1.mu2:t 1.t2b:v 1.tsa:v 1.ur1:a 1.ur3:a 1.tsb:v 1.ola:v 1.ul3:a 1.ur2:a 1.olb:v 1.ul1:a 1.ul2:a 1.x00:v 1.xg3:a 1.x03:v 1.x01:v 1.x02:v 1.xg1:a 1.xs:v 1.aq0:v 1.x12:v 1.x10:v 1.oc0:y 1.aq1:v 1.my0:t 1.yb0:v 1.osc2:a 1.my1:t 1.yb1:v 1.oc1:y 1.y0:y 1.osc3:y 1.osc0:y 1.osc1:a 1.y1:a
"""


def _bits(es):
    m = 0
    for e in es:
        m |= 1 << e
    return m


def _helpers(T, topo):
    out = {}
    for r, c in enumerate(T.cores):
        used = []
        for side, n in ((0, r - 1), (1, r + 1), (2, r - 1), (3, r + 1)):
            if 0 <= n < len(T.cores):
                ok = [h for h in topo.cores_of(c) if T.rank_of(h) is None and h not in used and topo.may_write(h, T.cores[n])]
                ok.sort(key=lambda h: topo.die(h) != topo.die(c))
                used.append(ok[0])
                out[(r, side)] = ok[0]
    return out


def _helper_program(g, core, T, topo, rank, side):
    dst = T.cores[rank - 1 + 2 * (side % 2)]
    rid, pid = topo.addr(dst, core)
    m = _bits(topo.engines(core, dst)[:FAR])
    lo = 128 - TM * (side % 2)
    for t in range(ROUNDS):
        g.wait_ge(T.sem["ha%d" % t], NEAR)
        if side < 2:
            g.remote_dma(T["lq%d" % t][:, lo:lo + TM].bitcast(dt.uint8), T["hq%d" % t][:].bitcast(dt.uint8),
                         T.sem["arr%d" % t], T.sem.sent, pid, rid, m)
        else:
            g.remote_dma(T["ls%d" % t][:, lo:lo + TM], T["hs%d" % t][:], T.sem["arr%d" % t], T.sem.sent, pid, rid, m)
    g.wait_ge(T.sem.sent, ROUNDS * FAR)


def _meet(u, v):
    return u[0] == v[0] and u[1] < v[2] and v[1] < u[2] and not (u[1] - v[1]) % math.gcd(u[3], v[3])


def _calls(g, core, T, topo, rank, helpers):
    N = len(T.cores)
    ops = []
    tag = [""]
    V, S = g.vector, g.scalar

    def vw(name, a=0, b=None, s=1, rev=False):
        t = T[name]
        if b is None:
            b = t.shape[1]
        if rev:
            e = a + (b - 1 - a) // s * s
            p = t[:, e::-s] if a < s else t[:, e:a - 1:-s]
        else:
            p = t[:, a:b:s] if s != 1 else t[:, a:b]
        if name == "ps":
            return (p, [(name, a // 512 * 512, (b + 511) // 512 * 512, 1)])
        return (p, [(name, a, b, s)])

    def ind(w, o):
        return (w[0].indirect(o[0]), w[1] + o[1])

    def op(name, fns, outs, ins, sem=None):
        cols = [[c for v in vs if isinstance(v, tuple) for c in v[1]] for vs in (outs, ins)]
        ops.append((tag[0] + name, fns, cols[0], cols[1], sem))

    def ap(x):
        return x[0] if isinstance(x, tuple) else x

    def ts(n, o, i, s1, op0, s2=None, op1=None):
        if op1 is None:
            op(n, {"v": lambda: V.tensor_scalar(o[0], i[0], ap(s1), None, op0)}, [o], [i, s1])
        else:
            op(n, {"v": lambda: V.tensor_scalar(o[0], i[0], ap(s1), ap(s2), op0, op1)}, [o], [i, s1, s2])

    def tt(n, o, a, b, f):
        op(n, {"v": lambda: V.tensor_tensor(o[0], a[0], b[0], f)}, [o], [a, b])

    def cp(n, o, i):
        op(n, {"v": lambda: V.tensor_copy(o[0], i[0])}, [o], [i])

    def mv(n, o, i):
        op(n, {"a": lambda: S.activation(o[0], i[0], F.Copy), "v": lambda: V.tensor_copy(o[0], i[0])}, [o], [i])

    def lin(n, o, i, scale, bias=0.0):
        op(n, {"a": lambda: S.activation(o[0], i[0], F.Identity, bias=ap(bias), scale=ap(scale)),
               "v": lambda: V.tensor_scalar(o[0], i[0], ap(scale), ap(bias), A.mult, A.add)}, [o], [i, scale, bias])

    def fill(n, o, c, k):
        fns = {"v": lambda: V.memset(o[0], c)}
        if n != "zero" and 1 < k <= 528:
            fns["a"] = lambda: S.activation(o[0], T.zero[:, 0:k], F.Identity, bias=c, scale=1.0)
        if c == int(c) and abs(c) < 1e7:
            fns["g"] = lambda: g.iota(o[0], [[0, k]], int(c), 0, allow_small_or_imprecise_dtypes=True)
        op(n, fns, [o], [] if n == "zero" else [vw("zero")])

    def scan(n, o, d0, d1, op0, op1, init=0.0):
        op(n, {"v": lambda: V.tensor_tensor_scan(o[0], d0[0], d1[0], ap(init), op0, op1)}, [o], [d0, d1, init])

    def tr(n, o, i):
        op(n, {"v": lambda: V.transpose(o[0], i[0])}, [o], [i])

    def qz(n, o, s, i):
        op(n, {"v": lambda: V.quantize_mx(o[0], s[0], i[0])}, [o, s], [i])

    def act(n, o, i, f, scale, bias):
        op(n, {"a": lambda: S.activation(o[0], i[0], f, bias=ap(bias), scale=ap(scale))}, [o], [i, scale, bias])

    def count(n, o, signs, i, scale, bias):
        op(n, {"a": lambda: S.activation(signs[0], i[0], F.Sign, bias=bias[0], scale=scale, accum_out=o[0])},
           [o, signs], [i, bias])

    def mm(n, o, l, ls, r, rs):
        op(n, {"t": lambda: g.tensor.matmul_mx(o[0], l[0], ls[0], r[0], rs[0], True, True)}, [o], [l, ls, r, rs])

    def iota(n, o, pat, base=0, cm=0, whole=False):
        if whole:
            op(n, {"g": lambda: g.iota(o[0], pat, base, cm)}, [o], [])
        else:
            op(n, {"g": lambda: g.iota(o[0], pat, base, cm, allow_small_or_imprecise_dtypes=True)}, [o], [])

    def dma(n, o, i, outs, ins, sem):
        op(n, {"y": lambda: g.sync.dma_start(o, i), "a": lambda: S.dma_start(o, i)}, outs, ins, sem)

    dma("lu", T.ub[:], T.u[:], [vw("ub")], [], "lu")
    for n, (a, e) in zip("ab", PIECES):
        dma("lx" + n, T.xb[:, 4 * a:4 * e], T.x[:, 4 * a:4 * e], [vw("xb", 4 * a, 4 * e)], [], "lx" + n)
    dma("lw", T.wq[:].bitcast(dt.uint8), T.wc[:], [vw("wq")], [], "lw")
    dma("ls", T.wsc[:], T.ws[:], [vw("wsc")], [], "ls")
    dma("lv", T.vb[:], T.v[:], [vw("vb")], [], "lv")

    def col(i):
        return vw("cf", i, i + 1)
    TC, HC, PAR, PN, NA, BO, HO, B1, B2, W16, TINY, NTINY, SQ, CO, A0, A1, C0, T2, GB, GC = [col(i) for i in range(20)]
    TCB = vw("cb", 0, 1)
    fill("zero", vw("zero"), 0.0, 528)
    iota("ci", vw("ci", 0, 1), [[0, 1]], 0, 1, True)
    iota("upi", vw("upi"), [[16, 8]], 0, 0, True)
    iota("r4", vw("r4"), [[0, 26], [1, 16]])
    iota("kc0", vw("kc"), [[-1, 2], [32, 4]], 2)
    at = 0
    for a in range(13):
        k = 25 - 2 * a if a < 12 else 176 - at
        iota("yf%d" % a, vw("yf", at, at + k), [[1 if a < 12 else 0, k]], 33 * a if a < 12 else 13 * 32)
        at += k
    iota("cpt", vw("cpt"), [[8, 32]], 1)
    iota("nb", vw("f1", 0, 96, 4), [[-1, 24]])
    iota("pos", vw("pos"), [[1, 192], [0, 2]], P0 // 2 - 32)
    op("eb", {"g": lambda: g.affine_select(T.eb[:], T.zero[:, 0:528], [[-1, 528]], A.not_equal, 1.0, 3, 4)},
       [vw("eb")], [vw("zero")])
    for n, (name, a, e, s, c) in enumerate((
            ("ab", 1, 2, 1, -1.0), ("ab", BR + 1153, BR + 1154, 1, 1.0), ("k16", 0, 544, 1, 0.0), ("k16", 0, 544, 16, -4.0),
            ("ab", 0, 1152, 3, 2.0), ("ab", 2, 1152, 3, -2.0),
            ("e0", 0, 96, 4, 0.0), ("e0", 1, 96, 4, 1.0), ("e0", 3, 96, 4, -1.0),
            ("f0", 0, 96, 4, -1e6), ("f0", 3, 96, 4, 0.0), ("f1", 1, 96, 4, -1e6),
            ("cf", 10, 11, 1, 1e-37), ("cf", 11, 12, 1, -1e-37), ("cf", 12, 13, 1, -204.5),
            ("rb", 0, 48, 1, 0.0), ("rb", 1200, 1248, 1, 0.0),
            ("sg", 0, 387, 386, 1.0), ("sg", 193, 194, 1, 0.0), ("da", 0, 256, 2, 1e29),
            ("da", 256, 512, 2, 1e29), ("db", 1, 512, 2, 1e29), ("vt", 132, GF, 2, 1.0 / 512), ("vt", 129, GF, 2, 194.0 / 512))):
        fill("f%d" % n, vw(name, a, e, s), c, len(range(a, e, s)))
    for c in (0, 64, 65, 66, 67, P0 + C, P0 + C + 1):
        fill("zz%d" % c, vw("zz", c, 4 * ROUNDS * ZW, ZW), 0.0, 4 * ROUNDS)
    iota("vt0", vw("vt", 0, 132, 2), [[1, 33], [0, 2]], -32)
    iota("vt1", vw("vt", 1, 128, 2), [[1, 32], [0, 2]], 195)
    for n, x in (("u0", vw("pos")), ("u1", vw("cpt")), ("u2", vw("vt", 0, 132, 2)), ("u3", vw("vt", 1, 128, 2))):
        lin(n, x, x, 1.0 / 512)

    ts("c1", vw("ci", 1, 2), vw("ci", 0, 1), 15, A.bitwise_and)
    ts("c2", vw("ci", 2, 3), vw("ci", 0, 1), 4, A.logical_shift_right, 1, A.bitwise_and)
    ts("c3", vw("ci", 3, 4), vw("ci", 0, 1), 1, A.bitwise_and)
    cp("upl", vw("upl"), vw("upi"))
    cp("cf", vw("cf", 0, 3), vw("ci", 1, 4))
    cp("cb", TCB, vw("ci", 1, 2))
    if rank == 0 or rank == N - 1:
        lo = 0 if rank == 0 else 128
        for t in range(ROUNDS):
            qz("zq%d" % t, vw("lq%d" % t, lo, lo + 128), vw("ls%d" % t, lo, lo + 128), vw("zero", 0, 512))
    lin("pn", PN, PAR, -1.0, 65.0)
    ts("na", NA, PAR, HC, A.not_equal)
    lin("bo", BO, TC, -1.0, 15.5)
    lin("bo0", C0, TC, 1.0, -14.5)
    lin("ho", HO, TC, -2.0, 30.0)
    lin("t2c", T2, TC, 2.0)
    lin("b2", B2, TC, 16.0 / 512, -96.0 - 120.0 / 512)
    lin("b1a", GB, PAR, 16.0 / 512)
    lin("b1", B1, B2, -1.0, GB)
    lin("w16", W16, TC, 16.0)
    lin("coa", GC, TC, -1.0, 223.0)
    lin("co", CO, PAR, float(TW), GC)
    for n, c, s, b in (("a0", A0, -33.0, 32.0), ("a1", A1, 33.0, -1.0), ("a2", vw("cb", 1, 2), -33.0, 32.0), ("a3", vw("cb", 2, 3), 33.0, -1.0)):
        lin(n, c, PAR, s / 1024, b / 1024)
    lin("kc", vw("kc"), vw("kc"), 1.0, T2)
    ts("kh", vw("kh"), vw("r4"), TCB, A.is_equal, 1024.0, A.mult)
    lin("kd", vw("kd"), vw("kh", 0, C), 1.0, -2.0)
    for h in range(2):
        o, x, y = vw("ta", TW * h, TW * h + TW), (A0, A1)[h], vw("cb", 1 + h, 2 + h)
        op("ta%d" % h, {"a": lambda o=o, x=x: S.activation(o[0], T.kh[:], F.Identity, scale=x[0]),
                        "v": lambda o=o, y=y: V.tensor_scalar(o[0], T.kh[:], y[0], None, A.mult)}, [o], [vw("kh"), x, y])
    lin("ari", vw("ga", 0, 176), vw("yf", 0, 176), 8.0, 32768.0 + 160.0)
    lin("arp", vw("arow", 0, 176), vw("ga", 0, 176), 1.0 / 512, -64.0)
    lin("arn", vw("arow", 176, 352), vw("ga", 0, 176), -1.0 / 512, 64.0)
    scan("yd", vw("yf", 176, 352), vw("kd", 0, 176), vw("yf", 0, 176), A.add, A.min)
    ts("gi0", vw("gi", 0, 11), vw("yf", 191, 352, 16), HO, A.add)
    ts("gi1", vw("gi", 12, 23), vw("gi", 0, 11), 31, A.bitwise_and)
    cp("gl0", vw("gl", 0, 11), vw("gi", 12, 23))
    ts("gl1", vw("gl", 11, 22), vw("gi", 12, 23), 25.0, A.add)
    mv("cap", vw("cap"), ind(vw("cpt"), vw("gl", 0, 11)))
    lin("sf0", vw("sf", 0, 1), NA, 272.0, W16)
    lin("sf1", vw("sf", 1, 2), NA, -144.0, W16)
    ts("sl0", vw("sl", 0, 1), vw("sf", 0, 1), 15.0, A.add)
    ts("sl1", vw("sl", 2, 3), vw("sf", 1, 2), 687.0, A.add, 799.0, A.min)
    lin("c90", vw("c9", 0, 1), PAR, 1.0, 196.0)
    lin("c91", vw("c9", 1, 2), PAR, -1.0, 195.0)
    for b in range(4):
        qz("eq%d" % b, vw("eq", 128 * b, 128 * b + 128), vw("es", 128 * b, 128 * b + 128), vw("eb", 3 - b, 515 - b))
    qz("uq", vw("uq"), vw("us"), vw("ub"))
    op("uq2", {"v": lambda: V.tensor_copy(T.uq2[:, 0:128].bitcast(dt.uint32),
                                          T.uq[:, 0:128].bitcast(dt.uint32).indirect(T.upl[:, 0:8]))},
       [vw("uq2")], [vw("uq"), vw("upl")])
    mv("us2", vw("us2", 0, 128), ind(vw("us", 0, 128), vw("upl", 0, 8)))
    qz("vq", vw("vq"), vw("vs"), vw("vb"))
    for n, (a, e) in zip("ab", PIECES):
        qz("xq" + n, vw("aq0", a, e), vw("as0", a, e), vw("xb", 4 * a, 4 * e))

    sides = [s for s in (0, 1) if (rank, s) in helpers]

    def send(t, kind, sem):
        xs = []
        for s in sides:
            h = helpers[(rank, s if kind == "q" else s + 2)]
            rid, pid = topo.addr(h, core)
            es = topo.engines(core, h)
            src, dst = T["m%s%d" % (kind, t)][:, TM * s:TM * s + TM], T["h%s%d" % (kind, t)][:]
            if kind == "q":
                src, dst = src.bitcast(dt.uint8), dst.bitcast(dt.uint8)
            xs.append(RemoteDMATransfer(dst_ids=[DstId(rid=rid, pnc=pid)], dma_engine_mask=_bits(es[NEAR * s:NEAR * s + NEAR]),
                                        remote_sem=T.sem[sem % t], src=src, dst=dst))
        op("send" + kind, {"g": lambda: g.remote_dma_fused(xs, local_sem=T.sem.sent)}, [(None, [("sent%d" % t, 0, 1, 1)])],
           [vw("m%s%d" % (kind, t))], "sent")

    def sb(i, n):
        return vw("sb", 32 * i, 32 * i + n)

    def bank(b, n, a=0):
        return vw("ps", 512 * b + a, 512 * b + n)

    def br(a, e, s=1, rev=False):
        return vw("ab", BR + a, BR + e, s, rev)

    for t in range(ROUNDS):
        tag[0] = "%d." % t

        def plane(b, a, e, t=t):
            return vw("zz", ZW * (4 * t + b) + a, ZW * (4 * t + b) + e)

        for n, (a, e) in enumerate(PIECES):
            mm("ms%d" % n, bank(n, e - a), vw("uq2"), vw("us2"), vw("aq%d" % t, a, e), vw("as%d" % t, a, e))
        act("ns", vw("sg", 1, 193), bank(0, 192), F.Sign, -1.0, NTINY)
        act("sg0", vw("sg", 194, HALF + 2), bank(0, HALF, 192), F.Sign, 1.0, TINY)
        act("sg1", vw("sg", HALF + 2, C + 2), bank(1, C - HALF), F.Sign, 1.0, TINY)
        for n, (a, e) in enumerate(PIECES):
            for b in range(4):
                k = (2 + 4 * n + b) % 8
                mm("mp%d%d" % (n, b), bank(k, e - a), vw("wq", 128 * b, 128 * b + 128), vw("wsc", 128 * b, 128 * b + 128),
                   vw("aq%d" % t, a, e), vw("as%d" % t, a, e))
                lin("lay%d%d" % (n, b), plane(b, P0 + a, P0 + e), bank(k, e - a), 0.0625)
                if n and b % 2:
                    lin("lb%d" % b, vw("db", b - 1, 512, 4), bank(k, e - a), 0.0625)
        for b in range(4):
            e = HALF if b % 2 else C
            dma("pp%d" % b, T.pp[:, C * b:C * b + e], plane(b, P0, P0 + e)[0], [vw("pp", C * b, C * b + e)],
                [plane(b, P0, P0 + e)], "p%d" % b)
        scan("dl", vw("ev", 0, 193, rev=True), vw("sg", 1, 194, rev=True), vw("sg", 0, 193, rev=True), A.add, A.add, -1.0)
        scan("dr", vw("ev", 193, 386), vw("sg", 193, C + 2), vw("sg", 194, C + 3), A.add, A.add, -1.0)
        E0, EE = vw("ev", 0, 1), vw("ev", 385, 386)
        for n, a, e, i in (("L0", 0, 193, 999.0), ("L1", 193, 385, vw("lr", 192, 193))) if t else (("L0", 0, 385, 999.0),):
            scan(n, vw("lr", a, e), vw("ev", a, e), vw("ev", a, e), A.min, A.min, i)
        scan("R0", vw("rr", 1, 386, rev=True), vw("ev", 1, 386, rev=True), vw("ev", 1, 386, rev=True), A.min, A.min, 999.0)
        scan("dd", vw("dd"), vw("kd"), vw("ev", 1, 385), A.add, A.min)
        scan("sd0", vw("sd", 0, 192), vw("kd", 0, 192), vw("sg", 1, 193), A.add, A.min)
        scan("sd1", vw("sd", 192, C), vw("kd", 0, 192), vw("sg", 194, C + 2), A.add, A.min)
        RAW, HV, OPEN = vw("dd", 15, C, 16), vw("e1", 3, 96, 4), vw("e0", 2, 96, 4)
        LV, RV = vw("lr", 0, 385, 16), vw("rr", 1, 386, 16)
        ND, AL = vw("al", 1, 2), vw("al", 0, 1)
        lin("nd", ND, E0, -1.0, -1.0)
        lin("th0", vw("th", 0, 4), vw("kc", 0, 4), 1.0, ND)
        lin("th1", vw("th", 4, 8), vw("kc", 4, 8), -1.0, EE)
        for i in range(8):
            count("n%d" % i, vw("n1", i, i + 1), vw("jk", 192 * i, 192 * i + 192),
                  vw("lr", 2, 385, 2) if i < 4 else vw("rr", 1, 385, 2), 1.0 if i < 4 else -1.0, vw("th", i, i + 1))
        for s in range(2):
            ts("ml%d" % s, vw("ml", 4 * s, 4 * s + 4), vw("n1", 4 * s, 4 * s + 4), vw("c9", s, s + 1), A.add)
            for b in range(4):
                mv("mt%d%d" % (s, b), vw("mt", 256 * s + b, 256 * s + 256, 4), ind(plane(b, 64, DR), vw("ml", 4 * s, 4 * s + 4)))
        qz("mq", vw("mq%d" % t), vw("ms%d" % t), vw("mt"))
        send(t, "q", "ha%d")
        send(t, "s", "ha%d")
        op("arr", {}, [vw("lq%d" % t, 64, 192), vw("ls%d" % t, 64, 192)], [(None, [("sent%d" % t, 0, 1, 1)])], "arr%d" % t)
        ts("o1", vw("o1"), RAW, 0.5, A.mult, CO, A.add)
        mv("xa", vw("xa"), ind(vw("ta"), vw("o1")))
        ts("xc", vw("xc"), vw("xa"), 32.0, A.mult, 1.0, A.min)
        ts("xm", br(5, 5 + 3 * C, 3), vw("xa"), 0.0, A.not_equal, 0.5, A.subtract)
        scan("ar", vw("ab", 4, 4 + 3 * C, 3), vw("xa"), vw("pos"), A.add, A.min, -1.0)
        scan("br", br(1, 1 + 3 * C, 3, True), vw("xc", rev=True), vw("pos", rev=True), A.add, A.max, 1.0)
        BASE = vw("e1", 2, 100, 4)
        tt("base", BASE, LV, RV, A.max)
        lin("q1", sb(1, 25), vw("ev", 1, 386, 16), 8.0 / 512, B1)
        lin("q2", sb(2, 25), BASE, -8.0 / 512, B2)
        tt("cc", vw("cc", 0, 25), sb(1, 25), sb(2, 25), A.add)
        tt("kf", vw("key", 0, 25), vw("ab", 1, 1156, 48), vw("cc", 0, 25), A.subtract)
        tt("kb", vw("key", 25, 50), br(1, 1156, 48), vw("cc", 0, 25), A.add)
        tt("ga", vw("ga"), ind(vw("key", 0, 50), vw("gl", 0, 22)), vw("arow"), A.add)
        scan("gf", vw("vt", GF, GF + 176), vw("ga", 0, 176), vw("cap"), A.max, A.min)
        scan("gr", vw("vt", GF + 176, GF + 352, rev=True), vw("ga", 176, 352, rev=True), vw("cap", rev=True), A.min, A.max, 1.0)
        lin("op0", vw("e0", 2, 48, 4), vw("sd", 15, 192, 16), -0.5, C0)
        lin("op1", vw("e0", 50, 96, 4), vw("sd", 207, C, 16), 0.5, BO)
        lin("hv", HV, RAW, 1.0, HO)
        lin("b0", vw("e1", 0, 96, 4), vw("e1", 6, 100, 4), 1.0)
        lin("bn", vw("e1", 1, 96, 4), vw("e1", 2, 96, 4), -1.0)
        scan("de", vw("e2"), vw("e0"), vw("e1", 0, 96), A.mult, A.add)
        DL = vw("e2", 3, 96, 4)
        lin("ab", sb(0, 24), DL, 1.0 / 32, 192.0 - 15.0 / 32)
        act("sq", vw("f0", 2, 96, 4), sb(0, 24), F.Square, 1.0, SQ)
        lin("rp", vw("f1", 2, 96, 4), DL, -1e5, -2.5e4)
        lin("ow", vw("f0", 1, 96, 4), OPEN, 177.0, GF + 156.25)
        lin("al", AL, EE, 1.0, ND)
        act("es", vw("sm"), OPEN, F.Identity, AL, E0)
        tt("v2", vw("f1", 3, 96, 4), vw("sm"), HV, A.subtract)
        scan("ogs", vw("f2"), vw("f0"), vw("f1"), A.subtract, A.max)
        cp("og", vw("og"), vw("f2", 3, 96, 4))
        for n, (a, e) in enumerate(((0, 160), (160, 288), (288, C))):
            mv("lk%d" % n, br(3 + 3 * a, 3 + 3 * e, 3), ind(vw("vt"), vw("og", a // 16, e // 16)))
            scan("rb%d" % n, vw("rb", 48 + 3 * a, 48 + 3 * e), vw("ab", 3 * a, 3 * e), br(3 + 3 * a, 3 + 3 * e), A.max, A.min)
        tr("t1a", vw("tt", 0, 256), vw("rb", 50, 816, 3))
        tr("t2a", vw("tt", 256, 544), vw("rb", 2, 864, 3))
        scan("tsa", vw("ts", 0, 544), vw("k16"), vw("tt", 0, 544), A.add, A.max)
        ts("ola", vw("ol", 0, 16), ind(vw("ts", 0, 544), vw("sl", 0, 1)), 1024.0, A.mult, PN, A.add)
        tr("t2b", vw("tt", 544, 672), vw("rb", 866, 1248, 3))
        tr("t1b", vw("tt", 672, 800), vw("rb", 818, 1200, 3))
        scan("tsb", vw("ts", 544, 800), vw("k16", 0, 256), vw("tt", 544, 800), A.add, A.max)
        ts("olb", vw("ol", 16, 32), ind(vw("ts"), vw("sl", 2, 3)), 1024.0, A.mult, PN, A.add)
        for b in range(4):
            mm("mu%d" % b, bank(2 + b, 128), vw("eq", 128 * b, 128 * b + 128), vw("es", 128 * b, 128 * b + 128),
               vw("lq%d" % t, 64, 192), vw("ls%d" % t, 64, 192))
            mv("ul%d" % b, plane(b, 1, 65), bank(2 + b, 64))
            mv("ur%d" % b, plane(b, DR, DR + TM), bank(2 + b, 128, 64))
        aq, asc = "aq%d" % (t + 1), "as%d" % (t + 1)
        for n, (a, e) in enumerate(PIECES):
            if n:
                for b in (1, 3):
                    mv("xg%d" % b, vw("da", b, 512, 4), ind(plane(b, 0, DR + TM), vw("ol", a // 16, e // 16)))
                scan("xs", vw("xt", 4 * a, 4 * e), vw("da"), vw("db"), A.add, A.min)
            for b in ((0, 2) if n else range(4)):
                tt("x%d%d" % (n, b), vw("xt", 4 * a + b, 4 * e, 4), ind(plane(b, 0, DR + TM), vw("ol", a // 16, e // 16)),
                   vw("pp", C * b + a, C * b + e), A.add)
            qz("aq%d" % n, vw(aq, a, e), vw(asc, a, e), vw("xt", 4 * a, 4 * e))
            if t == ROUNDS - 1:
                mm("my%d" % n, bank(n, e - a), vw("vq"), vw("vs"), vw(aq, a, e), vw(asc, a, e))
                dma("oc%d" % n, T.oc[:, 4 * a:4 * e], T[aq][:, a:e].bitcast(dt.uint8), [], [vw(aq, a, e)], "st")
                mv("yb%d" % n, vw("yb", a, e), bank(n, e - a))
                dma("y%d" % n, T.y[:, a:e], T.yb[:, a:e], [], [vw("yb", a, e)], "st")
    for k in range(4):
        dma("osc%d" % k, T.osc[4 * k:4 * k + 4, :], T[asc][32 * k:32 * k + 4, :], [], [vw(asc)], "st")
    return ops, len(sides)


def rank_program(g, core, T, topo):
    rank = T.rank_of(core)
    helpers = _helpers(T, topo)
    if rank is None:
        for (r, side), h in helpers.items():
            if h == core:
                _helper_program(g, core, T, topo, r, side)
        return
    ops, sides = _calls(g, core, T, topo, rank, helpers)
    byname = {o[0]: o for o in ops}
    plan = [(byname[w[:-2]], w[-1] if w[-1] != "-" else None) for w in PLAN.split() if w[:-2] in byname]
    assert len(plan) == len(ops)
    Q = {"v": g.vector, "a": g.scalar, "t": g.tensor, "g": g, "y": g.sync}
    cnt, seen, hist = {}, {}, []

    def need(q, key, val):
        if seen.get((q, key), 0) < val:
            seen[(q, key)] = val
            Q[q].wait_ge(T.sem[key], val)

    for (name, fns, outs, ins, sem), q in plan:
        if q is None:
            key, cnt[sem] = sem, 2 * FAR * sides
        else:
            want = {}
            for cols, wr in ((outs, True), (ins, False)):
                for c in cols:
                    for (d, k, n, w) in hist:
                        if _meet(c, d) and not (k == "nt" and q == "t") and k != "sent":
                            if w or wr or (c[0] == "ps" and k != "n" + q):
                                want[k] = max(want.get(k, 0), n)
            for k in want:
                need(q, k, want[k])
            key = sem or "n" + q
            step = NEAR * sides if sem == "sent" else 16 if sem else 1
            cnt[key] = cnt.get(key, 0) + step
            call = fns[q]()
            if sem != "sent":
                call.then_inc(T.sem[key], step)
        for cols, wr in ((outs, True), (ins, False)):
            for c in cols:
                hist.append((c, key, cnt[key], wr))
    g.wait_ge(T.sem.sent, cnt["sent"])
    for k in cnt:
        if k != "sent":
            need("y", k, cnt[k])
